import numpy as np, ml_dtypes
CORES = [35,38,43,46]
N = 4
import mx_ref
BF = ml_dtypes.bfloat16
def gcols(t, e):
    v = np.concatenate([t.reshape(8, 16, -1, 4), np.zeros((8, 16, 1, 4), BF)], axis=2)
    return np.ascontiguousarray(np.stack([v[g][:, e[g]] for g in range(8)])).reshape(128, -1)
def tile(rs):
    return np.stack(rs, axis=2).reshape(128, -1).astype(BF)
def cut(t, i, w=512):
    return t[:, w * i:w * i + w]
def pick(q, e):
    c = np.concatenate([q[0].reshape(128, -1, 4), np.zeros((128, 1, 4), np.uint8)], axis=1); s = np.concatenate([q[1], np.ones((16, 1), np.uint8)], axis=1)
    return (np.ascontiguousarray(c[:, e].reshape(128, -1)), np.ascontiguousarray(s[:, e]))
def join(*qs):
    return (np.concatenate([q[0] for q in qs], axis=1), np.concatenate([q[1] for q in qs], axis=1))
def put(q, e, v):
    c, s = q[0].reshape(128, -1, 4).copy(), q[1].copy(); c[:, e] = v[0].reshape(128, -1, 4); s[:, e] = v[1]
    return (c.reshape(128, -1), s)
def pk(c, s):
    return (np.ascontiguousarray(c), mx_ref.live(s))
def emit(q):
    return q[0], q[1]
def packed(v, rng):
    q = [mx_ref.quantize(np.ascontiguousarray(v[r])) for r in range(N)]
    return np.stack([a for a, b in q]), np.stack([mx_ref.plane(b, rng) for a, b in q])
def values_of_codes():
    e, c = np.zeros((128, 128, 4), np.float32), np.zeros((128, 2, 4), np.uint8)
    e[np.arange(128), np.arange(128), 0] = 1
    c[:127, :, 0] = np.arange(256).reshape(2, 128).T[:127]
    return mx_ref.matmul(mx_ref.quantize(e.reshape(128, 512).astype(BF)), (c.reshape(128, 8), np.full((16, 2), 127, np.uint8))).T.reshape(-1).astype(np.float64)
CODE_VALUE, SCALE_VALUE = values_of_codes(), 2.0 ** (np.arange(256) - 127.0)
def decode(q):
    return (CODE_VALUE[q[0]].reshape(16, 8, -1, 4) * SCALE_VALUE[q[1]][:, None, :, None] + 0.0).reshape(128, -1).astype(np.float32)
def f(rng, *shape):
    return mx_ref.flush((rng.standard_normal(shape, dtype=np.float32) * np.exp2(rng.integers(-2, 3, shape[:-1] + (1,)))).astype(BF))
def wide(rng, *shape, cols=0):
    v = rng.standard_normal(shape, dtype=np.float32) * np.exp2(rng.integers(-12, 13, shape)).astype(np.float32)
    if cols: v *= np.repeat(np.exp2(rng.integers(-cols, cols + 1, shape[:-2] + (1, shape[-1] // 4))) * (rng.random(shape[:-2] + (1, shape[-1] // 4)) > 0.0625), 4, axis=-1).astype(np.float32)
    return mx_ref.flush(v.astype(BF))
C, L1, H1, L2, H2, K, R = 320, 128, 192, 80, 104, 112, 3
def big(v):
    v = v.astype(np.float32)
    v[np.abs(v) < np.float32(2.0 ** -16)] = 0
    return v.astype(BF)
def numbers_of(rng):
    return {"x": big(f(rng, N, 128, 4 * C)), "u": np.array(f(rng, N, 128, 512)), "v": np.array(f(rng, N, 128, 512))}
def layers(rng):
    return big(f(rng, N, 128, 2048)).reshape(N, 8, 16, 4, 8, 16, 4)
def weights(rng, w):
    c, p = packed(np.ascontiguousarray(w).reshape(N, 128, 2048), rng)
    return {"wc": c, "ws": p}
def setup_inputs(rng):
    return {**numbers_of(rng), **weights(rng, layers(rng))}
def setup_inputs_ties(rng):
    d = numbers_of(rng)
    x = d["x"].reshape(N, 8, 16, C, 4)
    x[:, :, 0] = 0
    x[:, :, 0, :, :2] = np.where(rng.random((N, 8, C, 2)) < 0.125, 3, rng.integers(1, 3, (N, 8, C, 2))).astype(np.float32).astype(BF)
    u = d["u"].reshape(N, 128, 128, 4)
    u[:, :, ::16] = 0
    u[:, :, 1::16] = 0
    e = int(rng.integers(N))
    k = rng.permutation(N - 2) % 2 * 2.0 - 1.0
    for i in range(N - 2):
        r = (e + 1 + i) % N
        for h in range(0, 128, 16):
            u[r, h, h, 0] = k[i]
            u[r, h, h + 1, 1] = k[i]
    w = layers(rng)
    w[:, :, :, :, :, 0] = 0
    return {"x": x.reshape(N, 128, 4 * C), "u": u.reshape(N, 128, 512), "v": d["v"], **weights(rng, w)}
def setup_inputs_near(rng):
    d = numbers_of(rng)
    x = d["x"].astype(np.float32).reshape(N, 8, 16, C, 4)
    x[:, :, 0] = 0
    x[:, :, 8:] = 0
    u = d["u"].reshape(N, 128, 128, 4)
    u[:, :, ::16] = 0
    u[:, :, 1::16] = 0
    o = rng.permutation(N) % 4
    for r in range(N):
        k = 1.0 if o[r] == 0 else 2.0 ** -30
        if o[r] < 3:
            s = rng.integers(0, 16, (8, C))
            x[r, :, 8] = ((s[:, :, None] >> np.arange(4)) & 1) * np.exp2(np.arange(4) - 23.0)
        if o[r] < 2:
            x[r, :, 0, :, 0] = 1.0 - 2.0 * o[r]
            x[r, :, 11, :, 0] = 2.0 ** -10
        if o[r] == 2: x[r, :, 0, :, 0] = -1.0 * (rng.random((8, C)) < 0.25)
        if o[r] == 3:
            s = rng.random((8, C)) < 0.25
            x[r, :, 10, :, 0] = np.where(s, 9.0, 0.0) * 2.0 ** -32
            x[r, :, 12, :, 0] = np.where(s, 0.0, 8.0) * 2.0 ** -32
        for h in range(0, 128, 16):
            for i in (h, h + 1):
                u[r, h, i, 0] = 1.0 if o[r] == 2 else k
                u[r, h + 8, i] = k
                u[r, h + 10, i, 0] = k * 1.125
                u[r, h + 11, i, 0] = k
                u[r, h + 12, i, 0] = k * 1.25
    w = layers(rng)
    w[:, :, :, :, :, 0] = 0
    w[:, :, :, :, :, 8:] = 0
    return {"x": x.reshape(N, 128, 4 * C).astype(BF), "u": u.reshape(N, 128, 512), "v": d["v"], **weights(rng, w)}
def setup_inputs_huge(rng):
    d = numbers_of(rng)
    e = rng.permutation(N)
    x = -0.6 - 0.4 * rng.random((N, 8, 16, C, 4))
    a = 0.9 + 0.1 * rng.random((N, 128, 128, 4))
    x[e[0], :, :15] = -1.0
    for i in (L1 - 1, H1 + 1): x[e[0], :, :, i] = -0.625
    a[e[0]] = 1.0
    u = d["u"].astype(np.float32).reshape(N, 128, 128, 4)
    for r in range(N):
        both = r in e[1::2]
        if both: x[r] *= rng.choice([-1.0, 1.0], (8, 1, C, 1))
        for h in range(0, 128, 16):
            i = slice(h, h + 16) if both else slice(0, 128)
            u[r, :, h:h + 2] = 0
            u[r, i, h:h + 2] = 2.0 ** 30 * a[r, i, h:h + 2]
    w = np.zeros((N, 128, 4, 128, 4), np.float32)
    i = np.arange(128)
    for b in range(4): w[:, i, b, i, b] = -1
    return {"x": (2.0 ** 30 * x).astype(np.float32).reshape(N, 128, 4 * C).astype(BF), "u": u.astype(BF).reshape(N, 128, 512), "v": d["v"], **weights(rng, w.astype(BF))}
def setup_inputs_edge(rng):
    d = numbers_of(rng)
    x = d["x"].reshape(N, 8, 16, C, 4)
    c = np.where(rng.random((N, 8)) < 0.25, rng.integers(L1, H1 + 1, (N, 8)), rng.choice([L1, H1], (N, 8)))
    k = np.where(rng.random((N, 8)) < 0.25, rng.integers(L2, H2 + 1, (N, 8)), rng.choice([L2, H2], (N, 8)))
    e = int(rng.integers(N))
    for r in (e, (e + 1) % N):
        c[r] = H1
        k[r] = L2
    x[:, :, 0] = 0
    x[:, :, 0, :, :2] = rng.integers(-1, 2, (N, 8, C, 2)).astype(np.float32).astype(BF)
    for i in (L1 - 1, H1 + 1): x[:, :, 0, i, 0] = 4.0
    for i in (L2 - 1, H2 + 1): x[:, :, 0, i, 1] = 4.0
    for r in range(N):
        for g in range(8):
            x[r, g, 0, c[r, g], 0] = 2.0
            x[r, g, 0, k[r, g], 1] = 2.0
    n = (N, 8, 8, C, 4)
    s = np.exp2(-1.0 * rng.integers(8, 15, n)) * (1.0 + (2 * rng.integers(0, 64, n) + 1) * 2.0 ** -7) * rng.choice([-1.0, 1.0], n)
    s[:, :, 0, :, 0] = 1.96875 * rng.choice([-1.0, 1.0], (N, 8, C))
    x[:, :, 8:] = s.astype(np.float32).astype(BF)
    u = d["u"].reshape(N, 128, 128, 4)
    u[:, :, ::16] = 0
    u[:, :, 1::16] = 0
    for h in range(0, 128, 16):
        u[:, h, h, 0] = 1
        u[:, h, h + 1, 1] = 1
    return {"x": x.reshape(N, 128, 4 * C), "u": u.reshape(N, 128, 512), "v": d["v"], **weights(rng, layers(rng))}
def setup_inputs_spread(rng):
    d = setup_inputs(rng)
    d["x"] = big(wide(rng, N, 128, 4 * C, cols=6))
    return d
def check_inputs(d):
    b = []
    for k in ("x", "u", "v"):
        a = np.abs(d[k].astype(np.float32))
        if not (np.isfinite(a).all() and ((a == 0) | (a >= 2.0 ** -30) & (a <= 2.0 ** 30)).all()): b.append("a value of " + k)
    none, least, most = [emit(mx_ref.quantize(np.full((128, 16), k, np.float32).astype(BF)))[1][0, 0] for k in (0.0, 2.0 ** -30, 2.0 ** 30)]
    for r in range(N):
        if ((d["wc"][r] == 0x7F) | (d["wc"][r] == 0xFF)).any(): b.append("wc: a code that is no number")
        s = mx_ref.live(d["ws"][r])
        if ((s != none) & ((s < least) | (s > most))).any(): b.append("ws: a scale out of range")
    return b
def folded(c, k):
    p = np.arange(C)
    q = np.where(p < c, c - 1 - p, p - c)
    z = np.where(q < k, k - 1 - q, q - k)
    right = (p >= c).astype(np.int64)
    leaf = np.where(q < k, right, 3 - right)
    o = np.argsort(4 * z + leaf, axis=1)
    zo = np.take_along_axis(z, o, axis=1)
    first = np.ones((8, C), bool)
    first[:, 1:] = zo[:, 1:] != zo[:, :-1]
    low, above = np.full((8, K), -1), C + z
    g, j = np.nonzero(first)
    low[g, zo[g, j]] = o[g, j]
    g, j = np.nonzero(~first)
    above[g, o[g, j - 1]] = o[g, j]
    return o, low, above
def reference(x, u, v, wc, ws):
    qu = [mx_ref.quantize(u[r]) for r in range(N)]
    lay = [pk(wc[r], ws[r]) for r in range(N)]
    now = [x[r] for r in range(N)]
    for t in range(R):
        own, folds, sent = [], [], []
        for r in range(N):
            q = mx_ref.quantize(now[r])
            own.append(decode(q))
            s = mx_ref.matmul(qu[r], q) + np.float32(0.0)
            c = L1 + np.argmax(s[::16, L1:H1 + 1], axis=1)
            k = L2 + np.argmax(s[1::16, L2:H2 + 1], axis=1)
            folds.append(folded(c[:, None], k[:, None]))
            sent.append(mx_ref.quantize(gcols(now[r], folds[r][1])))
        came = decode(join(*sent)).astype(BF)
        for r in range(N):
            o, low, above = folds[r]
            a = np.concatenate([own[r].astype(BF), cut(came, (r + 1) % N, 4 * K)], axis=1)
            z = mx_ref.quantize(((own[r] + gcols(a, above).astype(np.float32)) * np.float32(0.5)).astype(BF))
            made = tile([mx_ref.matmul(pick(lay[r], np.arange(128 * b, 128 * b + 128)), z) * np.float32(0.03125) + own[r][:, b::4] for b in range(4)])
            now[r] = gcols(made, o)
    y, lo = np.zeros((N, 128, C), np.float32), np.zeros((N, 8, C), np.float32)
    oc, osc = np.zeros((N, 128, 4 * C), np.uint8), np.zeros((N, 16, C), np.uint8)
    for r in range(N):
        q = mx_ref.quantize(now[r])
        y[r] = mx_ref.matmul(mx_ref.quantize(v[r]), q)
        lo[r] = folds[r][0]
        oc[r], osc[r] = emit(q)
    return {"y": y, "lo": lo, "oc": oc, "osc": osc}

@@ -1,0 +1,411 @@
+import numpy as np
+from concourse.mybir import AluOpType as Op, AxisListType, ActivationFunctionType as Fn, dt
+
+NZ = 256
+PAD = 128 + NZ
+XW = PAD + 1280
+WIN = PAD + 832
+PART = ((0, 192), (192, 320))
+FCOLS = [
+    ("R0", (0, 2, 0), (2, -2, 0)), ("B1", (2, 2, -320), (0, 0, 0)),
+    ("R1", (2, 2, -320), (-2, -2, 1320)), ("tau", (-1, -3, -319), (-2, 2, 640)),
+    ("m4", (-4, -4, 1280), (8, 0, -1280)), ("de", (1, -2, 0), (-2, 0, 320)),
+    ("d2", (-2, 4, 0), (4, 0, -640)), ("X", (0, 0, -1), (0, 0, 2)), ("Z", (-1, 0, 319.5), (0, 0, -319)),
+]
+NCOLS = [
+    ("ck", (1, -1, 0)), ("base", (1, -1, 319)), ("n2n", (1, 1, -320)), ("cpk", (1, 1, 0)), ("c", (1, 0, 0)),
+    ("cm", (1, 0, -0.5)), ("X1", (-1, 1, 320)), ("k2n", (0, -2, 0)), ("k2", (0, 2, 0)), ("kh", (0, -1, 0.5)),
+]
+NF, NN = len(FCOLS), len(NCOLS)
+NL = 2 * NF + NN
+LIN = [a for _, a, _ in FCOLS] + [a for _, a in NCOLS] + [b for _, _, b in FCOLS]
+SCOL = {n: i for i, n in enumerate([n for n, _, _ in FCOLS] + [n for n, _ in NCOLS])}
+
+F8, U8, BF, F32, I32, U16 = "float8_e4m3fn_x4", "uint8", "bfloat16", "float32", "int32", "uint16"
+SCRATCH = {"PS": ("psum", [128, 4096], F32)}
+for _n, _w in (("X0", XW), ("X1", XW), ("X2", XW), ("X3", 1280), ("UT", 512), ("VT", 512), ("BT", 512), ("ZT", 1280), ("PL", 1728),
+               ("FP", 640), ("AB", 1280), ("YP", 1280), ("ED", 516), ("EDB", 516), ("HALF", 516)):
+    SCRATCH[_n] = ("sbuf", [128, _w], BF)
+for _n, _w in (("QU", 128), ("UU", 256), ("QV", 128), ("QW", 512), ("EH", 512), ("EB", 512), ("QS", 128), ("QX", 320), ("QZ", 320),
+               ("QF", 320), ("B0", 128), ("B1", 128), ("B2", 128), ("G0", 128), ("G1", 128), ("G2", 128)):
+    SCRATCH[_n] = ("sbuf", [128, _w], F8)
+    SCRATCH[_n + "s"] = ("sbuf", [128, _w], U8)
+for _n, _w in (("C16", 28), ("TJB", 28), ("TP", 20), ("TN", 20), ("Z4", 8), ("CZ", 8), ("LANE", 7), ("LAN2", 4), ("JF", 76), ("EP", 76), ("NIL", 68),
+               ("AL", NL), ("BE", NL), ("GA", NL), ("IOT", 320), ("LOR", 320), ("YO", 320), ("RMC", 65), ("RMK", 25), ("LTC", 66), ("LTK", 26),
+               ("CK", 2), ("S1", NL), ("S2", NL), ("S3", NL), ("S4", NL), ("FS", NF), ("FV", NF), ("SM", 16), ("W2", 64), ("WA", 320), ("WO", 1024)):
+    SCRATCH[_n] = ("sbuf", [128, _w], F32)
+for _n, _w in (("LI", 7), ("JI", 76), ("PO", 16), ("OQ", 56), ("OS", 56), ("O0", 56), ("O1", 56), ("OZ", 56)):
+    SCRATCH[_n] = ("sbuf", [128, _w], I32)
+for _n, _w in (("PU", 16), ("L1", 20), ("L2", 8), ("LA", 20), ("LO", 56)):
+    SCRATCH[_n] = ("sbuf", [128, _w], U16)
+SEMAPHORES = ["v", "a", "te", "gc", "dx", "dy", "du", "dv", "dw", "dn", "out", "arr0", "arr1", "arr2", "sent"]
+RBANK = ((0, 1, 4, 5), (6, 7, 2, 3))
+GBANK = (4, 6, 5, 7)
+
+
+def rank_program(g, core, T, topo):
+    rank = T.rank_of(core)
+    if rank is None:
+        return
+    N = len(T.cores)
+    prev, nxt = T.cores[(rank - 1) % N], T.cores[(rank + 1) % N]
+    queue = {"v": g.vector, "a": g.scalar, "te": g.tensor, "gc": g, "sy": g.sync}
+    total, known = {}, {}
+
+    def wait(q, deps):
+        need = {}
+        for s, n in deps:
+            need[s] = max(need.get(s, 0), n)
+        for s, n in need.items():
+            if known.get((q, s), 0) < n:
+                queue[q].wait_ge(T.sem[s], n)
+                known[(q, s)] = n
+
+    def run(q, fn, deps=()):
+        wait(q, deps)
+        ins = fn(queue[q])
+        total[q] = total.get(q, 0) + 1
+        ins.then_inc(T.sem[q], 1)
+        return (q, total[q])
+
+    def dma(q, out, in_, sem, deps=()):
+        wait(q, deps)
+        queue[q].dma_start(out, in_).then_inc(T.sem[sem], 16)
+        total[sem] = total.get(sem, 0) + 16
+        return (sem, total[sem])
+
+    def ts(out, in0, s1, op0, s2=None, op1=None, deps=()):
+        if op1 is None:
+            return run("v", lambda q: q.tensor_scalar(out, in0, s1, None, op0), deps)
+        return run("v", lambda q: q.tensor_scalar(out, in0, s1, s2, op0, op1), deps)
+
+    def tt(out, a, b, op, deps=()):
+        return run("v", lambda q: q.tensor_tensor(out, a, b, op), deps)
+
+    def vcopy(out, in_, deps=()):
+        return run("v", lambda q: q.tensor_copy(out, in_), deps)
+
+    def acopy(out, in_, deps=(), scale=1.0):
+        return run("a", lambda q: q.activation(out, in_, Fn.Copy, scale=scale), deps)
+
+    def affine(out, in_, bias, scale=1.0, deps=()):
+        return run("a", lambda q: q.activation(out, in_, Fn.Identity, bias=bias, scale=scale), deps)
+
+    def quant(name, lo, hi, in_, deps=()):
+        return run("v", lambda q: q.quantize_mx(T[name][:, lo:hi], T[name + "s"][:, lo:hi], in_), deps)
+
+    def mm(bank, n, w, wlo, x, xlo, deps=(), start=True, stop=True):
+        return run("te", lambda q: q.matmul_mx(T.PS[:, 512 * bank:512 * bank + n], T[w][:, wlo:wlo + 128], T[w + "s"][:, wlo:wlo + 128],
+                                               T[x][:, xlo:xlo + n], T[x + "s"][:, xlo:xlo + n], start, stop), deps)
+
+    def part(h, b, w, x, deps, start, stop):
+        lo, hi = PART[h]
+        return mm(RBANK[h][b], hi - lo, w, 128 * b, x, lo, deps, start, stop)
+
+    def bank(b, lo, hi):
+        return T.PS[:, 512 * b + lo:512 * b + hi]
+
+    def fill(ap, value):
+        return run("v", lambda q: q.memset(ap, value))
+
+    def iota(ap, pattern, base, cm, flag=True):
+        if flag:
+            return run("gc", lambda q: q.iota(ap, pattern, base, cm, allow_small_or_imprecise_dtypes=True))
+        return run("gc", lambda q: q.iota(ap, pattern, base, cm))
+
+    dx = dma("sy", T.X0[:, PAD:XW], T.x[:], "dx")
+    du = dma("a", T.UT[:], T.u[:], "du")
+    dy = dma("sy", T.X0[:, 0:128], T.x[:, 1152:1280], "dy")
+    dma("sy", T.QW[:].bitcast(dt.uint8), T.wc[:], "dw")
+    dw = dma("sy", T.QWs[:], T.ws[:], "dw")
+    dv = dma("sy", T.VT[:], T.v[:], "dv")
+
+    t_po = iota(T.PO[:], [[1, 2], [16, 8]], 0, 0, flag=False)
+    t_li = iota(T.LI[:, 0:1], [[0, 1]], 0, 1, flag=False)
+    t_c16 = iota(T.C16[:], [[16, 28]], 0, 0)
+    fill(T.NIL[:], 0.0)
+    fill(T.AL[:], 0.0)
+    fill(T.BE[:], 0.0)
+    t_nil = fill(T.GA[:], 0.0)
+    t_half = fill(T.HALF[:], 0.5)
+    t_ed = run("gc", lambda q: q.affine_select(T.ED[:], T.HALF[:], [[-1, 516]], Op.is_equal, 0.0, 3, 4), [t_half])
+    t_pad0 = iota(T.X0[:, 128:PAD], [[0, NZ]], 0, 0)
+    iota(T.JF[:, 0:8], [[16, 8]], 80, 0)
+    iota(T.JF[:, 8:28], [[4, 20]], 0, 0)
+    iota(T.JF[:, 28:56], [[4, 28]], 208, 0)
+    t_jf = iota(T.JF[:, 56:76], [[16, 20]], 0, 0)
+
+    def coefficients(name, i):
+        runs, j = [], 0
+        while j < NL:
+            e = j
+            while e < NL and LIN[e][i] == LIN[j][i]:
+                e += 1
+            if LIN[j][i] != 0:
+                runs.append((T[name][:, j:e], float(LIN[j][i]), e - j))
+            j = e
+        return runs
+
+    def put(runs):
+        for ap, value, n in runs:
+            tok = affine(ap, T.NIL[:, 0:n], value, deps=[t_nil])
+        return tok
+
+    coef = coefficients("AL", 0) + coefficients("BE", 1) + coefficients("GA", 2)
+    put(coef[:20])
+    t_pu = vcopy(T.PU[:], T.PO[:], [t_po])
+    for i, m in ((1, 15), (2, 12), (3, 12), (4, 3), (5, 1)):
+        ts(T.LI[:, i:i + 1], T.LI[:, 0:1], m, Op.bitwise_and, deps=[t_li])
+    t_l6 = ts(T.LI[:, 6:7], T.LI[:, 0:1], 2, Op.logical_shift_right, 1, Op.bitwise_and)
+    fill(T.LTC[:, 65:66], 512.0)
+    t_lt = fill(T.LTK[:, 25:26], 320.0)
+    t_lane = vcopy(T.LANE[:], T.LI[:], [t_l6])
+    t_bt = fill(T.BT[:], 0.0)
+    t_l1 = ts(T.LANE[:, 3:4], T.LANE[:, 2:3], 0.25, Op.mult, deps=[t_lane])
+    ts(T.LANE[:, 4:5], T.LANE[:, 4:5], 320.0, Op.mult)
+    ts(T.LAN2[:, 0:2], T.LANE[:, 5:7], -1.0, Op.mult, 0.5, Op.add)
+    t_lan2 = ts(T.LAN2[:, 2:4], T.LANE[:, 5:7], 319.5, Op.mult, -159.5, Op.add)
+    lane, l4, l1, b320 = (T.LANE[:, i:i + 1] for i in (1, 2, 3, 4))
+    t_tjb = ts(T.TJB[:], T.C16[:], lane, Op.add, float(PAD), Op.add, [t_c16, t_l1])
+    shift = float(PAD + 4 * 288)
+    ts(T.Z4[:], T.C16[:, 20:28], l4, Op.add)
+    t_cz = ts(T.CZ[:], T.C16[:, 20:28], l4, Op.add, 2.0 - shift / 2, Op.add)
+    t_qu = quant("QU", 0, 128, T.UT[:], [du])
+    t_us = run("a", lambda q: q.activation(T.UUs[:], T.QUs[:].indirect(T.PU[:]), Fn.Copy), [t_qu, t_pu])
+    t_uc = run("v", lambda q: q.tensor_copy(T.UU[:].bitcast(dt.uint32), T.QU[:].bitcast(dt.uint32).indirect(T.PU[:])), [t_qu, t_pu])
+    t_ab = put(coef[20:34])
+
+    def a_constants():
+        eb = acopy(T.EDB[:], T.ED[:], [t_ed], scale=64.0)
+        put(coef[34:])
+        affine(T.TP[:], T.C16[:, 0:20], lane, deps=[t_c16, t_tjb, t_lan2, t_jf])
+        affine(T.JF[:, 0:8], T.JF[:, 0:8], lane)
+        affine(T.JF[:, 8:56], T.JF[:, 8:56], l1)
+        j = affine(T.JF[:, 56:76], T.JF[:, 56:76], lane)
+        affine(T.TN[:], T.TP[:], 0.0, -1.0, [j])
+        for lo, hi, i in ((0, 8, 0), (8, 56, 1), (56, 76, 0)):
+            e = affine(T.EP[:, lo:hi], T.JF[:, lo:hi], T.LAN2[:, 2 + i:3 + i], T.LAN2[:, i:i + 1])
+        return [e], j, eb
+
+    CK, FV, SMT, WA, WO = T.CK, T.FV, T.SM, T.WA, T.WO
+    C4, K4, fv = CK[:, 0:1], CK[:, 1:2], SMT[:, 0:1]
+
+    def sc(name):
+        i = SCOL[name]
+        return FV[:, i:i + 1] if i < NF else T.S4[:, i:i + 1]
+
+    def lists(last, t_s, t_const, halves):
+        o = (56, 76) if last else (0, 56)
+        w = o[1] - o[0]
+        J, JI, E, P = T.JF[:, o[0]:o[1]], T.JI[:, o[0]:o[1]], T.EP[:, o[0]:o[1]], T.TP[:]
+        wa = lambda i: WA[:, 20 * i:20 * i + 20]
+        wo = lambda i: WO[:, 64 * i:64 * i + w]
+        it = lambda n: T[n][:, 0:w]
+        k = {"s": t_s, "con": t_const}
+
+        def step(name, fn, *deps):
+            k[name] = fn([x for d in deps for x in (k[d] if isinstance(k[d], list) else [k[d]])])
+
+        step("s3", lambda d: tt(T.S3[:], T.S1[:], T.GA[:], Op.add, d), "s", "con")
+        step("s4", lambda d: tt(T.S4[:], T.S3[:], T.S2[:], Op.add, d), "s3")
+        step("fs", lambda d: ts(T.FS[:], T.S4[:, NF + NN:NL], fv, Op.mult, deps=d), "s4")
+        step("m1", lambda d: ts(wa(0), P, sc("ck"), Op.is_ge, sc("n2n"), Op.mult, d), "s4")
+        step("fv", lambda d: tt(FV[:], T.FS[:], T.S4[:, 0:NF], Op.add, d), "fs")
+        step("m2", lambda d: ts(wa(1), P, sc("c"), Op.is_ge, sc("X1"), Op.mult, d), "s4")
+        step("m4x", lambda d: ts(wa(3), P, sc("cpk"), Op.is_ge, sc("k2n"), Op.mult, d), "s4")
+        t_hf = halves()
+        step("w", lambda d: affine(wa(6), P, sc("tau"), 2.0, d), "fv")
+        step("q", lambda d: affine(wo(4), J, sc("Z"), sc("X"), d), "fv")
+        for b in range(4):
+            step("f%d" % b, lambda d: acopy(T.PL[:, 432 * b:432 * b + 320], bank(b, 0, 320), [t_hf[b]]))
+            if b < 2:
+                step("p%d" % b, lambda d: acopy(T.FP[:, 320 * b:320 * b + 320], bank(b, 0, 320)))
+        ops_a = [
+            ("RB", lambda d: ts(SMT[:, 2:4], FV[:, 0:2], sc("c"), Op.max, deps=d), "fv"),
+            ("r2", lambda d: ts(wa(5), P, sc("R1"), Op.is_lt, deps=d), "fv"),
+            ("a1", lambda d: tt(wa(8), wa(0), T.TN[:], Op.add, d), "m1"),
+            ("m3", lambda d: ts(wa(2), P, SMT[:, 3:4], Op.is_ge, sc("n2n"), Op.mult, d), "RB"),
+            ("r1", lambda d: ts(wa(4), P, SMT[:, 2:3], Op.is_ge, deps=d), "RB"),
+            ("a2", lambda d: tt(wa(9), wa(1), wa(2), Op.add, d), "m2", "m3"),
+            ("rw", lambda d: tt(wa(7), wa(5), wa(4), Op.mult, d), "r2", "r1"),
+            ("a4", lambda d: tt(wa(11), wa(8), wa(9), Op.add, d), "a1", "a2"),
+            ("rv", lambda d: tt(wa(10), wa(6), wa(7), Op.mult, d), "w", "rw"),
+            ("a6", lambda d: tt(wa(12), wa(11), wa(3), Op.add, d), "a4", "m4x"),
+            ("a5", lambda d: tt(wa(13), wa(10), wa(12), Op.add, d), "rv", "a6"),
+            ("LA", lambda d: ts(T.LA[:], wa(13), sc("base"), Op.add, deps=d), "a5"),
+        ]
+        ops_o = [
+            ("t", lambda d: ts(wo(0), J, sc("m4"), Op.subtract, 0.0, Op.max, d), "fv"),
+            ("ma", lambda d: ts(wo(5), J, sc("d2"), Op.add, 320.0, Op.is_ge, d), "fv"),
+            ("Q", lambda d: ts(it("OQ"), wo(0), fv, Op.subtract, 1.0 / 3.0, Op.mult, d), "t"),
+            ("mb", lambda d: ts(wo(8), J, sc("de"), Op.add, 320.0, Op.is_ge, d), "fv"),
+            ("s5", lambda d: tt(it("OS"), it("OQ"), JI, Op.add, d), "Q"),
+            ("b1", lambda d: ts(it("O1"), it("OS"), 1, Op.logical_shift_right, 1, Op.bitwise_and, d), "s5"),
+            ("z", lambda d: ts(it("OZ"), it("OS"), 2, Op.logical_shift_right, deps=d), "s5"),
+            ("b0", lambda d: ts(it("O0"), it("OS"), 1, Op.bitwise_and, deps=d), "s5"),
+            ("sk", lambda d: ts(wo(1), it("O1"), sc("k2"), Op.mult, sc("kh"), Op.add, d), "b1"),
+            ("s12", lambda d: ts(wo(2), it("O0"), -2.0, Op.mult, 1.0, Op.add, d), "b0"),
+            ("u", lambda d: tt(wo(3), wo(1), it("OZ"), Op.add, d), "sk", "z"),
+            ("p12", lambda d: tt(wo(6), wo(2), wo(3), Op.mult, d), "s12", "u"),
+            ("da", lambda d: tt(wo(7), E, wo(6), Op.subtract, d), "p12"),
+            ("db", lambda d: tt(wo(9), wo(4), wo(6), Op.subtract, d), "q", "p12"),
+            ("xa", lambda d: tt(wo(10), wo(7), wo(5), Op.mult, d), "da", "ma"),
+            ("xb", lambda d: tt(wo(12), wo(9), wo(8), Op.mult, d), "db", "mb"),
+            ("x1", lambda d: tt(wo(13), wo(10), wo(6), Op.add, d), "xa"),
+            ("pl", lambda d: tt(wo(11), wo(13), wo(12), Op.add, d), "x1", "xb"),
+        ]
+        na, no = len(ops_a), len(ops_o)
+        for j in range(max(na, no)):
+            if j < na:
+                step(*ops_a[j])
+            if j < no:
+                step(*ops_o[j])
+
+        def finish():
+            if last:
+                return ts(T.LO[:, 0:20], wo(11), sc("cm"), Op.add, deps=[k["pl"]])
+            ts(T.LO[:, 0:8], WO[:, 704:712], sc("cm"), Op.add, deps=[k["pl"]])
+            return ts(T.LO[:, 8:56], WO[:, 712:760], sc("cm"), Op.add, b320, Op.add)
+
+        return k, finish
+
+    first, low, tail, behind = [dx], [dx, dy, t_pad0], None, None
+    for t in range(3):
+        X, last = T["X%d" % t], t == 2
+        t_qs = quant("QS", 0, 128, X[:, PAD + 320:PAD + 832], first)
+        t_s1 = mm(6, 128, "UU", 0, "QS", 0, [t_qs, t_uc, t_us])
+        t_s2 = mm(7, 128, "UU", 128, "QS", 0)
+        if tail:
+            low = low + [tail()]
+        t1 = run("v", lambda q: q.tensor_tensor_scan(T.RMC[:], T.NIL[:, 0:65], bank(6, 48, 113), -1e29, Op.add, Op.max), [t_s1, t_nil])
+        t2 = run("v", lambda q: q.tensor_tensor_scan(T.RMK[:], T.NIL[:, 0:25], bank(7, 0, 25), -1e29, Op.add, Op.max), [t_s2])
+        t3 = ts(T.LTC[:, 0:65], T.RMC[:], T.RMC[:, 64:65], Op.is_lt, 4.0, Op.mult, [t1])
+        t4 = ts(T.LTK[:, 0:25], T.RMK[:], T.RMK[:, 24:25], Op.is_lt, 4.0, Op.mult, [t2])
+        t5 = run("v", lambda q: q.tensor_reduce(C4, T.LTC[:], AxisListType.X, Op.add), [t3, t_lt])
+        t6 = run("v", lambda q: q.tensor_reduce(K4, T.LTK[:], AxisListType.X, Op.add), [t4])
+        w2 = lambda i: T.W2[:, 8 * i:8 * i + 8]
+        fm, k8 = SMT[:, 12:13], SMT[:, 13:14]
+        t7 = ts(fm, C4, 640.0, Op.is_ge, -1.0, Op.mult, [t5])
+        t_l1 = ts(T.L1[:], T.TJB[:, 0:20], C4, Op.add, K4, Op.subtract, [t6, t_tjb])
+        t_b1 = acopy(T.BT[:, 0:320], X[:, 0:WIN].indirect(T.L1[:]), [t_l1, t_bt] + low)
+        t9 = ts(k8, K4, 2.0, Op.mult, -shift, Op.add)
+        t10 = ts(w2(1), T.CZ[:], K4, Op.add, fm, Op.mult, [t7, t_cz])
+        t8 = ts(w2(0), T.Z4[:], K4, Op.is_ge, 2.0, Op.mult)
+        tx = ts(w2(4), T.Z4[:], K4, Op.is_ge, k8, Op.mult, [t9])
+        t11 = tt(w2(2), w2(0), w2(1), Op.mult, [t8, t10])
+        tb = tt(w2(5), w2(4), T.TJB[:, 20:28], Op.add, [tx])
+        ts(fv, C4, 640.0, Op.is_lt)
+        t12 = tt(w2(3), w2(2), w2(5), Op.add, [t11, tb])
+        ts(T.S1[:], T.AL[:], C4, Op.mult, 0.25, Op.mult, [t_ab])
+        t_l2 = ts(T.L2[:], w2(3), C4, Op.add, K4, Op.subtract, [t12])
+        t_s = ts(T.S2[:], T.BE[:], K4, Op.mult, 0.25, Op.mult)
+        t_b2 = vcopy(T.BT[:, 320:448], X[:, 0:WIN].indirect(T.L2[:]), [t_l2] + low)
+        B, G = "B%d" % t, "G%d" % t
+        t_qb = quant(B, 0, 128, T.BT[:], [t_b1, t_b2])
+        engines = topo.engines(core, prev)[:8]
+        mask = sum(1 << e for e in engines)
+        rid, pid = topo.addr(prev)[:2]
+        wait("gc", [t_qb])
+        for out, in_ in ((T[G][:, 0:112].bitcast(dt.uint8), T[B][:, 0:112].bitcast(dt.uint8)), (T[G + "s"][:, 0:112], T[B + "s"][:, 0:112])):
+            g.remote_dma(out, in_, T.sem["arr%d" % t], T.sem.sent, pid, rid, mask)
+            total["sent"] = total.get("sent", 0) + len(engines)
+        total["arr%d" % t] = 2 * len(topo.engines(nxt, core)[:8])
+        rest = low + ([behind()] if behind else [])
+        if t == 0:
+            for i in range(3):
+                dma("sy", T["G%d" % i][:, 112:128].bitcast(dt.uint8), T.B0[:, 112:128].bitcast(dt.uint8), "dn", [t_qb])
+                t_gn = dma("sy", T["G%ds" % i][:, 112:128], T.B0s[:, 112:128], "dn")
+            t_con, t_j, t_edb = a_constants()
+            for n in ("X1", "X2"):
+                t_pad = iota(T[n][:, 128:PAD], [[0, NZ]], 0, 0)
+            t_iot = iota(T.IOT[:], [[1, 320]], 0, 0)
+            for b in range(4):
+                t_eh = quant("EH", 128 * b, 128 * b + 128, T.ED[:, 3 - b:515 - b], [t_ed])
+            for b in range(4):
+                t_eb = quant("EB", 128 * b, 128 * b + 128, T.EDB[:, 3 - b:515 - b], [t_edb])
+            t_con.append(vcopy(T.JI[:], T.JF[:], [t_j]))
+
+        def halves(X=X, rest=rest, t_eh=t_eh):
+            qx = quant("QX", 0, 320, X[:, PAD:XW], rest)
+            return [mm(b, 320, "EH", 128 * b, "QX", 0, [qx, t_eh]) for b in range(4)]
+
+        k, finish = lists(last, [t_s], t_con, halves)
+        for b in range(2):
+            part(0, b, "EB", "QX", [k["p%d" % b], t_eb], True, False)
+        if t == 0:
+            t_qv = quant("QV", 0, 128, T.VT[:], [dv])
+        if last:
+            t_lo = finish()
+            t_lor = run("a", lambda q: q.activation(T.LOR[:], T.IOT[:].indirect(T.LO[:, 0:20]), Fn.Copy), [t_lo, t_iot])
+            dma("sy", T.lo[:], T.LOR[0:128:16, :], "out", [t_lor])
+        t_g = {}
+        for b in (0, 2, 1, 3):
+            t_g[b] = mm(GBANK[b], 128, "EH", 128 * b, G, 0, [("arr%d" % t, total["arr%d" % t]), t_gn])
+        win = lambda b: T.PL[:, 432 * b:432 * b + 432]
+        late = lambda b: T.PL[:, 432 * b + 320:432 * b + 432]
+        la = lambda h: T.LA[:, PART[h][0] // 16:PART[h][1] // 16]
+        zt = lambda b, h: T.ZT[:, 4 * PART[h][0] + b:4 * PART[h][1]:4]
+        at = lambda buf, b, h: buf[:, 320 * b + PART[h][0]:320 * b + PART[h][1]]
+        t_c, t_a, t_z = {}, {}, {}
+        for h in range(2):
+            for b in (2, 3):
+                if h == 0:
+                    t_c[b] = acopy(late(b), bank(GBANK[b], 0, 112), [t_g[b]])
+                t_a[b, h] = acopy(at(T.AB, b, h), win(b).indirect(la(h)), [k["LA"], t_c[b]])
+        for h in range(2):
+            for b in (0, 1):
+                if h == 0:
+                    t_c[b] = vcopy(late(b), bank(GBANK[b], 0, 112), [t_g[b]])
+                tt(zt(b, h), win(b).indirect(la(h)), at(T.FP, b, h), Op.add, [t_c[b], k["LA"], k["f3"]])
+            if h == 0:
+                part(0, 2, "EB", "QX", [t_c[0]], True, False)
+                part(0, 3, "EB", "QX", [t_c[2]], True, False)
+                part(1, 0, "EB", "QX", [t_c[1]], True, False)
+                part(1, 1, "EB", "QX", [t_c[3]], True, False)
+            for b in (2, 3):
+                t_z[b, h] = tt(zt(b, h), bank(b, *PART[h]), at(T.AB, b, h), Op.add, [t_a[b, h]] + ([t_z["pre", b]] if h else []))
+                if h == 0:
+                    t_z["pre", b] = part(1, b, "EB", "QX", [t_z[b, 0]], True, False)
+            lo, hi = PART[h]
+            t_z[h] = quant("QZ", lo, hi, T.ZT[:, 4 * lo:4 * hi], [t_z[3, h]])
+        t_r = [[part(h, b, "QW", "QZ", [t_z[h], dw], False, True) for b in range(4)] for h in range(2)]
+        new = [acopy(at(T.YP, b, 0), bank(RBANK[0][b], 0, 192), [t_r[0][b]], scale=0.03125) for b in range(4)]
+        if not last:
+            t_lo = finish()
+        XN, YP, LO = T["X%d" % (t + 1)], T.YP, T.LO
+        for b in range(4):
+            src, copy = bank(RBANK[1][b], 0, 128), (vcopy, acopy)[b % 2]
+            if b % 2 == 0:
+                ty = ts(at(YP, b, 1), src, 0.03125, Op.mult, deps=[t_r[1][b]])
+            else:
+                ty = acopy(at(YP, b, 1), src, [t_r[1][b]], scale=0.03125)
+            window, deps = YP[:, 320 * b:320 * b + 320], [ty, new[b], t_lo]
+            new.append(ty)
+            if last:
+                new.append(copy(XN[:, b:768:4], window.indirect(LO[:, 0:12]), deps))
+            else:
+                new.append(copy(XN[:, PAD + 320 + b:PAD + 832:4], window.indirect(LO[:, 0:8]), deps))
+        first = list(new)
+        if not last:
+            r1 = acopy(XN[:, 0:128], YP[:].indirect(LO[:, 48:56]), new)
+            r2 = acopy(XN[:, PAD + 128:PAD + 320], YP[:].indirect(LO[:, 16:28]))
+            tail = lambda XN=XN, new=new: vcopy(XN[:, PAD:PAD + 128], T.YP[:].indirect(T.LO[:, 8:16]), new)
+            behind = lambda XN=XN: acopy(XN[:, PAD + 832:XW], T.YP[:].indirect(T.LO[:, 28:56]))
+            low = new + [r1, r2, t_pad]
+
+    second = []
+    for b in range(4):
+        second.append((vcopy, acopy)[b % 2](XN[:, 768 + b:1280:4], YP[:, 320 * b:320 * b + 320].indirect(LO[:, 12:20]), new))
+        if b == 0:
+            t_q0 = quant("QF", 0, 192, XN[:, 0:768], first)
+    t_q1 = quant("QF", 192, 320, XN[:, 768:1280], second)
+    t_y0 = mm(2, 192, "QV", 0, "QF", 0, [t_q0, t_qv])
+    t_y1 = mm(3, 128, "QV", 0, "QF", 192, [t_q1])
+    t_o0 = acopy(T.YO[:, 0:192], bank(2, 0, 192), [t_y0])
+    dma("a", T.y[:, 0:192], T.YO[:, 0:192], "out", [t_o0])
+    dma("sy", T.oc[:], T.QF[:].bitcast(dt.uint8), "out", [t_q0, t_q1])
+    t_o1 = vcopy(T.YO[:, 192:320], bank(3, 0, 128), [t_y1])
+    for i in range(4):
+        dma("a" if i < 2 else "sy", T.osc[4 * i:4 * i + 4, :], T.QFs[32 * i:32 * i + 4, :], "out", [t_q0, t_q1])
+    dma("sy", T.y[:, 192:320], T.YO[:, 192:320], "out", [t_o1])
+    wait("gc", list(total.items()))

@@ -1,46 +1,35 @@
 import numpy as np
 from concourse.mybir import AluOpType as Op, AxisListType, ActivationFunctionType as Fn, dt
 
-NZ = 256
-PAD = 128 + NZ
+PAD = 384
 XW = PAD + 1280
-WIN = PAD + 832
+WIN = PAD + 768
 PART = ((0, 192), (192, 320))
-FCOLS = [
-    ("R0", (0, 2, 0), (2, -2, 0)), ("B1", (2, 2, -320), (0, 0, 0)),
-    ("R1", (2, 2, -320), (-2, -2, 1320)), ("tau", (-1, -3, -319), (-2, 2, 640)),
-    ("m4", (-4, -4, 1280), (8, 0, -1280)), ("de", (1, -2, 0), (-2, 0, 320)),
-    ("d2", (-2, 4, 0), (4, 0, -640)), ("X", (0, 0, -1), (0, 0, 2)), ("Z", (-1, 0, 319.5), (0, 0, -319)),
-]
-NCOLS = [
-    ("ck", (1, -1, 0)), ("base", (1, -1, 319)), ("n2n", (1, 1, -320)), ("cpk", (1, 1, 0)), ("c", (1, 0, 0)),
-    ("cm", (1, 0, -0.5)), ("X1", (-1, 1, 320)), ("k2n", (0, -2, 0)), ("k2", (0, 2, 0)), ("kh", (0, -1, 0.5)),
-]
-NF, NN = len(FCOLS), len(NCOLS)
-NL = 2 * NF + NN
-LIN = [a for _, a, _ in FCOLS] + [a for _, a in NCOLS] + [b for _, _, b in FCOLS]
-SCOL = {n: i for i, n in enumerate([n for n, _, _ in FCOLS] + [n for n, _ in NCOLS])}
+W1, W2 = 64, 20
+BIG = 4096.0
 
 F8, U8, BF, F32, I32, U16 = "float8_e4m3fn_x4", "uint8", "bfloat16", "float32", "int32", "uint16"
 SCRATCH = {"PS": ("psum", [128, 4096], F32)}
-for _n, _w in (("X0", XW), ("X1", XW), ("X2", XW), ("X3", 1280), ("UT", 512), ("VT", 512), ("BT", 512), ("ZT", 1280), ("PL", 1728),
-               ("FP", 640), ("AB", 1280), ("YP", 1280), ("ED", 516), ("EDB", 516), ("HALF", 516)):
+for _n, _w in (("X", XW), ("UT", 512), ("VT", 512), ("BT", 512), ("ZT", 1280), ("PL", 1728), ("AB", 1280), ("FP", 640), ("YP", 1280),
+               ("ED", 516), ("EDB", 516), ("HALF", 516)):
     SCRATCH[_n] = ("sbuf", [128, _w], BF)
 for _n, _w in (("QU", 128), ("UU", 256), ("QV", 128), ("QW", 512), ("EH", 512), ("EB", 512), ("QS", 128), ("QX", 320), ("QZ", 320),
                ("QF", 320), ("B0", 128), ("B1", 128), ("B2", 128), ("G0", 128), ("G1", 128), ("G2", 128)):
     SCRATCH[_n] = ("sbuf", [128, _w], F8)
     SCRATCH[_n + "s"] = ("sbuf", [128, _w], U8)
-for _n, _w in (("C16", 28), ("TJB", 28), ("TP", 20), ("TN", 20), ("Z4", 8), ("CZ", 8), ("LANE", 7), ("LAN2", 4), ("JF", 76), ("EP", 76), ("NIL", 68),
-               ("AL", NL), ("BE", NL), ("GA", NL), ("IOT", 320), ("LOR", 320), ("YO", 320), ("RMC", 65), ("RMK", 25), ("LTC", 66), ("LTK", 26),
-               ("CK", 2), ("S1", NL), ("S2", NL), ("S3", NL), ("S4", NL), ("FS", NF), ("FV", NF), ("SM", 16), ("W2", 64), ("WA", 320), ("WO", 1024)):
+for _n, _w in (("C4", 28), ("C16", 20), ("CT", 49), ("TC", 49), ("ZQ", 8), ("Z2", 8), ("LANE", 4), ("PM", 2), ("NIL", 65), ("JF", 84), ("JY", 84),
+               ("JB", 84), ("JA", 84), ("JT", 84), ("LN1", 4 * W1), ("LN2", 4 * W2), ("MX", 2 * W1), ("IOT", 320), ("LOR", 320), ("YO", 320),
+               ("RMC", 65), ("RMK", 105), ("SGC", 65), ("SGK", 105), ("CK", 16), ("QK", 21), ("W8", 64), ("WA", 320), ("WO", 256)):
     SCRATCH[_n] = ("sbuf", [128, _w], F32)
-for _n, _w in (("LI", 7), ("JI", 76), ("PO", 16), ("OQ", 56), ("OS", 56), ("O0", 56), ("O1", 56), ("OZ", 56)):
+for _n, _w in (("LI", 4), ("JI", 84), ("PO", 16), ("SH", 2 * W1), ("BB", 2 * W1)):
     SCRATCH[_n] = ("sbuf", [128, _w], I32)
-for _n, _w in (("PU", 16), ("L1", 20), ("L2", 8), ("LA", 20), ("LO", 56)):
+for _n, _w in (("PU", 16), ("LR", 8), ("L1", 20), ("L2", 8), ("LA", 20), ("LO", W1)):
     SCRATCH[_n] = ("sbuf", [128, _w], U16)
-SEMAPHORES = ["v", "a", "te", "gc", "dx", "dy", "du", "dv", "dw", "dn", "out", "arr0", "arr1", "arr2", "sent"]
+DMAS = ["d%d" % i for i in range(16)]
+SEMAPHORES = ["v", "a", "te", "gc", "out", "arr0", "arr1", "arr2", "sent"] + DMAS
 RBANK = ((0, 1, 4, 5), (6, 7, 2, 3))
-GBANK = (4, 6, 5, 7)
+GBANK = (6, 4, 7, 5)
+HBANK = ((0, 4), (1, 5), 2, 3)
 
 
 def rank_program(g, core, T, topo):
@@ -50,362 +39,391 @@ def rank_program(g, core, T, topo):
     N = len(T.cores)
     prev, nxt = T.cores[(rank - 1) % N], T.cores[(rank + 1) % N]
     queue = {"v": g.vector, "a": g.scalar, "te": g.tensor, "gc": g, "sy": g.sync}
-    total, known = {}, {}
+    total, seen, clock, uses, free = {}, {q: {} for q in queue}, {}, {}, list(DMAS)
+
+    def R(name, lo=0, hi=None, step=1):
+        return (name, lo, SCRATCH[name][1][1] if hi is None else hi, step)
+
+    def col(name, i):
+        return (name, i, i + 1, 1)
+
+    def ap(r, cast=None):
+        if not isinstance(r, tuple):
+            return r
+        if len(r) == 2:
+            return ap(r[0], cast).indirect(ap(r[1]))
+        view = T[r[0]][:, r[1]:r[2]:r[3]] if r[3] > 1 else T[r[0]][:, r[1]:r[2]]
+        return view.bitcast(cast) if cast is not None else view
 
     def wait(q, deps):
         need = {}
         for s, n in deps:
             need[s] = max(need.get(s, 0), n)
-        for s, n in need.items():
-            if known.get((q, s), 0) < n:
+        for s, n in sorted(need.items(), key=lambda e: -len(clock.get(e, {}))):
+            if seen[q].get(s, 0) < n:
                 queue[q].wait_ge(T.sem[s], n)
-                known[(q, s)] = n
+                for s2, n2 in list(clock.get((s, n), {}).items()) + [(s, n)]:
+                    seen[q][s2] = max(seen[q].get(s2, 0), n2)
 
-    def run(q, fn, deps=()):
-        wait(q, deps)
-        ins = fn(queue[q])
+    def order(q, outs, ins):
+        deps = []
+        for rs, writes in ((ins, False), (outs, True)):
+            for r in rs:
+                cols = set(range(*r[1:]))
+                for w2, cols2, q2, tok in uses.get(r[0], []):
+                    if r[0] == "PS" and q2 != q:
+                        hit = {c // 512 for c in cols} & {c // 512 for c in cols2}
+                    else:
+                        hit = (writes or w2) and not (q == q2 == "te") and not cols.isdisjoint(cols2)
+                    if hit:
+                        deps.append(tok)
+        return deps
+
+    def note(q, outs, ins, tok):
+        for rs, writes in ((ins, False), (outs, True)):
+            for r in rs:
+                cols = set(range(*r[1:]))
+                old = uses.get(r[0], [])
+                if writes and r[0] != "PS":
+                    old = [e for e in old if not e[1] <= cols]
+                uses[r[0]] = old + [(writes, cols, q, tok)]
+
+    def pieces(rs):
+        out = []
+        for r in rs:
+            if isinstance(r, tuple):
+                out += list(r) if len(r) == 2 else [r]
+        return out
+
+    def run(q, fn, outs, ins, deps=()):
+        outs, ins = pieces(outs), pieces(ins)
+        wait(q, order(q, outs, ins) + list(deps))
         total[q] = total.get(q, 0) + 1
-        ins.then_inc(T.sem[q], 1)
-        return (q, total[q])
-
-    def dma(q, out, in_, sem, deps=()):
-        wait(q, deps)
-        queue[q].dma_start(out, in_).then_inc(T.sem[sem], 16)
-        total[sem] = total.get(sem, 0) + 16
-        return (sem, total[sem])
-
-    def ts(out, in0, s1, op0, s2=None, op1=None, deps=()):
-        if op1 is None:
-            return run("v", lambda q: q.tensor_scalar(out, in0, s1, None, op0), deps)
-        return run("v", lambda q: q.tensor_scalar(out, in0, s1, s2, op0, op1), deps)
-
-    def tt(out, a, b, op, deps=()):
-        return run("v", lambda q: q.tensor_tensor(out, a, b, op), deps)
-
-    def vcopy(out, in_, deps=()):
-        return run("v", lambda q: q.tensor_copy(out, in_), deps)
-
-    def acopy(out, in_, deps=(), scale=1.0):
-        return run("a", lambda q: q.activation(out, in_, Fn.Copy, scale=scale), deps)
-
-    def affine(out, in_, bias, scale=1.0, deps=()):
-        return run("a", lambda q: q.activation(out, in_, Fn.Identity, bias=bias, scale=scale), deps)
-
-    def quant(name, lo, hi, in_, deps=()):
-        return run("v", lambda q: q.quantize_mx(T[name][:, lo:hi], T[name + "s"][:, lo:hi], in_), deps)
-
-    def mm(bank, n, w, wlo, x, xlo, deps=(), start=True, stop=True):
-        return run("te", lambda q: q.matmul_mx(T.PS[:, 512 * bank:512 * bank + n], T[w][:, wlo:wlo + 128], T[w + "s"][:, wlo:wlo + 128],
-                                               T[x][:, xlo:xlo + n], T[x + "s"][:, xlo:xlo + n], start, stop), deps)
-
-    def part(h, b, w, x, deps, start, stop):
-        lo, hi = PART[h]
-        return mm(RBANK[h][b], hi - lo, w, 128 * b, x, lo, deps, start, stop)
-
-    def bank(b, lo, hi):
-        return T.PS[:, 512 * b + lo:512 * b + hi]
-
-    def fill(ap, value):
-        return run("v", lambda q: q.memset(ap, value))
-
-    def iota(ap, pattern, base, cm, flag=True):
-        if flag:
-            return run("gc", lambda q: q.iota(ap, pattern, base, cm, allow_small_or_imprecise_dtypes=True))
-        return run("gc", lambda q: q.iota(ap, pattern, base, cm))
-
-    dx = dma("sy", T.X0[:, PAD:XW], T.x[:], "dx")
-    du = dma("a", T.UT[:], T.u[:], "du")
-    dy = dma("sy", T.X0[:, 0:128], T.x[:, 1152:1280], "dy")
-    dma("sy", T.QW[:].bitcast(dt.uint8), T.wc[:], "dw")
-    dw = dma("sy", T.QWs[:], T.ws[:], "dw")
-    dv = dma("sy", T.VT[:], T.v[:], "dv")
-
-    t_po = iota(T.PO[:], [[1, 2], [16, 8]], 0, 0, flag=False)
-    t_li = iota(T.LI[:, 0:1], [[0, 1]], 0, 1, flag=False)
-    t_c16 = iota(T.C16[:], [[16, 28]], 0, 0)
-    fill(T.NIL[:], 0.0)
-    fill(T.AL[:], 0.0)
-    fill(T.BE[:], 0.0)
-    t_nil = fill(T.GA[:], 0.0)
-    t_half = fill(T.HALF[:], 0.5)
-    t_ed = run("gc", lambda q: q.affine_select(T.ED[:], T.HALF[:], [[-1, 516]], Op.is_equal, 0.0, 3, 4), [t_half])
-    t_pad0 = iota(T.X0[:, 128:PAD], [[0, NZ]], 0, 0)
-    iota(T.JF[:, 0:8], [[16, 8]], 80, 0)
-    iota(T.JF[:, 8:28], [[4, 20]], 0, 0)
-    iota(T.JF[:, 28:56], [[4, 28]], 208, 0)
-    t_jf = iota(T.JF[:, 56:76], [[16, 20]], 0, 0)
-
-    def coefficients(name, i):
-        runs, j = [], 0
-        while j < NL:
-            e = j
-            while e < NL and LIN[e][i] == LIN[j][i]:
-                e += 1
-            if LIN[j][i] != 0:
-                runs.append((T[name][:, j:e], float(LIN[j][i]), e - j))
-            j = e
-        return runs
-
-    def put(runs):
-        for ap, value, n in runs:
-            tok = affine(ap, T.NIL[:, 0:n], value, deps=[t_nil])
+        fn(queue[q]).then_inc(T.sem[q], 1)
+        tok = (q, total[q])
+        clock[tok] = dict(seen[q])
+        note(q, outs, ins, tok)
         return tok
 
-    coef = coefficients("AL", 0) + coefficients("BE", 1) + coefficients("GA", 2)
-    put(coef[:20])
-    t_pu = vcopy(T.PU[:], T.PO[:], [t_po])
-    for i, m in ((1, 15), (2, 12), (3, 12), (4, 3), (5, 1)):
-        ts(T.LI[:, i:i + 1], T.LI[:, 0:1], m, Op.bitwise_and, deps=[t_li])
-    t_l6 = ts(T.LI[:, 6:7], T.LI[:, 0:1], 2, Op.logical_shift_right, 1, Op.bitwise_and)
-    fill(T.LTC[:, 65:66], 512.0)
-    t_lt = fill(T.LTK[:, 25:26], 320.0)
-    t_lane = vcopy(T.LANE[:], T.LI[:], [t_l6])
-    t_bt = fill(T.BT[:], 0.0)
-    t_l1 = ts(T.LANE[:, 3:4], T.LANE[:, 2:3], 0.25, Op.mult, deps=[t_lane])
-    ts(T.LANE[:, 4:5], T.LANE[:, 4:5], 320.0, Op.mult)
-    ts(T.LAN2[:, 0:2], T.LANE[:, 5:7], -1.0, Op.mult, 0.5, Op.add)
-    t_lan2 = ts(T.LAN2[:, 2:4], T.LANE[:, 5:7], 319.5, Op.mult, -159.5, Op.add)
-    lane, l4, l1, b320 = (T.LANE[:, i:i + 1] for i in (1, 2, 3, 4))
-    t_tjb = ts(T.TJB[:], T.C16[:], lane, Op.add, float(PAD), Op.add, [t_c16, t_l1])
-    shift = float(PAD + 4 * 288)
-    ts(T.Z4[:], T.C16[:, 20:28], l4, Op.add)
-    t_cz = ts(T.CZ[:], T.C16[:, 20:28], l4, Op.add, 2.0 - shift / 2, Op.add)
-    t_qu = quant("QU", 0, 128, T.UT[:], [du])
-    t_us = run("a", lambda q: q.activation(T.UUs[:], T.QUs[:].indirect(T.PU[:]), Fn.Copy), [t_qu, t_pu])
-    t_uc = run("v", lambda q: q.tensor_copy(T.UU[:].bitcast(dt.uint32), T.QU[:].bitcast(dt.uint32).indirect(T.PU[:])), [t_qu, t_pu])
-    t_ab = put(coef[20:34])
+    def dma(q, out, in_, outs, ins, sem=None):
+        wait(q, order("dma", outs, ins))
+        sem = sem or free.pop(0)
+        queue[q].dma_start(out, in_).then_inc(T.sem[sem], 16)
+        total[sem] = total.get(sem, 0) + 16
+        tok = (sem, total[sem])
+        clock[tok] = dict(seen[q])
+        note("dma", outs, ins, tok)
 
-    def a_constants():
-        eb = acopy(T.EDB[:], T.ED[:], [t_ed], scale=64.0)
-        put(coef[34:])
-        affine(T.TP[:], T.C16[:, 0:20], lane, deps=[t_c16, t_tjb, t_lan2, t_jf])
-        affine(T.JF[:, 0:8], T.JF[:, 0:8], lane)
-        affine(T.JF[:, 8:56], T.JF[:, 8:56], l1)
-        j = affine(T.JF[:, 56:76], T.JF[:, 56:76], lane)
-        affine(T.TN[:], T.TP[:], 0.0, -1.0, [j])
-        for lo, hi, i in ((0, 8, 0), (8, 56, 1), (56, 76, 0)):
-            e = affine(T.EP[:, lo:hi], T.JF[:, lo:hi], T.LAN2[:, 2 + i:3 + i], T.LAN2[:, i:i + 1])
-        return [e], j, eb
+    def load(q, r, src, cast=None):
+        dma(q, ap(r, cast), src, [r], [])
 
-    CK, FV, SMT, WA, WO = T.CK, T.FV, T.SM, T.WA, T.WO
-    C4, K4, fv = CK[:, 0:1], CK[:, 1:2], SMT[:, 0:1]
+    def ts(out, in0, s1, op0, s2=None, op1=None):
+        if op1 is None:
+            return run("v", lambda q: q.tensor_scalar(ap(out), ap(in0), ap(s1), None, op0), [out], [in0, s1])
+        return run("v", lambda q: q.tensor_scalar(ap(out), ap(in0), ap(s1), ap(s2), op0, op1), [out], [in0, s1, s2])
 
-    def sc(name):
-        i = SCOL[name]
-        return FV[:, i:i + 1] if i < NF else T.S4[:, i:i + 1]
+    def tt(out, a, b, op):
+        return run("v", lambda q: q.tensor_tensor(ap(out), ap(a), ap(b), op), [out], [a, b])
 
-    def lists(last, t_s, t_const, halves):
-        o = (56, 76) if last else (0, 56)
-        w = o[1] - o[0]
-        J, JI, E, P = T.JF[:, o[0]:o[1]], T.JI[:, o[0]:o[1]], T.EP[:, o[0]:o[1]], T.TP[:]
-        wa = lambda i: WA[:, 20 * i:20 * i + 20]
-        wo = lambda i: WO[:, 64 * i:64 * i + w]
-        it = lambda n: T[n][:, 0:w]
-        k = {"s": t_s, "con": t_const}
+    def act(out, in_, fn, bias=0.0, scale=1.0, accum=None):
+        if accum is None:
+            return run("a", lambda q: q.activation(ap(out), ap(in_), fn, bias=ap(bias), scale=ap(scale)), [out], [in_, bias, scale])
+        return run("a", lambda q: q.activation(ap(out), ap(in_), fn, bias=ap(bias), scale=ap(scale), accum_out=ap(accum)), [out, accum], [in_, bias, scale])
 
-        def step(name, fn, *deps):
-            k[name] = fn([x for d in deps for x in (k[d] if isinstance(k[d], list) else [k[d]])])
+    def copy(q, out, in_, scale=None, cast=None):
+        if q == "a":
+            if scale is None:
+                return run("a", lambda e: e.activation(ap(out), ap(in_), Fn.Copy), [out], [in_])
+            return run("a", lambda e: e.activation(ap(out), ap(in_), Fn.Copy, scale=scale), [out], [in_])
+        if scale is not None:
+            return ts(out, in_, scale, Op.mult)
+        return run("v", lambda e: e.tensor_copy(ap(out, cast), ap(in_, cast)), [out], [in_])
 
-        step("s3", lambda d: tt(T.S3[:], T.S1[:], T.GA[:], Op.add, d), "s", "con")
-        step("s4", lambda d: tt(T.S4[:], T.S3[:], T.S2[:], Op.add, d), "s3")
-        step("fs", lambda d: ts(T.FS[:], T.S4[:, NF + NN:NL], fv, Op.mult, deps=d), "s4")
-        step("m1", lambda d: ts(wa(0), P, sc("ck"), Op.is_ge, sc("n2n"), Op.mult, d), "s4")
-        step("fv", lambda d: tt(FV[:], T.FS[:], T.S4[:, 0:NF], Op.add, d), "fs")
-        step("m2", lambda d: ts(wa(1), P, sc("c"), Op.is_ge, sc("X1"), Op.mult, d), "s4")
-        step("m4x", lambda d: ts(wa(3), P, sc("cpk"), Op.is_ge, sc("k2n"), Op.mult, d), "s4")
-        t_hf = halves()
-        step("w", lambda d: affine(wa(6), P, sc("tau"), 2.0, d), "fv")
-        step("q", lambda d: affine(wo(4), J, sc("Z"), sc("X"), d), "fv")
-        for b in range(4):
-            step("f%d" % b, lambda d: acopy(T.PL[:, 432 * b:432 * b + 320], bank(b, 0, 320), [t_hf[b]]))
-            if b < 2:
-                step("p%d" % b, lambda d: acopy(T.FP[:, 320 * b:320 * b + 320], bank(b, 0, 320)))
-        ops_a = [
-            ("RB", lambda d: ts(SMT[:, 2:4], FV[:, 0:2], sc("c"), Op.max, deps=d), "fv"),
-            ("r2", lambda d: ts(wa(5), P, sc("R1"), Op.is_lt, deps=d), "fv"),
-            ("a1", lambda d: tt(wa(8), wa(0), T.TN[:], Op.add, d), "m1"),
-            ("m3", lambda d: ts(wa(2), P, SMT[:, 3:4], Op.is_ge, sc("n2n"), Op.mult, d), "RB"),
-            ("r1", lambda d: ts(wa(4), P, SMT[:, 2:3], Op.is_ge, deps=d), "RB"),
-            ("a2", lambda d: tt(wa(9), wa(1), wa(2), Op.add, d), "m2", "m3"),
-            ("rw", lambda d: tt(wa(7), wa(5), wa(4), Op.mult, d), "r2", "r1"),
-            ("a4", lambda d: tt(wa(11), wa(8), wa(9), Op.add, d), "a1", "a2"),
-            ("rv", lambda d: tt(wa(10), wa(6), wa(7), Op.mult, d), "w", "rw"),
-            ("a6", lambda d: tt(wa(12), wa(11), wa(3), Op.add, d), "a4", "m4x"),
-            ("a5", lambda d: tt(wa(13), wa(10), wa(12), Op.add, d), "rv", "a6"),
-            ("LA", lambda d: ts(T.LA[:], wa(13), sc("base"), Op.add, deps=d), "a5"),
-        ]
-        ops_o = [
-            ("t", lambda d: ts(wo(0), J, sc("m4"), Op.subtract, 0.0, Op.max, d), "fv"),
-            ("ma", lambda d: ts(wo(5), J, sc("d2"), Op.add, 320.0, Op.is_ge, d), "fv"),
-            ("Q", lambda d: ts(it("OQ"), wo(0), fv, Op.subtract, 1.0 / 3.0, Op.mult, d), "t"),
-            ("mb", lambda d: ts(wo(8), J, sc("de"), Op.add, 320.0, Op.is_ge, d), "fv"),
-            ("s5", lambda d: tt(it("OS"), it("OQ"), JI, Op.add, d), "Q"),
-            ("b1", lambda d: ts(it("O1"), it("OS"), 1, Op.logical_shift_right, 1, Op.bitwise_and, d), "s5"),
-            ("z", lambda d: ts(it("OZ"), it("OS"), 2, Op.logical_shift_right, deps=d), "s5"),
-            ("b0", lambda d: ts(it("O0"), it("OS"), 1, Op.bitwise_and, deps=d), "s5"),
-            ("sk", lambda d: ts(wo(1), it("O1"), sc("k2"), Op.mult, sc("kh"), Op.add, d), "b1"),
-            ("s12", lambda d: ts(wo(2), it("O0"), -2.0, Op.mult, 1.0, Op.add, d), "b0"),
-            ("u", lambda d: tt(wo(3), wo(1), it("OZ"), Op.add, d), "sk", "z"),
-            ("p12", lambda d: tt(wo(6), wo(2), wo(3), Op.mult, d), "s12", "u"),
-            ("da", lambda d: tt(wo(7), E, wo(6), Op.subtract, d), "p12"),
-            ("db", lambda d: tt(wo(9), wo(4), wo(6), Op.subtract, d), "q", "p12"),
-            ("xa", lambda d: tt(wo(10), wo(7), wo(5), Op.mult, d), "da", "ma"),
-            ("xb", lambda d: tt(wo(12), wo(9), wo(8), Op.mult, d), "db", "mb"),
-            ("x1", lambda d: tt(wo(13), wo(10), wo(6), Op.add, d), "xa"),
-            ("pl", lambda d: tt(wo(11), wo(13), wo(12), Op.add, d), "x1", "xb"),
-        ]
-        na, no = len(ops_a), len(ops_o)
-        for j in range(max(na, no)):
-            if j < na:
-                step(*ops_a[j])
-            if j < no:
-                step(*ops_o[j])
+    def quant(name, lo, hi, in_):
+        c, s = R(name, lo, hi), R(name + "s", lo, hi)
+        return run("v", lambda q: q.quantize_mx(ap(c), ap(s), ap(in_)), [c, s], [in_])
 
-        def finish():
-            if last:
-                return ts(T.LO[:, 0:20], wo(11), sc("cm"), Op.add, deps=[k["pl"]])
-            ts(T.LO[:, 0:8], WO[:, 704:712], sc("cm"), Op.add, deps=[k["pl"]])
-            return ts(T.LO[:, 8:56], WO[:, 712:760], sc("cm"), Op.add, b320, Op.add)
+    def bank(b, lo, hi):
+        return ("PS", 512 * b + lo, 512 * b + hi, 1)
 
-        return k, finish
+    def mm(b, n, w, wlo, x, xlo, start=True, stop=True):
+        ins = [R(w, wlo, wlo + 128), R(w + "s", wlo, wlo + 128), R(x, xlo, xlo + n), R(x + "s", xlo, xlo + n)]
+        return run("te", lambda q: q.matmul_mx(ap(bank(b, 0, n)), *[ap(r) for r in ins], start, stop), [bank(b, 0, n)], ins)
 
-    first, low, tail, behind = [dx], [dx, dy, t_pad0], None, None
+    def part(h, b, w, x, start, stop):
+        lo, hi = PART[h]
+        return mm(RBANK[h][b], hi - lo, w, 128 * b, x, lo, start, stop)
+
+    def fill(r, value):
+        return run("v", lambda q: q.memset(ap(r), value), [r], [])
+
+    def iota(r, pattern, base, cm=0):
+        if SCRATCH[r[0]][2] == I32:
+            return run("gc", lambda q: q.iota(ap(r), pattern, base, cm), [r], [])
+        return run("gc", lambda q: q.iota(ap(r), pattern, base, cm, allow_small_or_imprecise_dtypes=True), [r], [])
+
+    def scan(out, scores):
+        zero = R("NIL", 0, out[2] - out[1])
+        return run("v", lambda q: q.tensor_tensor_scan(ap(out), ap(zero), ap(scores), -1e29, Op.add, Op.max), [out], [zero, scores])
+
+    X = lambda lo, hi, b=None: R("X", PAD + 4 * lo, PAD + 4 * hi) if b is None else R("X", PAD + 4 * lo + b, PAD + 4 * hi, 4)
+
+    load("sy", X(80, 208), T.x[:, 320:832])
+    load("a", R("UT"), T.u[:])
+    load("sy", X(208, 320), T.x[:, 832:1280])
+    load("sy", X(0, 80), T.x[:, 0:320])
+    load("sy", R("QW"), T.wc[:], dt.uint8)
+    load("sy", R("QWs"), T.ws[:])
+    load("sy", R("VT"), T.v[:])
+
+    iota(col("LI", 0), [[0, 1]], 0, 1)
+    iota(R("PO"), [[1, 2], [16, 8]], 0)
+    fill(R("HALF"), 0.5)
+    iota(R("C4"), [[4, 28]], 0)
+    iota(R("C16"), [[16, 20]], 0)
+    run("gc", lambda q: q.affine_select(T.ED[:], T.HALF[:], [[-1, 516]], Op.is_equal, 0.0, 3, 4), [R("ED")], [R("HALF")])
+    iota(R("JF", 0, 8), [[16, 8]], 80)
+    iota(R("JF", 8, 28), [[4, 20]], 0)
+    iota(R("JF", 28, 56), [[4, 28]], 208)
+    iota(R("IOT"), [[1, 320]], 0)
+    fill(R("NIL"), 0.0)
+    fill(R("RMK", 0, 80), -1e29)
+    ts(col("LI", 1), col("LI", 0), 15, Op.bitwise_and)
+    ts(col("LI", 2), col("LI", 0), 2, Op.logical_shift_right, 3, Op.bitwise_and)
+    ts(col("LI", 3), col("LI", 0), 3, Op.bitwise_and)
+    copy("v", R("PU"), R("PO"))
+    copy("v", R("LANE"), R("LI"))
+    lane, l1, lb, lq = col("LANE", 1), col("LANE", 2), col("LANE", 3), col("LANE", 0)
+    fill(R("X", 0, 32), 0.0)
+    fill(R("X", 160, PAD), 0.0)
+    fill(R("BT", 448, 512), 0.0)
+    fill(col("CT", 48), -31.875)
+    fill(col("PM", 0), 1.0)
+    fill(col("PM", 1), -1.0)
+    ts(lq, lane, 0.25, Op.mult)
+    act(R("W8", 0, 8), R("C4", 20, 28), Fn.Identity, l1)
+    act(R("W8", 8, 16), R("C4", 0, 8), Fn.Identity, l1)
+    ts(R("CT", 28, 48), R("C16"), lane, Op.add, -127.5, Op.add)
+    ts(R("CT", 0, 28), R("C4"), lq, Op.add, PAD / 4 + 128, Op.add)
+    act(R("ZQ"), R("C4", 20, 28), Fn.Identity, lq)
+    act(R("Z2"), R("W8", 0, 8), Fn.Identity, -1.0, -2.0)
+    act(R("W8", 16, 24), R("W8", 8, 16), Fn.Identity, 124.0, -4.0)
+    ts(R("CT", 28, 48), R("CT", 28, 48), -1.0, Op.mult)
+    ts(R("LR"), R("W8", 16, 24), lb, Op.add)
+    cb = col("CK", 15)
+    act(cb, lb, Fn.Identity, 127.5, 320.0)
+    copy("a", R("EDB"), R("ED"), 64.0)
+    quant("QU", 0, 128, R("UT"))
+    for h in range(2):
+        pick = R("PU", 8 * h, 8 * h + 8)
+        copy("v", R("UU", 128 * h, 128 * h + 128), (R("QU"), pick), cast=dt.uint32)
+        copy("a", R("UUs", 128 * h, 128 * h + 128), (R("QUs"), pick))
+
+    def late_constants():
+        act(R("JF", 0, 8), R("JF", 0, 8), Fn.Identity, lane)
+        act(R("JF", 8, 56), R("JF", 8, 56), Fn.Identity, l1)
+        act(R("JF", 64, 84), R("C16"), Fn.Identity, lane)
+        act(R("JF", 56, 64), R("W8", 8, 16), Fn.Identity, 319.0, -1.0)
+        for b in (0, 2, 1, 3):
+            quant("EH", 128 * b, 128 * b + 128, R("ED", 3 - b, 515 - b))
+        copy("v", R("JI"), R("JF"))
+        act(R("JY"), R("JF"), Fn.Identity, -160.125)
+        act(R("JB"), R("JF"), Fn.Identity, -159.375)
+        act(R("JT"), R("JF"), Fn.Identity, -160.0, 0.5)
+        ts(R("JI"), R("JI"), 1, Op.bitwise_and)
+        act(R("LN1", 3 * W1, 4 * W1), R("JF", 0, W1), Fn.Identity)
+        act(R("LN2", 3 * W2, 4 * W2), R("JF", W1, 84), Fn.Identity)
+        ts(R("JA"), R("JI"), -0.25, Op.mult)
+        for b in (0, 2, 1, 3):
+            quant("EB", 128 * b, 128 * b + 128, R("EDB", 3 - b, 515 - b))
+        tt(R("JA"), R("JA"), R("JT"), Op.add)
+
+    C, K, rr, fj, k2, thr, k41, k21, mn = (col("CK", i) for i in (0, 1, 2, 3, 4, 5, 6, 7, 8))
+    akp, akm, ak = col("CK", 10), col("CK", 11), col("QK", 20)
+    w8 = lambda i: R("W8", 24 + 8 * i, 32 + 8 * i)
+    wa = lambda i: R("WA", 20 * i, 20 * i + 20)
+    PL = lambda b, lo=0, hi=432: R("PL", 432 * b + lo, 432 * b + hi)
+    YP = lambda b, lo=0, hi=320: R("YP", 320 * b + lo, 320 * b + hi)
+    AB = lambda b, lo, hi: R("AB", 320 * b + lo, 320 * b + hi)
+    FP = lambda b, lo, hi: R("FP", 320 * b + lo, 320 * b + hi)
+    LO = lambda lo, hi: R("LO", lo, hi)
+
     for t in range(3):
-        X, last = T["X%d" % t], t == 2
-        t_qs = quant("QS", 0, 128, X[:, PAD + 320:PAD + 832], first)
-        t_s1 = mm(6, 128, "UU", 0, "QS", 0, [t_qs, t_uc, t_us])
-        t_s2 = mm(7, 128, "UU", 128, "QS", 0)
-        if tail:
-            low = low + [tail()]
-        t1 = run("v", lambda q: q.tensor_tensor_scan(T.RMC[:], T.NIL[:, 0:65], bank(6, 48, 113), -1e29, Op.add, Op.max), [t_s1, t_nil])
-        t2 = run("v", lambda q: q.tensor_tensor_scan(T.RMK[:], T.NIL[:, 0:25], bank(7, 0, 25), -1e29, Op.add, Op.max), [t_s2])
-        t3 = ts(T.LTC[:, 0:65], T.RMC[:], T.RMC[:, 64:65], Op.is_lt, 4.0, Op.mult, [t1])
-        t4 = ts(T.LTK[:, 0:25], T.RMK[:], T.RMK[:, 24:25], Op.is_lt, 4.0, Op.mult, [t2])
-        t5 = run("v", lambda q: q.tensor_reduce(C4, T.LTC[:], AxisListType.X, Op.add), [t3, t_lt])
-        t6 = run("v", lambda q: q.tensor_reduce(K4, T.LTK[:], AxisListType.X, Op.add), [t4])
-        w2 = lambda i: T.W2[:, 8 * i:8 * i + 8]
-        fm, k8 = SMT[:, 12:13], SMT[:, 13:14]
-        t7 = ts(fm, C4, 640.0, Op.is_ge, -1.0, Op.mult, [t5])
-        t_l1 = ts(T.L1[:], T.TJB[:, 0:20], C4, Op.add, K4, Op.subtract, [t6, t_tjb])
-        t_b1 = acopy(T.BT[:, 0:320], X[:, 0:WIN].indirect(T.L1[:]), [t_l1, t_bt] + low)
-        t9 = ts(k8, K4, 2.0, Op.mult, -shift, Op.add)
-        t10 = ts(w2(1), T.CZ[:], K4, Op.add, fm, Op.mult, [t7, t_cz])
-        t8 = ts(w2(0), T.Z4[:], K4, Op.is_ge, 2.0, Op.mult)
-        tx = ts(w2(4), T.Z4[:], K4, Op.is_ge, k8, Op.mult, [t9])
-        t11 = tt(w2(2), w2(0), w2(1), Op.mult, [t8, t10])
-        tb = tt(w2(5), w2(4), T.TJB[:, 20:28], Op.add, [tx])
-        ts(fv, C4, 640.0, Op.is_lt)
-        t12 = tt(w2(3), w2(2), w2(5), Op.add, [t11, tb])
-        ts(T.S1[:], T.AL[:], C4, Op.mult, 0.25, Op.mult, [t_ab])
-        t_l2 = ts(T.L2[:], w2(3), C4, Op.add, K4, Op.subtract, [t12])
-        t_s = ts(T.S2[:], T.BE[:], K4, Op.mult, 0.25, Op.mult)
-        t_b2 = vcopy(T.BT[:, 320:448], X[:, 0:WIN].indirect(T.L2[:]), [t_l2] + low)
+        last = t == 2
+        quant("QS", 0, 128, X(80, 208))
+        mm(6, 128, "UU", 0, "QS", 0)
+        mm(7, 128, "UU", 128, "QS", 0)
+        if t == 0:
+            copy("a", R("X", 32, 160), (X(288, 320), R("LR")))
+        else:
+            copy("a", R("X", 32, 160), (R("YP"), LO(56, 64)))
+            copy("v", X(0, 32), (R("YP"), LO(8, 16)))
+            copy("a", X(32, 80), (R("YP"), LO(16, 28)))
+        scan(R("RMC"), bank(6, 48, 113))
+        scan(R("RMK", 80, 105), bank(7, 0, 25))
+        act(R("SGC"), R("RMC"), Fn.Sign, col("RMC", 64), -1.0, C)
+        act(R("SGK"), R("RMK"), Fn.Sign, col("RMK", 104), -1.0, K)
+        act(rr, C, Fn.Relu, 64.0, -2.0)
+        ts(R("TC", 0, 48), R("CT", 0, 48), C, Op.add)
+        ts(fj, C, 32.0, Op.is_lt, -88.0, Op.mult)
+        act(R("QK"), R("CT", 28, 49), Fn.Abs, C)
+        ts(w8(0), R("ZQ"), K, Op.is_ge)
+        ts(w8(1), R("Z2"), rr, Op.add, fj, Op.add)
+        ts(R("L1"), R("TC", 0, 20), K, Op.subtract, 4.0, Op.mult)
+        tt(w8(2), w8(0), w8(1), Op.mult)
+        copy("a", R("BT", 0, 320), (R("X", 0, WIN), R("L1")))
+        ts(R("CK", 10, 12), R("PM"), K, Op.mult, ak, Op.add)
+        tt(w8(3), w8(2), R("TC", 20, 28), Op.add)
+        ts(k2, K, 2.0, Op.mult)
+        ts(R("L2"), w8(3), K, Op.subtract, 4.0, Op.mult)
+        ts(mn, C, 128.0, Op.add, k2, Op.min)
+        copy("v", R("BT", 320, 448), (R("X", 0, WIN), R("L2")))
         B, G = "B%d" % t, "G%d" % t
-        t_qb = quant(B, 0, 128, T.BT[:], [t_b1, t_b2])
+        t_qb = quant(B, 0, 128, R("BT"))
         engines = topo.engines(core, prev)[:8]
         mask = sum(1 << e for e in engines)
         rid, pid = topo.addr(prev)[:2]
         wait("gc", [t_qb])
-        for out, in_ in ((T[G][:, 0:112].bitcast(dt.uint8), T[B][:, 0:112].bitcast(dt.uint8)), (T[G + "s"][:, 0:112], T[B + "s"][:, 0:112])):
-            g.remote_dma(out, in_, T.sem["arr%d" % t], T.sem.sent, pid, rid, mask)
+        for name, cast in (("", dt.uint8), ("s", None)):
+            g.remote_dma(ap(R(G + name, 0, 112), cast), ap(R(B + name, 0, 112), cast), T.sem["arr%d" % t], T.sem.sent, pid, rid, mask)
             total["sent"] = total.get("sent", 0) + len(engines)
         total["arr%d" % t] = 2 * len(topo.engines(nxt, core)[:8])
-        rest = low + ([behind()] if behind else [])
+        note("far", [R(G, 0, 112), R(G + "s", 0, 112)], [], ("arr%d" % t, total["arr%d" % t]))
         if t == 0:
             for i in range(3):
-                dma("sy", T["G%d" % i][:, 112:128].bitcast(dt.uint8), T.B0[:, 112:128].bitcast(dt.uint8), "dn", [t_qb])
-                t_gn = dma("sy", T["G%ds" % i][:, 112:128], T.B0s[:, 112:128], "dn")
-            t_con, t_j, t_edb = a_constants()
-            for n in ("X1", "X2"):
-                t_pad = iota(T[n][:, 128:PAD], [[0, NZ]], 0, 0)
-            t_iot = iota(T.IOT[:], [[1, 320]], 0, 0)
-            for b in range(4):
-                t_eh = quant("EH", 128 * b, 128 * b + 128, T.ED[:, 3 - b:515 - b], [t_ed])
-            for b in range(4):
-                t_eb = quant("EB", 128 * b, 128 * b + 128, T.EDB[:, 3 - b:515 - b], [t_edb])
-            t_con.append(vcopy(T.JI[:], T.JF[:], [t_j]))
+                for name, cast in (("", dt.uint8), ("s", None)):
+                    dst, src = R("G%d%s" % (i, name), 112, 128), R("B0" + name, 112, 128)
+                    dma("sy", ap(dst, cast), ap(src, cast), [dst], [src])
+            late_constants()
+        else:
+            copy("a", X(208, 320), (R("YP"), LO(28, 56)))
 
-        def halves(X=X, rest=rest, t_eh=t_eh):
-            qx = quant("QX", 0, 320, X[:, PAD:XW], rest)
-            return [mm(b, 320, "EH", 128 * b, "QX", 0, [qx, t_eh]) for b in range(4)]
-
-        k, finish = lists(last, [t_s], t_con, halves)
+        j0, w, LN = (W1, W2, "LN2") if last else (0, W1, "LN1")
+        J = lambda n: R(n, j0, j0 + w)
+        ln = lambda i, e=None: R(LN, w * i, w * (e or i + 1))
+        wo = lambda i: R("WO", 64 * i, 64 * i + w)
+        TN = R("TC", 28, 48)
+        quant("QX", 0, 192, X(0, 192))
         for b in range(2):
-            part(0, b, "EB", "QX", [k["p%d" % b], t_eb], True, False)
-        if t == 0:
-            t_qv = quant("QV", 0, 128, T.VT[:], [dv])
-        if last:
-            t_lo = finish()
-            t_lor = run("a", lambda q: q.activation(T.LOR[:], T.IOT[:].indirect(T.LO[:, 0:20]), Fn.Copy), [t_lo, t_iot])
-            dma("sy", T.lo[:], T.LOR[0:128:16, :], "out", [t_lor])
-        t_g = {}
+            mm(HBANK[b][0], 192, "EH", 128 * b, "QX", 0)
+        act(wa(0), TN, Fn.Abs, K, -2.0)
+        act(thr, C, Fn.Identity, 192.0, -1.0)
+        act(wa(1), wa(0), Fn.Abs, k2, -1.0)
+        act(wa(2), R("QK", 0, 20), Fn.Abs, K, -1.0)
+        act(k41, K, Fn.Identity, -1.0, 4.0)
+        act(k21, K, Fn.Identity, 1.0, -2.0)
+        act(wa(3), wa(2), Fn.Identity, thr)
+        ts(ln(0), J("JY"), akp, Op.add, 4.0 / 3.0, Op.mult)
+        ts(ln(1), J("JB"), akm, Op.add, 4.0, Op.mult)
+        ts(ln(2), J("JA"), K, Op.add, 4.0, Op.mult)
+        quant("QX", 192, 320, X(192, 320))
         for b in (0, 2, 1, 3):
-            t_g[b] = mm(GBANK[b], 128, "EH", 128 * b, G, 0, [("arr%d" % t, total["arr%d" % t]), t_gn])
-        win = lambda b: T.PL[:, 432 * b:432 * b + 432]
-        late = lambda b: T.PL[:, 432 * b + 320:432 * b + 432]
-        la = lambda h: T.LA[:, PART[h][0] // 16:PART[h][1] // 16]
-        zt = lambda b, h: T.ZT[:, 4 * PART[h][0] + b:4 * PART[h][1]:4]
-        at = lambda buf, b, h: buf[:, 320 * b + PART[h][0]:320 * b + PART[h][1]]
-        t_c, t_a, t_z = {}, {}, {}
-        for h in range(2):
-            for b in (2, 3):
-                if h == 0:
-                    t_c[b] = acopy(late(b), bank(GBANK[b], 0, 112), [t_g[b]])
-                t_a[b, h] = acopy(at(T.AB, b, h), win(b).indirect(la(h)), [k["LA"], t_c[b]])
-        for h in range(2):
-            for b in (0, 1):
-                if h == 0:
-                    t_c[b] = vcopy(late(b), bank(GBANK[b], 0, 112), [t_g[b]])
-                tt(zt(b, h), win(b).indirect(la(h)), at(T.FP, b, h), Op.add, [t_c[b], k["LA"], k["f3"]])
-            if h == 0:
-                part(0, 2, "EB", "QX", [t_c[0]], True, False)
-                part(0, 3, "EB", "QX", [t_c[2]], True, False)
-                part(1, 0, "EB", "QX", [t_c[1]], True, False)
-                part(1, 1, "EB", "QX", [t_c[3]], True, False)
-            for b in (2, 3):
-                t_z[b, h] = tt(zt(b, h), bank(b, *PART[h]), at(T.AB, b, h), Op.add, [t_a[b, h]] + ([t_z["pre", b]] if h else []))
-                if h == 0:
-                    t_z["pre", b] = part(1, b, "EB", "QX", [t_z[b, 0]], True, False)
-            lo, hi = PART[h]
-            t_z[h] = quant("QZ", lo, hi, T.ZT[:, 4 * lo:4 * hi], [t_z[3, h]])
-        t_r = [[part(h, b, "QW", "QZ", [t_z[h], dw], False, True) for b in range(4)] for h in range(2)]
-        new = [acopy(at(T.YP, b, 0), bank(RBANK[0][b], 0, 192), [t_r[0][b]], scale=0.03125) for b in range(4)]
-        if not last:
-            t_lo = finish()
-        XN, YP, LO = T["X%d" % (t + 1)], T.YP, T.LO
-        for b in range(4):
-            src, copy = bank(RBANK[1][b], 0, 128), (vcopy, acopy)[b % 2]
-            if b % 2 == 0:
-                ty = ts(at(YP, b, 1), src, 0.03125, Op.mult, deps=[t_r[1][b]])
+            if b < 2:
+                mm(HBANK[b][1], 128, "EH", 128 * b, "QX", 192)
             else:
-                ty = acopy(at(YP, b, 1), src, [t_r[1][b]], scale=0.03125)
-            window, deps = YP[:, 320 * b:320 * b + 320], [ty, new[b], t_lo]
-            new.append(ty)
-            if last:
-                new.append(copy(XN[:, b:768:4], window.indirect(LO[:, 0:12]), deps))
-            else:
-                new.append(copy(XN[:, PAD + 320 + b:PAD + 832:4], window.indirect(LO[:, 0:8]), deps))
-        first = list(new)
-        if not last:
-            r1 = acopy(XN[:, 0:128], YP[:].indirect(LO[:, 48:56]), new)
-            r2 = acopy(XN[:, PAD + 128:PAD + 320], YP[:].indirect(LO[:, 16:28]))
-            tail = lambda XN=XN, new=new: vcopy(XN[:, PAD:PAD + 128], T.YP[:].indirect(T.LO[:, 8:16]), new)
-            behind = lambda XN=XN: acopy(XN[:, PAD + 832:XW], T.YP[:].indirect(T.LO[:, 28:56]))
-            low = new + [r1, r2, t_pad]
+                mm(HBANK[b], 320, "EH", 128 * b, "QX", 0)
+        tt(R("MX", 0, 2 * w), ln(0, 2), ln(2, 4), Op.max)
+        ts(wa(4), wa(1), K, Op.is_lt, k2, Op.mult)
+        tt(R("SH", 0, w), R("MX", 0, w), R("MX", w, 2 * w), Op.max)
+        tt(wa(5), wa(4), TN, Op.add)
+        ts(R("SH", w, 2 * w), R("SH", 0, w), 1, Op.logical_shift_right)
 
-    second = []
+        def plane(b, h=None):
+            if b < 2:
+                lo, hi = PART[h]
+                copy("a", PL(b, lo, hi), bank(HBANK[b][h], 0, hi - lo))
+            else:
+                copy("a", PL(b, 0, 320), bank(HBANK[b], 0, 320))
+
+        plane(0, 0)
+        plane(0, 1)
+        act(wa(6), wa(5), Fn.Sign, thr, -1.0)
+        plane(2)
+        plane(1, 0)
+        plane(1, 1)
+        plane(3)
+        ts(R("BB", 0, 2 * w), R("SH", 0, 2 * w), 1, Op.bitwise_and)
+        tt(wa(7), wa(5), wa(6), Op.mult)
+        ts(wo(0), R("BB", w, 2 * w), k41, Op.mult, k21, Op.add)
+        ts(wa(8), wa(7), mn, Op.add, -BIG, Op.mult)
+        ts(wo(1), R("BB", 0, w), -1.0, Op.mult, 0.5, Op.add)
+        tt(wa(9), wa(8), wa(3), Op.min)
+        tt(wo(2), wo(0), R("SH", w, 2 * w), Op.add)
+        tt(wa(10), wa(9), wa(7), Op.max)
+        tt(wo(3), wo(2), wo(1), Op.mult)
+        ts(R("LA"), wa(10), C, Op.add, 127.5, Op.add)
+        copy("v", FP(0, 0, 320), PL(0, 0, 320))
+        if t == 0:
+            quant("QV", 0, 128, R("VT"))
+        la = lambda h: R("LA", PART[h][0] // 16, PART[h][1] // 16)
+        zt = lambda b, h: R("ZT", 4 * PART[h][0] + b, 4 * PART[h][1], 4)
+        unpack = lambda b: mm(GBANK[b], 128, "EH", 128 * b, G, 0)
+        late = lambda q, b: copy(q, PL(b, 320, 432), bank(GBANK[b], 0, 112))
+        fused = lambda b, h: tt(zt(b, h), (PL(b), la(h)), FP(b, *PART[h]), Op.add)
+        gather = lambda b, h: copy("a", AB(b, *PART[h]), (PL(b), la(h)))
+        add = lambda b, h: tt(zt(b, h), bank(HBANK[b], *PART[h]), AB(b, *PART[h]), Op.add)
+        part(0, 0, "EB", "QX", True, False)
+        for b in (0, 2, 1, 3):
+            unpack(b)
+        part(0, 1, "EB", "QX", True, False)
+        late("v", 0)
+        late("a", 2)
+        copy("v", FP(1, 0, 320), PL(1, 0, 320))
+        fused(0, 0)
+        gather(2, 0)
+        late("v", 1)
+        late("a", 3)
+        gather(3, 0)
+        for h, b in ((1, 0), (1, 1), (0, 2), (0, 3)):
+            part(h, b, "EB", "QX", True, False)
+        add(2, 0)
+        part(1, 2, "EB", "QX", True, False)
+        fused(1, 0)
+        add(3, 0)
+        part(1, 3, "EB", "QX", True, False)
+        gather(2, 1)
+        gather(3, 1)
+        if last:
+            ts(LO(0, 20), wo(3), C, Op.add, 127.5, Op.add)
+        else:
+            ts(LO(0, 8), R("WO", 192, 200), C, Op.add, 127.5, Op.add)
+        quant("QZ", 0, 192, R("ZT", 0, 768))
+        for b in range(4):
+            part(0, b, "QW", "QZ", False, True)
+        fused(0, 1)
+        fused(1, 1)
+        add(2, 1)
+        add(3, 1)
+        if not last:
+            ts(LO(8, 64), R("WO", 200, 256), C, Op.add, cb, Op.add)
+        quant("QZ", 192, 320, R("ZT", 768, 1280))
+        for b in range(4):
+            part(1, b, "QW", "QZ", False, True)
+        if last:
+            copy("a", R("LOR"), (R("IOT"), LO(0, 20)))
+            dma("sy", T.lo[:], T.LOR[0:128:16, :], [], [R("LOR")], "out")
+        for b in range(4):
+            copy("a", YP(b, 0, 192), bank(RBANK[0][b], 0, 192), 0.03125)
+        for b in range(4):
+            q = "va"[b % 2]
+            copy(q, YP(b, 192, 320), bank(RBANK[1][b], 0, 128), 0.03125)
+            if last:
+                copy(q, X(0, 192, b), (YP(b), LO(0, 12)))
+            else:
+                copy(q, X(80, 208, b), (YP(b), LO(0, 8)))
+
     for b in range(4):
-        second.append((vcopy, acopy)[b % 2](XN[:, 768 + b:1280:4], YP[:, 320 * b:320 * b + 320].indirect(LO[:, 12:20]), new))
+        copy("va"[b % 2], X(192, 320, b), (YP(b), LO(12, 20)))
         if b == 0:
-            t_q0 = quant("QF", 0, 192, XN[:, 0:768], first)
-    t_q1 = quant("QF", 192, 320, XN[:, 768:1280], second)
-    t_y0 = mm(2, 192, "QV", 0, "QF", 0, [t_q0, t_qv])
-    t_y1 = mm(3, 128, "QV", 0, "QF", 192, [t_q1])
-    t_o0 = acopy(T.YO[:, 0:192], bank(2, 0, 192), [t_y0])
-    dma("a", T.y[:, 0:192], T.YO[:, 0:192], "out", [t_o0])
-    dma("sy", T.oc[:], T.QF[:].bitcast(dt.uint8), "out", [t_q0, t_q1])
-    t_o1 = vcopy(T.YO[:, 192:320], bank(3, 0, 128), [t_y1])
+            quant("QF", 0, 192, X(0, 192))
+    quant("QF", 192, 320, X(192, 320))
+    mm(2, 192, "QV", 0, "QF", 0)
+    mm(3, 128, "QV", 0, "QF", 192)
+    copy("a", R("YO", 0, 192), bank(2, 0, 192))
+    dma("a", T.y[:, 0:192], T.YO[:, 0:192], [], [R("YO", 0, 192)], "out")
+    dma("sy", T.oc[:], T.QF[:].bitcast(dt.uint8), [], [R("QF")], "out")
+    copy("v", R("YO", 192, 320), bank(3, 0, 128))
     for i in range(4):
-        dma("a" if i < 2 else "sy", T.osc[4 * i:4 * i + 4, :], T.QFs[32 * i:32 * i + 4, :], "out", [t_q0, t_q1])
-    dma("sy", T.y[:, 192:320], T.YO[:, 192:320], "out", [t_o1])
+        dma("a" if i < 2 else "sy", T.osc[4 * i:4 * i + 4, :], T.QFs[32 * i:32 * i + 4, :], [], [R("QFs")], "out")
+    dma("sy", T.y[:, 192:320], T.YO[:, 192:320], [], [R("YO", 192, 320)], "out")
     wait("gc", list(total.items()))

@@ -1,5 +1,4 @@
-import numpy as np
-from concourse.mybir import AluOpType as Op, AxisListType, ActivationFunctionType as Fn, dt
+from concourse.mybir import AluOpType as Op, ActivationFunctionType as Fn, dt
 
 PAD = 384
 XW = PAD + 1280
@@ -17,7 +16,7 @@ for _n, _w in (("QU", 128), ("UU", 256), ("QV", 128), ("QW", 512), ("EH", 512), 
                ("QF", 320), ("B0", 128), ("B1", 128), ("B2", 128), ("G0", 128), ("G1", 128), ("G2", 128)):
     SCRATCH[_n] = ("sbuf", [128, _w], F8)
     SCRATCH[_n + "s"] = ("sbuf", [128, _w], U8)
-for _n, _w in (("C4", 28), ("C16", 20), ("CT", 49), ("TC", 49), ("ZQ", 8), ("Z2", 8), ("LANE", 4), ("PM", 2), ("NIL", 65), ("JF", 84), ("JY", 84),
+for _n, _w in (("C4", 28), ("C16", 20), ("CT", 51), ("TC", 51), ("ZQ", 8), ("Z2", 8), ("LANE", 4), ("PM", 2), ("NIL", 65), ("JF", 84), ("JY", 84),
                ("JB", 84), ("JA", 84), ("JT", 84), ("LN1", 4 * W1), ("LN2", 4 * W2), ("MX", 2 * W1), ("IOT", 320), ("LOR", 320), ("YO", 320),
                ("RMC", 65), ("RMK", 105), ("SGC", 65), ("SGK", 105), ("CK", 16), ("QK", 21), ("W8", 64), ("WA", 320), ("WO", 256)):
     SCRATCH[_n] = ("sbuf", [128, _w], F32)
@@ -26,10 +25,38 @@ for _n, _w in (("LI", 4), ("JI", 84), ("PO", 16), ("SH", 2 * W1), ("BB", 2 * W1)
 for _n, _w in (("PU", 16), ("LR", 8), ("L1", 20), ("L2", 8), ("LA", 20), ("LO", W1)):
     SCRATCH[_n] = ("sbuf", [128, _w], U16)
 DMAS = ["d%d" % i for i in range(16)]
-SEMAPHORES = ["v", "a", "te", "gc", "out", "arr0", "arr1", "arr2", "sent"] + DMAS
-RBANK = ((0, 1, 4, 5), (6, 7, 2, 3))
+SEMAPHORES = ["v", "a", "t", "g", "out", "arr0", "arr1", "arr2", "sent"] + DMAS
+RBANK = ((0, 7, 4, 5), (6, 1, 2, 3))
 GBANK = (6, 4, 7, 5)
-HBANK = ((0, 4), (1, 5), 2, 3)
+ORDER = """
+cUT0:a cX704:s cCT49:v cLI0:g cJF0:g cJF28:g cC160:g cC40:g cCT48:v cNIL0:v cLI1:v cLI3:v cLI2:v cX0:v cLANE0:v cCT50:v cW88:a cW80:a cZ20:a cW816:a
+cX160:v cX1216:s cX384:s cQW0:s cQWs0:s cVT0:s cLANE0':a cZQ0:a cCT28:v cHALF0:v cPO0:g cPU0:v cQU0:v cUUs0:a cLR0:v cUU0:v cQS0:v cUU128:v cCT0:v
+cUUs128:a cCT28':a 0JF0:a 0UU0QS0:t 0RMC0:v 0JF56:a cJF8:g 0JF8:a 0SGC0:a cRMK0:v cPM1:v 0UU1QS0:t 0RMK80:v 0JF64:a 0CK2:v 0CK3:v 0TC0:v 0W832:v
+0SGK0:a 0W824:v 0L10:v 0X32:a 0W840:v 0BT0:a 0CK4:a 0JB0:a 0JI0:v 0QK0:a 0JY0:a 0W848:v 0L20:v cBT448:v 0BT320:v cED0:g cPM0:v 0CK10:a 0B00:v 0G0112:s
+0G0s112:s 0G1112:s 0G2112:s 0G1s112:s 0G2s112:s 0JI0':v 0EH384:v 0QX192:v 0G00:g 0EH256:v 0EH128:v 0QX0:v 0EH1QX0:t 0EDB0:a 0JT0:a 0WA0:a 0WA20:a
+0LN10:v 0EB0:v 0WA40:a 0CK5:a 0EH3QX0:t 0EB0QX0:t 0LN164:v 0JA0:v 0EB128:v 0WA80:v 0WA60:a 0JA0':v 0WA100:v 0CK6:v 0PL432:a 0LN1192:a 0EB1QX192:t
+0EB0QX192:t 0PL0:a 0EB0QX0':t 0EH2QX0:t 0WA120:a 0QV0:v 0LN1128:v 0EB256:v 0WA140:v 0PL192:a 0EH1G00:t 0PL1296:a 0LN260:a 0MX0:v 0WA160:v 0SH0:v
+0WA180:v cIOT0:g 0FP320:g 0PL864:a cCK15:a 0PL752:a 0EB0G00:t 0PL320:a 0EH2G00:t 0PL1184:a 0EH3G00:t 0BB64:v 0SH64:v 0EB384:v 0WA200:v 0WO0:v 0LA0:v
+0AB640:a 0WO128:v 0ZT1:v 0PL1616:v 0FP0:g 0ZT0:v 0EB2QX0:t 0EB3QX0:t 0EB1QX0:t 0ZT2:v 0EB2QX192:t 0EB0QX192':t 0AB960:a 0ZT3:v 0EB3QX192:t 0BB0:v
+0QZ0:v 0QW3QZ0:t 0QW2QZ0:t 0QW1QZ0:t 0AB832:a 0AB1152:a 0AB512:a 0YP960:a 0YP640:a 0YP320:a 0QW0QZ0:t 0ZT770:v 0ZT768:v 0ZT769:v 0ZT771:v 0WO64:v
+0QZ192:v 0QW0QZ192:t 0YP192:a 0QW1QZ192:t 0YP512:a 0QW2QZ192:t 0YP832:a 0WO192:v 0YP0:v 0LO0:v 0X704:v 0X705:a 0QW3QZ192:t 0YP1152:v 0X706:a 0LO8:v
+0X707:v 1QS0:v 1UU0QS0:t 1X32:a 1X512:a 1X1216:v 1RMC0:v 1UU1QS0:t 1RMK80:v 1SGC0:a 1CK2:v 1CK3:v 1SGK0:a 1W824:v 1W832:v 1TC0:a 1L10:v 1W840:v 1CK4:v
+1W848:v 1LN1128:v 1L20:v 1X384:a 1QK0:a 1BT0:a 1BT320:v 1B10:v 1G10:g 1QX0:v 1EB0QX0:t 1X1440:a 1QX192:v 1EH1QX0:t 1WA40:a 1WA0:a 1CK10:a 1LN10:v
+1WA20:a 1WA80:v 1LN164:v 1WA60:a 1CK5:a 1WA100:v 1EB0QX192:t 1EH3QX0:t 1EH2QX0:t 1PL0:a 1CK6:v 1MX0:v 1WA120:a 1WA140:v 1PL432:a 1EB1QX192:t
+1EB0QX0':t 1PL192:a 1SH0:v 1WA160:v 1BB64:v 1WA180:v 1SH64:v 1BB0:v 1WO0:v 1PL1296:a 1WA200:v 1WO128:v 1PL864:a 1EH2G10:t 1PL1184:a 1LA0:v 1AB640:a
+1EB0G10:t 1PL320:v 1FP0:g 1ZT0:v 1EH1G10:t 1EH3G10:t 1PL1616:a 1ZT2:v 1FP320:g 1PL752:a 1ZT1:v 1EB1QX0:t 1EB0QX192':t 1EB2QX0:t 1EB3QX0:t 1EB2QX192:t
+1AB960:a 1ZT3:v 1EB3QX192:t 1WO64:v 1QZ0:v 1QW1QZ0:t 1ZT768:v 1AB832:a 1AB1152:a 1ZT771:v 1AB512:a 1ZT770:v 1ZT769:v 1QZ192:v 1YP320:a 1QW2QZ0:t
+1YP640:a 1QW3QZ0:t 1YP960:a 1WO192:v 1LO0:v 1QW0QZ0:t 1QW0QZ192:t 1YP192:v 1YP0:a 1X704:v 1QW1QZ192:t 1YP512:a 1QW2QZ192:t 1YP832:a 1X705:a
+1QW3QZ192:t 1YP1152:v 1LO8:v 1X706:a 1X707:v 2QS0:v 2X384:v 2UU0QS0:t 2RMC0:v 2UU1QS0:t 2RMK80:v 2X32:a 2X512:a 2QX0:v 2EB0QX0:t 2SGC0:a 2CK2:v 2CK3:v
+2SGK0:a 2W824:v 2W832:v 2QK0:a 2TC0:a 2L10:v 2X1440:a 2W840:v 2W848:v 2CK10:v 2L20:v 2CK4:v 2BT0:a 2BT320:v 2B20:v 2LN20:v 2LN220:v 2X1216:a 2QX192:v
+2EB0QX192:t 2EH1QX0:t 2EH3QX0:t 2WA0:a 2WA40:a 2WA20:a 2LN240:v 2WA80:v 2CK6:v 2PL0:a 2EB0QX0':t 2WA100:v 2WA60:a 2WA120:a 2PL192:a 2PL432:a 2PL1296:a
+2EH2QX0:t 2PL864:a 2MX0:v 2CK5:v 2SH0:v 2WA140:v 2BB0:v 2BB20:v 2WA160:v 2WO64:v 2WA180:v 2WO0:v 2SH20:v 2WA200:v 2WO128:v 2LA0:v 2G20:g 2EB0G20:t
+2PL320:v 2WO192:v 2FP0:g 2ZT0:v 2ZT768:v 2EH2G20:t 2PL1184:a 2AB640:a 2ZT2:v 2EH3G20:t 2PL1616:a 2EH1G20:t 2EB1QX192:t 2EB0QX192':t 2EB1QX0:t 2PL752:a
+2FP320:g 2ZT1:v 2EB2QX0:t 2EB3QX0:t 2EB2QX192:t 2AB960:a 2ZT3:v 2EB3QX192:t 2LO0:v 2QZ0:v 2QW0QZ0:t 2QW2QZ0:t 2QW3QZ0:t 2QW1QZ0:t 2AB512:a 2ZT769:v
+2AB832:a 2ZT770:v 2AB1152:a 2ZT771:v 2LOR0:a 2lo:s 2QZ192:v 2QW0QZ192:t 2YP0:v 2YP640:v 2YP320:v 2YP960:a 2YP192:a 2X384':v 2QW1QZ192:t 2YP512:a
+2QW3QZ192:t 2QW2QZ192:t 2YP832:v 2YP1152:a 2X387:v eX1152:v 2X385:a 2X386:a eQF0:v eQV0QF0:t eoc0:s eX1155:v eX1153:a eX1154:a eQF192:v eoc1:a
+eQV0QF192:t eYO0:v ey0:s eosc3:s eosc2:s eYO192:a eosc1:a eosc0:s ey1:s
+"""
 
 
 def rank_program(g, core, T, topo):
@@ -38,8 +65,9 @@ def rank_program(g, core, T, topo):
         return
     N = len(T.cores)
     prev, nxt = T.cores[(rank - 1) % N], T.cores[(rank + 1) % N]
-    queue = {"v": g.vector, "a": g.scalar, "te": g.tensor, "gc": g, "sy": g.sync}
+    queue = {"v": g.vector, "a": g.scalar, "t": g.tensor, "g": g, "s": g.sync}
     total, seen, clock, uses, free = {}, {q: {} for q in queue}, {}, {}, list(DMAS)
+    calls, stage = {}, ["c"]
 
     def R(name, lo=0, hi=None, step=1):
         return (name, lo, SCRATCH[name][1][1] if hi is None else hi, step)
@@ -55,6 +83,20 @@ def rank_program(g, core, T, topo):
         view = T[r[0]][:, r[1]:r[2]:r[3]] if r[3] > 1 else T[r[0]][:, r[1]:r[2]]
         return view.bitcast(cast) if cast is not None else view
 
+    def pieces(rs):
+        out = []
+        for r in rs:
+            if isinstance(r, tuple):
+                out += list(r) if len(r) == 2 else [r]
+        return out
+
+    def call(forms, outs, ins, kind="run", name=None):
+        outs, ins = pieces(outs), pieces(ins)
+        name = stage[0] + (name or outs[0][0] + str(outs[0][1]))
+        while name in calls:
+            name += "'"
+        calls[name] = (forms, outs, ins, kind)
+
     def wait(q, deps):
         need = {}
         for s, n in deps:
@@ -65,123 +107,119 @@ def rank_program(g, core, T, topo):
                 for s2, n2 in list(clock.get((s, n), {}).items()) + [(s, n)]:
                     seen[q][s2] = max(seen[q].get(s2, 0), n2)
 
-    def order(q, outs, ins):
-        deps = []
-        for rs, writes in ((ins, False), (outs, True)):
+    def issue(name, q):
+        forms, outs, ins, kind = calls[name]
+        deps, who = [], q if kind == "run" else "dma"
+        for rs, writes in ((ins, False), (outs if kind != "far" else [], True)):
             for r in rs:
                 cols = set(range(*r[1:]))
                 for w2, cols2, q2, tok in uses.get(r[0], []):
-                    if r[0] == "PS" and q2 != q:
-                        hit = {c // 512 for c in cols} & {c // 512 for c in cols2}
+                    if seen[q].get(tok[0], 0) >= tok[1]:
+                        hit = False
+                    elif r[0] == "PS" and q2 != who:
+                        hit = r[1] // 512 == min(cols2) // 512
                     else:
-                        hit = (writes or w2) and not (q == q2 == "te") and not cols.isdisjoint(cols2)
+                        hit = (writes or w2) and not (who == q2 == "t") and not cols.isdisjoint(cols2)
                     if hit:
                         deps.append(tok)
-        return deps
-
-    def note(q, outs, ins, tok):
+        wait(q, deps)
+        if kind == "far":
+            tok = forms[q](queue[q])
+            ins = []
+        else:
+            sem, n = (q, 1) if kind == "run" else ("out" if kind == "out" else free.pop(0), 16)
+            forms[q](queue[q]).then_inc(T.sem[sem], n)
+            total[sem] = total.get(sem, 0) + n
+            tok = (sem, total[sem])
+            clock[tok] = dict(seen[q])
         for rs, writes in ((ins, False), (outs, True)):
             for r in rs:
                 cols = set(range(*r[1:]))
                 old = uses.get(r[0], [])
                 if writes and r[0] != "PS":
                     old = [e for e in old if not e[1] <= cols]
-                uses[r[0]] = old + [(writes, cols, q, tok)]
+                uses[r[0]] = old + [(writes, cols, who, tok)]
 
-    def pieces(rs):
-        out = []
-        for r in rs:
-            if isinstance(r, tuple):
-                out += list(r) if len(r) == 2 else [r]
-        return out
+    def load(q, r, src, cast=None, ins=()):
+        call({q: lambda e: e.dma_start(ap(r, cast), src)}, [r], ins, "dma")
 
-    def run(q, fn, outs, ins, deps=()):
-        outs, ins = pieces(outs), pieces(ins)
-        wait(q, order(q, outs, ins) + list(deps))
-        total[q] = total.get(q, 0) + 1
-        fn(queue[q]).then_inc(T.sem[q], 1)
-        tok = (q, total[q])
-        clock[tok] = dict(seen[q])
-        note(q, outs, ins, tok)
-        return tok
+    def store(qs, dst, src, r, name):
+        call({q: lambda e: e.dma_start(dst, src) for q in qs}, [], [r], "out", name)
 
-    def dma(q, out, in_, outs, ins, sem=None):
-        wait(q, order("dma", outs, ins))
-        sem = sem or free.pop(0)
-        queue[q].dma_start(out, in_).then_inc(T.sem[sem], 16)
-        total[sem] = total.get(sem, 0) + 16
-        tok = (sem, total[sem])
-        clock[tok] = dict(seen[q])
-        note("dma", outs, ins, tok)
-
-    def load(q, r, src, cast=None):
-        dma(q, ap(r, cast), src, [r], [])
+    def ts_form(out, in0, s1, op0, s2=None, op1=None):
+        if op1 is None:
+            return lambda e: e.tensor_scalar(ap(out), ap(in0), ap(s1), None, op0)
+        return lambda e: e.tensor_scalar(ap(out), ap(in0), ap(s1), ap(s2), op0, op1)
 
     def ts(out, in0, s1, op0, s2=None, op1=None):
-        if op1 is None:
-            return run("v", lambda q: q.tensor_scalar(ap(out), ap(in0), ap(s1), None, op0), [out], [in0, s1])
-        return run("v", lambda q: q.tensor_scalar(ap(out), ap(in0), ap(s1), ap(s2), op0, op1), [out], [in0, s1, s2])
+        call({"v": ts_form(out, in0, s1, op0, s2, op1)}, [out], [in0, s1, s2])
 
     def tt(out, a, b, op):
-        return run("v", lambda q: q.tensor_tensor(ap(out), ap(a), ap(b), op), [out], [a, b])
+        call({"v": lambda e: e.tensor_tensor(ap(out), ap(a), ap(b), op)}, [out], [a, b])
 
     def act(out, in_, fn, bias=0.0, scale=1.0, accum=None):
-        if accum is None:
-            return run("a", lambda q: q.activation(ap(out), ap(in_), fn, bias=ap(bias), scale=ap(scale)), [out], [in_, bias, scale])
-        return run("a", lambda q: q.activation(ap(out), ap(in_), fn, bias=ap(bias), scale=ap(scale), accum_out=ap(accum)), [out, accum], [in_, bias, scale])
+        more = {} if accum is None else {"accum_out": ap(accum)}
+        call({"a": lambda e: e.activation(ap(out), ap(in_), fn, bias=ap(bias), scale=ap(scale), **more)}, [out, accum], [in_, bias, scale])
 
-    def copy(q, out, in_, scale=None, cast=None):
-        if q == "a":
-            if scale is None:
-                return run("a", lambda e: e.activation(ap(out), ap(in_), Fn.Copy), [out], [in_])
-            return run("a", lambda e: e.activation(ap(out), ap(in_), Fn.Copy, scale=scale), [out], [in_])
-        if scale is not None:
-            return ts(out, in_, scale, Op.mult)
-        return run("v", lambda e: e.tensor_copy(ap(out, cast), ap(in_, cast)), [out], [in_])
+    def either(q, forms):
+        return {p: forms[p] for p in q + "".join(p for p in forms if p != q)}
+
+    def lin(q, out, in_, bias, scale=1.0):
+        call(either(q, {"v": ts_form(out, in_, scale, Op.mult, bias, Op.add),
+                        "a": lambda e: e.activation(ap(out), ap(in_), Fn.Identity, bias=ap(bias), scale=ap(scale))}), [out], [in_, bias, scale])
+
+    def copy(q, out, in_, scale=None, more=None):
+        if scale is None:
+            forms = {"v": lambda e: e.tensor_copy(ap(out), ap(in_)), "a": lambda e: e.activation(ap(out), ap(in_), Fn.Copy)}
+        else:
+            forms = {"v": ts_form(out, in_, scale, Op.mult), "a": lambda e: e.activation(ap(out), ap(in_), Fn.Copy, scale=scale)}
+        call(either(q, dict(forms, **(more or {}))), [out], [in_])
+
+    def cast(out, in_, as_=None):
+        call({"v": lambda e: e.tensor_copy(ap(out, as_), ap(in_, as_))}, [out], [in_])
 
     def quant(name, lo, hi, in_):
         c, s = R(name, lo, hi), R(name + "s", lo, hi)
-        return run("v", lambda q: q.quantize_mx(ap(c), ap(s), ap(in_)), [c, s], [in_])
+        call({"v": lambda e: e.quantize_mx(ap(c), ap(s), ap(in_))}, [c, s], [in_])
 
     def bank(b, lo, hi):
         return ("PS", 512 * b + lo, 512 * b + hi, 1)
 
     def mm(b, n, w, wlo, x, xlo, start=True, stop=True):
         ins = [R(w, wlo, wlo + 128), R(w + "s", wlo, wlo + 128), R(x, xlo, xlo + n), R(x + "s", xlo, xlo + n)]
-        return run("te", lambda q: q.matmul_mx(ap(bank(b, 0, n)), *[ap(r) for r in ins], start, stop), [bank(b, 0, n)], ins)
+        call({"t": lambda e: e.matmul_mx(ap(bank(b, 0, n)), *[ap(r) for r in ins], start, stop)}, [bank(b, 0, n)], ins, name=w + str(wlo // 128) + x + str(xlo))
 
     def part(h, b, w, x, start, stop):
         lo, hi = PART[h]
-        return mm(RBANK[h][b], hi - lo, w, 128 * b, x, lo, start, stop)
+        mm(RBANK[h][b], hi - lo, w, 128 * b, x, lo, start, stop)
 
     def fill(r, value):
-        return run("v", lambda q: q.memset(ap(r), value), [r], [])
+        call({"v": lambda e: e.memset(ap(r), value)}, [r], [])
 
     def iota(r, pattern, base, cm=0):
-        if SCRATCH[r[0]][2] == I32:
-            return run("gc", lambda q: q.iota(ap(r), pattern, base, cm), [r], [])
-        return run("gc", lambda q: q.iota(ap(r), pattern, base, cm, allow_small_or_imprecise_dtypes=True), [r], [])
+        more = {} if SCRATCH[r[0]][2] == I32 else {"allow_small_or_imprecise_dtypes": True}
+        call({"g": lambda e: e.iota(ap(r), pattern, base, cm, **more)}, [r], [])
 
     def scan(out, scores):
         zero = R("NIL", 0, out[2] - out[1])
-        return run("v", lambda q: q.tensor_tensor_scan(ap(out), ap(zero), ap(scores), -1e29, Op.add, Op.max), [out], [zero, scores])
+        call({"v": lambda e: e.tensor_tensor_scan(ap(out), ap(zero), ap(scores), -1e29, Op.add, Op.max)}, [out], [zero, scores])
 
     X = lambda lo, hi, b=None: R("X", PAD + 4 * lo, PAD + 4 * hi) if b is None else R("X", PAD + 4 * lo + b, PAD + 4 * hi, 4)
 
-    load("sy", X(80, 208), T.x[:, 320:832])
     load("a", R("UT"), T.u[:])
-    load("sy", X(208, 320), T.x[:, 832:1280])
-    load("sy", X(0, 80), T.x[:, 0:320])
-    load("sy", R("QW"), T.wc[:], dt.uint8)
-    load("sy", R("QWs"), T.ws[:])
-    load("sy", R("VT"), T.v[:])
+    load("s", X(80, 208), T.x[:, 320:832])
+    load("s", X(208, 320), T.x[:, 832:1280])
+    load("s", X(0, 80), T.x[:, 0:320])
+    load("s", R("QW"), T.wc[:], dt.uint8)
+    load("s", R("QWs"), T.ws[:])
+    load("s", R("VT"), T.v[:])
 
     iota(col("LI", 0), [[0, 1]], 0, 1)
     iota(R("PO"), [[1, 2], [16, 8]], 0)
     fill(R("HALF"), 0.5)
     iota(R("C4"), [[4, 28]], 0)
     iota(R("C16"), [[16, 20]], 0)
-    run("gc", lambda q: q.affine_select(T.ED[:], T.HALF[:], [[-1, 516]], Op.is_equal, 0.0, 3, 4), [R("ED")], [R("HALF")])
+    call({"g": lambda e: e.affine_select(T.ED[:], T.HALF[:], [[-1, 516]], Op.is_equal, 0.0, 3, 4)}, [R("ED")], [R("HALF")])
     iota(R("JF", 0, 8), [[16, 8]], 80)
     iota(R("JF", 8, 28), [[4, 20]], 0)
     iota(R("JF", 28, 56), [[4, 28]], 208)
@@ -191,55 +229,64 @@ def rank_program(g, core, T, topo):
     ts(col("LI", 1), col("LI", 0), 15, Op.bitwise_and)
     ts(col("LI", 2), col("LI", 0), 2, Op.logical_shift_right, 3, Op.bitwise_and)
     ts(col("LI", 3), col("LI", 0), 3, Op.bitwise_and)
-    copy("v", R("PU"), R("PO"))
-    copy("v", R("LANE"), R("LI"))
+    cast(R("PU"), R("PO"))
+    cast(R("LANE"), R("LI"))
     lane, l1, lb, lq = col("LANE", 1), col("LANE", 2), col("LANE", 3), col("LANE", 0)
     fill(R("X", 0, 32), 0.0)
     fill(R("X", 160, PAD), 0.0)
     fill(R("BT", 448, 512), 0.0)
     fill(col("CT", 48), -31.875)
+    fill(col("CT", 49), -192.0)
+    fill(col("CT", 50), 127.5)
     fill(col("PM", 0), 1.0)
     fill(col("PM", 1), -1.0)
-    ts(lq, lane, 0.25, Op.mult)
-    act(R("W8", 0, 8), R("C4", 20, 28), Fn.Identity, l1)
-    act(R("W8", 8, 16), R("C4", 0, 8), Fn.Identity, l1)
+    lin("v", lq, lane, 0.0, 0.25)
+    lin("a", R("W8", 0, 8), R("C4", 20, 28), l1)
+    lin("a", R("W8", 8, 16), R("C4", 0, 8), l1)
     ts(R("CT", 28, 48), R("C16"), lane, Op.add, -127.5, Op.add)
     ts(R("CT", 0, 28), R("C4"), lq, Op.add, PAD / 4 + 128, Op.add)
-    act(R("ZQ"), R("C4", 20, 28), Fn.Identity, lq)
-    act(R("Z2"), R("W8", 0, 8), Fn.Identity, -1.0, -2.0)
-    act(R("W8", 16, 24), R("W8", 8, 16), Fn.Identity, 124.0, -4.0)
-    ts(R("CT", 28, 48), R("CT", 28, 48), -1.0, Op.mult)
+    lin("a", R("ZQ"), R("C4", 20, 28), lq)
+    lin("a", R("Z2"), R("W8", 0, 8), 63.0, -2.0)
+    lin("a", R("W8", 16, 24), R("W8", 8, 16), 124.0, -4.0)
+    lin("v", R("CT", 28, 48), R("CT", 28, 48), 0.0, -1.0)
     ts(R("LR"), R("W8", 16, 24), lb, Op.add)
     cb = col("CK", 15)
-    act(cb, lb, Fn.Identity, 127.5, 320.0)
-    copy("a", R("EDB"), R("ED"), 64.0)
+    lin("a", cb, lb, 127.5, 320.0)
     quant("QU", 0, 128, R("UT"))
+    quant("QS", 0, 128, X(80, 208))
     for h in range(2):
         pick = R("PU", 8 * h, 8 * h + 8)
-        copy("v", R("UU", 128 * h, 128 * h + 128), (R("QU"), pick), cast=dt.uint32)
+        cast(R("UU", 128 * h, 128 * h + 128), (R("QU"), pick), dt.uint32)
         copy("a", R("UUs", 128 * h, 128 * h + 128), (R("QUs"), pick))
 
+    def unit(name, b):
+        quant(name, 128 * b, 128 * b + 128, R({"EH": "ED", "EB": "EDB"}[name], 3 - b, 515 - b))
+
     def late_constants():
-        act(R("JF", 0, 8), R("JF", 0, 8), Fn.Identity, lane)
-        act(R("JF", 8, 56), R("JF", 8, 56), Fn.Identity, l1)
-        act(R("JF", 64, 84), R("C16"), Fn.Identity, lane)
-        act(R("JF", 56, 64), R("W8", 8, 16), Fn.Identity, 319.0, -1.0)
-        for b in (0, 2, 1, 3):
-            quant("EH", 128 * b, 128 * b + 128, R("ED", 3 - b, 515 - b))
-        copy("v", R("JI"), R("JF"))
-        act(R("JY"), R("JF"), Fn.Identity, -160.125)
-        act(R("JB"), R("JF"), Fn.Identity, -159.375)
-        act(R("JT"), R("JF"), Fn.Identity, -160.0, 0.5)
+        copy("a", R("EDB"), R("ED"), 64.0)
+        lin("a", R("JF", 0, 8), R("JF", 0, 8), lane)
+        lin("a", R("JF", 8, 56), R("JF", 8, 56), l1)
+        lin("a", R("JF", 64, 84), R("C16"), lane)
+        lin("a", R("JF", 56, 64), R("W8", 8, 16), 319.0, -1.0)
+        for b in (2, 1, 3):
+            unit("EH", b)
+        unit("EB", 0)
+        cast(R("JI"), R("JF"))
+        lin("a", R("JY"), R("JF"), -160.125)
+        lin("a", R("JB"), R("JF"), -159.375)
+        lin("a", R("JT"), R("JF"), -160.0, 0.5)
+        unit("EB", 1)
         ts(R("JI"), R("JI"), 1, Op.bitwise_and)
-        act(R("LN1", 3 * W1, 4 * W1), R("JF", 0, W1), Fn.Identity)
-        act(R("LN2", 3 * W2, 4 * W2), R("JF", W1, 84), Fn.Identity)
+        copy("a", R("LN1", 3 * W1, 4 * W1), R("JF", 0, W1))
+        copy("a", R("LN2", 3 * W2, 4 * W2), R("JF", W1, 84))
+        unit("EB", 2)
         ts(R("JA"), R("JI"), -0.25, Op.mult)
-        for b in (0, 2, 1, 3):
-            quant("EB", 128 * b, 128 * b + 128, R("EDB", 3 - b, 515 - b))
+        unit("EB", 3)
         tt(R("JA"), R("JA"), R("JT"), Op.add)
 
-    C, K, rr, fj, k2, thr, k41, k21, mn = (col("CK", i) for i in (0, 1, 2, 3, 4, 5, 6, 7, 8))
+    C, K, rr, fj, k2, kh, mn = (col("CK", i) for i in range(7))
     akp, akm, ak = col("CK", 10), col("CK", 11), col("QK", 20)
+    TN, cm, cp = R("TC", 28, 48), col("TC", 49), col("TC", 50)
     w8 = lambda i: R("W8", 24 + 8 * i, 32 + 8 * i)
     wa = lambda i: R("WA", 20 * i, 20 * i + 20)
     PL = lambda b, lo=0, hi=432: R("PL", 432 * b + lo, 432 * b + hi)
@@ -247,10 +294,28 @@ def rank_program(g, core, T, topo):
     AB = lambda b, lo, hi: R("AB", 320 * b + lo, 320 * b + hi)
     FP = lambda b, lo, hi: R("FP", 320 * b + lo, 320 * b + hi)
     LO = lambda lo, hi: R("LO", lo, hi)
+    engines = topo.engines(core, prev)[:8]
+    mask = sum(1 << e for e in engines)
+    rid, pid = topo.addr(prev)[:2]
+
+    def send(t):
+        def form(e):
+            for name, as_ in (("", dt.uint8), ("s", None)):
+                e.remote_dma(ap(R("G%d%s" % (t, name), 0, 112), as_), ap(R("B%d%s" % (t, name), 0, 112), as_), T.sem["arr%d" % t], T.sem.sent, pid, rid, mask)
+                total["sent"] = total.get("sent", 0) + len(engines)
+            total["arr%d" % t] = 2 * len(topo.engines(nxt, core)[:8])
+            return ("arr%d" % t, total["arr%d" % t])
+        call({"g": form}, [R("G%d" % t, 0, 112), R("G%ds" % t, 0, 112)], [R("B%d" % t), R("B%ds" % t)], "far")
+
+    def twin(b, n):
+        out, in_ = FP(b, 0, n), PL(b, 0, n)
+        copy("g", out, in_, more={"g": lambda e: e.affine_select(ap(out), ap(in_), [[0, n]], Op.is_ge, 0.0, 0, 0)})
 
     for t in range(3):
         last = t == 2
-        quant("QS", 0, 128, X(80, 208))
+        stage[0] = str(t)
+        if t:
+            quant("QS", 0, 128, X(80, 208))
         mm(6, 128, "UU", 0, "QS", 0)
         mm(7, 128, "UU", 128, "QS", 0)
         if t == 0:
@@ -263,126 +328,98 @@ def rank_program(g, core, T, topo):
         scan(R("RMK", 80, 105), bank(7, 0, 25))
         act(R("SGC"), R("RMC"), Fn.Sign, col("RMC", 64), -1.0, C)
         act(R("SGK"), R("RMK"), Fn.Sign, col("RMK", 104), -1.0, K)
-        act(rr, C, Fn.Relu, 64.0, -2.0)
-        ts(R("TC", 0, 48), R("CT", 0, 48), C, Op.add)
+        ts(rr, C, 32.0, Op.min, -2.0, Op.mult)
         ts(fj, C, 32.0, Op.is_lt, -88.0, Op.mult)
+        lin("v", R("TC"), R("CT"), C)
         act(R("QK"), R("CT", 28, 49), Fn.Abs, C)
-        ts(w8(0), R("ZQ"), K, Op.is_ge)
         ts(w8(1), R("Z2"), rr, Op.add, fj, Op.add)
+        ts(w8(0), R("ZQ"), K, Op.is_ge)
         ts(R("L1"), R("TC", 0, 20), K, Op.subtract, 4.0, Op.mult)
         tt(w8(2), w8(0), w8(1), Op.mult)
         copy("a", R("BT", 0, 320), (R("X", 0, WIN), R("L1")))
-        ts(R("CK", 10, 12), R("PM"), K, Op.mult, ak, Op.add)
+        lin("v", R("CK", 10, 12), R("PM"), ak, K)
         tt(w8(3), w8(2), R("TC", 20, 28), Op.add)
-        ts(k2, K, 2.0, Op.mult)
+        lin("v", k2, K, 0.0, 2.0)
         ts(R("L2"), w8(3), K, Op.subtract, 4.0, Op.mult)
         ts(mn, C, 128.0, Op.add, k2, Op.min)
         copy("v", R("BT", 320, 448), (R("X", 0, WIN), R("L2")))
         B, G = "B%d" % t, "G%d" % t
-        t_qb = quant(B, 0, 128, R("BT"))
-        engines = topo.engines(core, prev)[:8]
-        mask = sum(1 << e for e in engines)
-        rid, pid = topo.addr(prev)[:2]
-        wait("gc", [t_qb])
-        for name, cast in (("", dt.uint8), ("s", None)):
-            g.remote_dma(ap(R(G + name, 0, 112), cast), ap(R(B + name, 0, 112), cast), T.sem["arr%d" % t], T.sem.sent, pid, rid, mask)
-            total["sent"] = total.get("sent", 0) + len(engines)
-        total["arr%d" % t] = 2 * len(topo.engines(nxt, core)[:8])
-        note("far", [R(G, 0, 112), R(G + "s", 0, 112)], [], ("arr%d" % t, total["arr%d" % t]))
+        quant(B, 0, 128, R("BT"))
+        send(t)
         if t == 0:
             for i in range(3):
-                for name, cast in (("", dt.uint8), ("s", None)):
-                    dst, src = R("G%d%s" % (i, name), 112, 128), R("B0" + name, 112, 128)
-                    dma("sy", ap(dst, cast), ap(src, cast), [dst], [src])
+                for name, as_ in (("", dt.uint8), ("s", None)):
+                    src = R("B0" + name, 112, 128)
+                    load("s", R("G%d%s" % (i, name), 112, 128), ap(src, as_), as_, [src])
             late_constants()
         else:
-            copy("a", X(208, 320), (R("YP"), LO(28, 56)))
+            copy("a", X(208, 264), (R("YP"), LO(28, 42)))
+            copy("a", X(264, 320), (R("YP"), LO(42, 56)))
 
         j0, w, LN = (W1, W2, "LN2") if last else (0, W1, "LN1")
         J = lambda n: R(n, j0, j0 + w)
         ln = lambda i, e=None: R(LN, w * i, w * (e or i + 1))
         wo = lambda i: R("WO", 64 * i, 64 * i + w)
-        TN = R("TC", 28, 48)
         quant("QX", 0, 192, X(0, 192))
-        for b in range(2):
-            mm(HBANK[b][0], 192, "EH", 128 * b, "QX", 0)
+        mm(0, 192, "EB", 0, "QX", 0)
         act(wa(0), TN, Fn.Abs, K, -2.0)
-        act(thr, C, Fn.Identity, 192.0, -1.0)
         act(wa(1), wa(0), Fn.Abs, k2, -1.0)
         act(wa(2), R("QK", 0, 20), Fn.Abs, K, -1.0)
-        act(k41, K, Fn.Identity, -1.0, 4.0)
-        act(k21, K, Fn.Identity, 1.0, -2.0)
-        act(wa(3), wa(2), Fn.Identity, thr)
+        lin("a", kh, K, 0.5, -1.0)
+        lin("a", wa(3), wa(2), cm, -1.0)
         ts(ln(0), J("JY"), akp, Op.add, 4.0 / 3.0, Op.mult)
         ts(ln(1), J("JB"), akm, Op.add, 4.0, Op.mult)
         ts(ln(2), J("JA"), K, Op.add, 4.0, Op.mult)
         quant("QX", 192, 320, X(192, 320))
-        for b in (0, 2, 1, 3):
-            if b < 2:
-                mm(HBANK[b][1], 128, "EH", 128 * b, "QX", 192)
-            else:
-                mm(HBANK[b], 320, "EH", 128 * b, "QX", 0)
+        mm(4, 128, "EB", 0, "QX", 192)
+        for b in (2, 1, 3):
+            mm(b, 320, "EH", 128 * b, "QX", 0)
         tt(R("MX", 0, 2 * w), ln(0, 2), ln(2, 4), Op.max)
         ts(wa(4), wa(1), K, Op.is_lt, k2, Op.mult)
         tt(R("SH", 0, w), R("MX", 0, w), R("MX", w, 2 * w), Op.max)
         tt(wa(5), wa(4), TN, Op.add)
-        ts(R("SH", w, 2 * w), R("SH", 0, w), 1, Op.logical_shift_right)
-
-        def plane(b, h=None):
-            if b < 2:
-                lo, hi = PART[h]
-                copy("a", PL(b, lo, hi), bank(HBANK[b][h], 0, hi - lo))
-            else:
-                copy("a", PL(b, 0, 320), bank(HBANK[b], 0, 320))
-
-        plane(0, 0)
-        plane(0, 1)
-        act(wa(6), wa(5), Fn.Sign, thr, -1.0)
-        plane(2)
-        plane(1, 0)
-        plane(1, 1)
-        plane(3)
-        ts(R("BB", 0, 2 * w), R("SH", 0, 2 * w), 1, Op.bitwise_and)
+        ts(R("BB", w, 2 * w), R("SH", 0, w), 1, Op.logical_shift_right, 1, Op.bitwise_and)
+        copy("a", PL(0, 0, 192), bank(0, 0, 192), 1.0 / 64.0)
+        copy("a", PL(0, 192, 320), bank(4, 0, 128), 1.0 / 64.0)
+        twin(0, 320)
+        act(wa(6), wa(5), Fn.Sign, cm)
+        for b in (2, 1, 3):
+            copy("a", PL(b, 0, 320), bank(b, 0, 320))
+        twin(1, 192)
+        ts(R("BB", 0, w), R("SH", 0, w), 1, Op.bitwise_and)
+        ts(R("SH", w, 2 * w), R("SH", 0, w), 2, Op.logical_shift_right)
         tt(wa(7), wa(5), wa(6), Op.mult)
-        ts(wo(0), R("BB", w, 2 * w), k41, Op.mult, k21, Op.add)
-        ts(wa(8), wa(7), mn, Op.add, -BIG, Op.mult)
-        ts(wo(1), R("BB", 0, w), -1.0, Op.mult, 0.5, Op.add)
-        tt(wa(9), wa(8), wa(3), Op.min)
+        ts(wo(0), R("BB", w, 2 * w), k2, Op.mult, kh, Op.add)
+        ts(wa(8), wa(7), mn, Op.subtract, -BIG, Op.mult)
+        ts(wo(1), R("BB", 0, w), -2.0, Op.mult, 1.0, Op.add)
+        tt(wa(9), wa(8), wa(3), Op.max)
         tt(wo(2), wo(0), R("SH", w, 2 * w), Op.add)
-        tt(wa(10), wa(9), wa(7), Op.max)
+        tt(wa(10), wa(9), wa(7), Op.min)
         tt(wo(3), wo(2), wo(1), Op.mult)
-        ts(R("LA"), wa(10), C, Op.add, 127.5, Op.add)
-        copy("v", FP(0, 0, 320), PL(0, 0, 320))
-        if t == 0:
-            quant("QV", 0, 128, R("VT"))
+        ts(R("LA"), wa(10), -1.0, Op.mult, cp, Op.add)
         la = lambda h: R("LA", PART[h][0] // 16, PART[h][1] // 16)
         zt = lambda b, h: R("ZT", 4 * PART[h][0] + b, 4 * PART[h][1], 4)
-        unpack = lambda b: mm(GBANK[b], 128, "EH", 128 * b, G, 0)
-        late = lambda q, b: copy(q, PL(b, 320, 432), bank(GBANK[b], 0, 112))
         fused = lambda b, h: tt(zt(b, h), (PL(b), la(h)), FP(b, *PART[h]), Op.add)
         gather = lambda b, h: copy("a", AB(b, *PART[h]), (PL(b), la(h)))
-        add = lambda b, h: tt(zt(b, h), bank(HBANK[b], *PART[h]), AB(b, *PART[h]), Op.add)
+        add = lambda b, h: tt(zt(b, h), bank(b, *PART[h]), AB(b, *PART[h]), Op.add)
         part(0, 0, "EB", "QX", True, False)
         for b in (0, 2, 1, 3):
-            unpack(b)
-        part(0, 1, "EB", "QX", True, False)
-        late("v", 0)
-        late("a", 2)
-        copy("v", FP(1, 0, 320), PL(1, 0, 320))
+            mm(GBANK[b], 128, "EH" if b else "EB", 128 * b, G, 0)
+        part(1, 1, "EB", "QX", True, False)
+        for b in (0, 2, 1, 3):
+            copy("vvaa"[b], PL(b, 320, 432), bank(GBANK[b], 0, 112), None if b else 1.0 / 64.0)
         fused(0, 0)
         gather(2, 0)
-        late("v", 1)
-        late("a", 3)
         gather(3, 0)
-        for h, b in ((1, 0), (1, 1), (0, 2), (0, 3)):
+        for h, b in ((1, 0), (0, 1), (0, 2), (0, 3)):
             part(h, b, "EB", "QX", True, False)
         add(2, 0)
         part(1, 2, "EB", "QX", True, False)
         fused(1, 0)
         add(3, 0)
         part(1, 3, "EB", "QX", True, False)
-        gather(2, 1)
-        gather(3, 1)
+        for b in (1, 2, 3):
+            gather(b, 1)
         if last:
             ts(LO(0, 20), wo(3), C, Op.add, 127.5, Op.add)
         else:
@@ -391,39 +428,40 @@ def rank_program(g, core, T, topo):
         for b in range(4):
             part(0, b, "QW", "QZ", False, True)
         fused(0, 1)
-        fused(1, 1)
-        add(2, 1)
-        add(3, 1)
+        for b in (1, 2, 3):
+            add(b, 1)
         if not last:
             ts(LO(8, 64), R("WO", 200, 256), C, Op.add, cb, Op.add)
         quant("QZ", 192, 320, R("ZT", 768, 1280))
         for b in range(4):
             part(1, b, "QW", "QZ", False, True)
+        if t == 0:
+            quant("QV", 0, 128, R("VT"))
         if last:
             copy("a", R("LOR"), (R("IOT"), LO(0, 20)))
-            dma("sy", T.lo[:], T.LOR[0:128:16, :], [], [R("LOR")], "out")
+            store("s", T.lo[:], T.LOR[0:128:16, :], R("LOR"), "lo")
         for b in range(4):
             copy("a", YP(b, 0, 192), bank(RBANK[0][b], 0, 192), 0.03125)
         for b in range(4):
-            q = "va"[b % 2]
-            copy(q, YP(b, 192, 320), bank(RBANK[1][b], 0, 128), 0.03125)
+            copy("vaav"[b], YP(b, 192, 320), bank(RBANK[1][b], 0, 128), 0.03125)
+        for b in range(4):
             if last:
-                copy(q, X(0, 192, b), (YP(b), LO(0, 12)))
+                copy("vaav"[b], X(0, 192, b), (YP(b), LO(0, 12)))
             else:
-                copy(q, X(80, 208, b), (YP(b), LO(0, 8)))
+                copy("vaav"[b], X(80, 208, b), (YP(b), LO(0, 8)))
 
+    stage[0] = "e"
     for b in range(4):
-        copy("va"[b % 2], X(192, 320, b), (YP(b), LO(12, 20)))
-        if b == 0:
-            quant("QF", 0, 192, X(0, 192))
-    quant("QF", 192, 320, X(192, 320))
-    mm(2, 192, "QV", 0, "QF", 0)
-    mm(3, 128, "QV", 0, "QF", 192)
-    copy("a", R("YO", 0, 192), bank(2, 0, 192))
-    dma("a", T.y[:, 0:192], T.YO[:, 0:192], [], [R("YO", 0, 192)], "out")
-    dma("sy", T.oc[:], T.QF[:].bitcast(dt.uint8), [], [R("QF")], "out")
-    copy("v", R("YO", 192, 320), bank(3, 0, 128))
+        copy("vaav"[b], X(192, 320, b), (YP(b), LO(12, 20)))
+    for h, (lo, hi) in enumerate(PART):
+        quant("QF", lo, hi, X(lo, hi))
+        store("sa", T.oc[:, 4 * lo:4 * hi], T.QF[:, lo:hi].bitcast(dt.uint8), R("QF", lo, hi), "oc%d" % h)
+        mm(2 + h, hi - lo, "QV", 0, "QF", lo)
+        copy("av"[h], R("YO", lo, hi), bank(2 + h, 0, hi - lo))
+        store("as", T.y[:, lo:hi], T.YO[:, lo:hi], R("YO", lo, hi), "y%d" % h)
     for i in range(4):
-        dma("a" if i < 2 else "sy", T.osc[4 * i:4 * i + 4, :], T.QFs[32 * i:32 * i + 4, :], [], [R("QFs")], "out")
-    dma("sy", T.y[:, 192:320], T.YO[:, 192:320], [], [R("YO", 192, 320)], "out")
-    wait("gc", list(total.items()))
+        store("sa", T.osc[4 * i:4 * i + 4, :], T.QFs[32 * i:32 * i + 4, :], R("QFs"), "osc%d" % i)
+
+    for name, q in [e.split(":") for e in ORDER.split()] or [(name, list(c[0])[0]) for name, c in calls.items()]:
+        issue(name, q)
+    wait("g", list(total.items()))

@@ -10,14 +10,14 @@ BIG = 4096.0
 F8, U8, BF, F32, I32, U16 = "float8_e4m3fn_x4", "uint8", "bfloat16", "float32", "int32", "uint16"
 SCRATCH = {"PS": ("psum", [128, 4096], F32)}
 for _n, _w in (("X", XW), ("UT", 512), ("VT", 512), ("BT", 512), ("ZT", 1280), ("PL", 1728), ("AB", 1280), ("FP", 640), ("YP", 1280),
-               ("ED", 516), ("EDB", 516), ("HALF", 516)):
+               ("ED", 516), ("EDB", 516), ("NUL", 516)):
     SCRATCH[_n] = ("sbuf", [128, _w], BF)
 for _n, _w in (("QU", 128), ("UU", 256), ("QV", 128), ("QW", 512), ("EH", 512), ("EB", 512), ("QS", 128), ("QX", 320), ("QZ", 320),
                ("QF", 320), ("B0", 128), ("B1", 128), ("B2", 128), ("G0", 128), ("G1", 128), ("G2", 128)):
     SCRATCH[_n] = ("sbuf", [128, _w], F8)
     SCRATCH[_n + "s"] = ("sbuf", [128, _w], U8)
-for _n, _w in (("C4", 28), ("C16", 20), ("CT", 51), ("TC", 51), ("ZQ", 8), ("Z2", 8), ("LANE", 4), ("PM", 2), ("NIL", 65), ("JF", 84), ("JY", 84),
-               ("JB", 84), ("JA", 84), ("JT", 84), ("LN1", 4 * W1), ("LN2", 4 * W2), ("MX", 2 * W1), ("IOT", 320), ("LOR", 320), ("YO", 320),
+for _n, _w in (("C4", 28), ("C16", 20), ("CT", 51), ("TC", 51), ("ZQ", 8), ("Z2", 8), ("LANE", 4), ("PM", 2), ("NIL", 65), ("JY", 84),
+               ("JB", 84), ("JA", 84), ("JT", 84), ("LN", 4 * W1 + 4 * W2), ("MX", 2 * W1), ("LF", 32), ("LT", 32), ("YO", 320),
                ("RMC", 65), ("RMK", 105), ("SGC", 65), ("SGK", 105), ("CK", 16), ("QK", 21), ("W8", 64), ("WA", 320), ("WO", 256)):
     SCRATCH[_n] = ("sbuf", [128, _w], F32)
 for _n, _w in (("LI", 4), ("JI", 84), ("PO", 16), ("SH", 2 * W1), ("BB", 2 * W1)):
@@ -56,6 +56,93 @@ cUUs128:a cCT28':a 0JF0:a 0UU0QS0:t 0RMC0:v 0JF56:a cJF8:g 0JF8:a 0SGC0:a cRMK0:
 2AB832:a 2ZT770:v 2AB1152:a 2ZT771:v 2LOR0:a 2lo:s 2QZ192:v 2QW0QZ192:t 2YP0:v 2YP640:v 2YP320:v 2YP960:a 2YP192:a 2X384':v 2QW1QZ192:t 2YP512:a
 2QW3QZ192:t 2QW2QZ192:t 2YP832:v 2YP1152:a 2X387:v eX1152:v 2X385:a 2X386:a eQF0:v eQV0QF0:t eoc0:s eX1155:v eX1153:a eX1154:a eQF192:v eoc1:a
 eQV0QF192:t eYO0:v ey0:s eosc3:s eosc2:s eYO192:a eosc1:a eosc0:s ey1:s
+"""
+ORDER = """
+cUT0:a cNUL0:v cLI0:g cLI3:v cLI2:v cLI1:v cCT48:v cLANE0:v cCK15:a cPO0:g cC40:g cCT49:g cLN192:g cLN220:g 0LN192:a cW88:a cRMK0:v cX160:v cLANE0':v
+cX704:s cX1216:s cX384:s cPU0:v cC160:g cCT0:v cCT28:v cCT50:v cLN200:g cNIL0:g cW80:a cW816:a cZ20:a cZQ0:a cQW0:s cQWs0:s cVT0:s cED0:g cBT448:g
+cX0:g cPM0:g cQU0:v cUUs0:a cLR0:v cUU0:v cQS0:v cUU128:v 0LN256:v 0UU0QS0:t 0RMC0:v 0QX192:v cUUs128:a 0UU1QS0:t 0RMK80:v 0LN200:a 0LN248:a 0JI0:v
+0SGC0:a 0CK2:v 0CK3:v cCT28':a 0SGK0:a 0W824:v 0W832:v 0TC0:a 0L10:v 0W840:v 0CK4:v 0W848:v 0CK6:v 0L20:v 0JI0':v 0X32:a 0BT320:v 0QK0:a 0JA0:v 0BT0:a
+0B00:v 0G0112:s cEDB0:g 0G00:g 0EB0:v 0EB0QX192:t 0QX0:v 0EB0QX0:t 0EH128:v 0WA0:a 0WA40:a 0WA20:a 0WA80:v 0CK10:a 0JB0:a 0JT0:a 0JY0:a 0WA60:a
+0PL192:a 0LN64:v 0WA100:v 0WA120:a 0EH1QX0:t 0PL432:a 0CK5:a 0EH256:v 0JA0':v 0EH384:v 0LN0:v 0WA140:v 0EB256:v 0EB384:v 0LN128:v 0WA160:v 0EB128:v
+0MX0:v 0WA180:v 0EH2QX0:t 0EH3QX0:t 0PL0:a 0EB0QX0':t 0PL1296:a 0PL864:a 0G0s112:s 0EH1G00:t 0PL752:a 0G1112:s 0G2112:s 0G1s112:s 0G2s112:s 0EH2G00:t
+0PL1184:a 0SH0:v 0WA200:v 0BB0:v 0LA0:v 0BB64:v 0FP320:g 0ZT1:v 0EB0G00:t 0PL320:a 0EH3G00:t 0PL1616:a 0EB1QX192:t 0EB3QX0:t 0FP0:g 0ZT0:v 0WO64:v
+0AB640:a 0ZT2:v 0AB960:a 0ZT3:v 0SH64:v 0QZ0:v 0EB1QX0:t 0EB0QX192':t 0EB2QX192:t 0EB2QX0:t 0AB1152:a 0AB832:a 0ZT768:v 0ZT770:v 0EB3QX192:t 0AB512:a
+0ZT771:v 0ZT769:v 0QW2QZ0:t 0YP640:a 0QW0QZ0:t 0YP0:a 0QW3QZ0:t 0YP960:a 0QW1QZ0:t 0YP320:a 0WO0:v 0QZ192:v 0QW1QZ192:t 0QW0QZ192:t 0YP192:a
+0QW2QZ192:t 0YP832:a 0WO128:v 0WO192:v 0YP512:v 0LO0:v 0X705:a 0LO8:v 0QW3QZ192:t 0YP1152:v 0X704:v 0X706:a 0X707:v 1QS0:v 1UU0QS0:t 1X1216:v 1RMC0:v
+1UU1QS0:t 1RMK80:v 1X384:a 1X512:a 1QX0:v 1EB0QX0:t 1X32:a 1SGC0:a 1CK2:v 1CK3:v 1SGK0:a 1W824:v 1W832:v 1TC0:v 1W840:v 1L10:v 1W848:v 1CK4:v 1L20:v
+1QK0:a 1X1440:a 1QX192:v 1EB0QX192:t 1WA0:a 1BT320:v 1LN128:v 1BT0:a 1B10:v 1G10:g cLF20:g 1WA20:a 1WA80:v 1CK10:a 1LN0:v 1LN64:v 1WA100:v 1CK6:v
+1MX0:v 1PL192:a 1PL0:a 1FP0:g 1WA40:a 1WA120:a 1WA140:v 1WA60:v 1SH0:v 1WA160:v 1CK5:a 1EH1QX0:t 1EH3QX0:t 1PL1296:a 1PL432:a 1EH2QX0:t 1PL864:a
+1BB64:v 1WA180:v 1SH64:v 0QV0:v 1WA200:v 1WO0:v 1EH2G10:t 1PL1184:a 1LA0:v 1AB640:a 1EB0G10:t 1EH1G10:t 1EH3G10:t 1PL1616:a 1EB1QX192:t 1EB1QX0:t
+1WO128:v 1PL320:v 1BB0:v 1ZT0:v 1EB0QX192':t 1ZT2:v 1PL752:a 1FP320:g 1ZT1:v 1EB3QX0:t 1EB0QX0':t 1EB2QX192:t 1EB2QX0:t 1AB960:a 1ZT3:v 1EB3QX192:t
+1QZ0:v 1AB512:a 1ZT769:v 1AB1152:a 1ZT768:v 1ZT771:v 1AB832:a 1ZT770:v 1QW1QZ0:t 1QW3QZ0:t 1YP320:a 1QW0QZ0:t 1YP960:a 1YP0:a 1WO64:v 1QW2QZ0:t
+1QZ192:v 1WO192:v 1YP640:v 1QW0QZ192:t 1YP192:a 1LO0:v 1LO8:v 1X704:v 1QW1QZ192:t 1YP512:a 1QW2QZ192:t 1YP832:a 1X705:a 1QW3QZ192:t 1YP1152:v 1X707:v
+1X706:a 2QS0:v 2X32:a 2X384:v 2UU0QS0:t 2RMC0:v 2UU1QS0:t 2RMK80:v 2X512:a 2QX0:v 2SGC0:a 2CK2:v 2CK3:v 2SGK0:a 2W824:v 2W832:v 2TC0:a 2L10:v 2QK0:a
+2X1440:a 2W840:v 2LN296:v 2W848:v 2CK4:v 2L20:v 2CK10:v 2BT320:v 2LN276:v 2BT0:a 2B20:v 2G20:g 2LN316:v 2X1216:a 2QX192:v 2WA0:a 2WA20:a 2WA80:v
+2MX0:v 2WA100:v 2SH0:v 2CK6:v 2CK5:a 2WA40:a 2EB0QX0:t 2PL0:a 2BB0:v 2WA120:a 2WA140:v 2WO64:v 2WA60:v 2WA160:v 2SH20:v 2WA180:v 2BB20:v 2WA200:v
+2WO0:v 2EB0QX192:t 2PL192:a 2FP0:g 2EH1QX0:t 2PL432:a 2FP320:g 2EH3QX0:t 2PL1296:a 2EH2QX0:t 2PL864:a 2LA0:v 2EB0G20:t 2PL320:v 2WO128:v 2ZT0:v
+2ZT768:v 2EH2G20:t 2PL1184:a 2AB640:a 2ZT2:v 2EH1G20:t 2EH3G20:t 2EB1QX192:t 2EB0QX192':t 2EB0QX0':t 2PL1616:a 2PL752:a 2ZT1:v 2EB1QX0:t 2EB3QX0:t
+2AB960:a 2ZT3:v 2WO192:v 2QZ0:v 2EB2QX192:t 2EB2QX0:t 2AB832:a 2ZT770:v 2AB512:a 2ZT769:v 2EB3QX192:t 2AB1152:a 2ZT771:v 2LF0:a 2LT0:v 2lo0:s 2lo4:s
+2lo2:s 2lo5:s 2lo1:s 2lo7:s 2lo3:s 2lo6:s 2QZ192:v 2QW1QZ0:t 2YP320:a 2QW0QZ0:t 2YP0:a 2QW3QZ0:t 2YP960:v 2LO0:v 2QW2QZ0:t 2YP640:a 2QW0QZ192:t
+2YP192:v 2X384':v 2QW1QZ192:t 2YP512:a 2QW3QZ192:t 2QW2QZ192:t 2YP832:v 2YP1152:a 2X387:v eX1152:v 2X385:a 2X386:a eQF0:v eQV0QF0:t eoc0:s eX1154:a
+eX1155:v eX1153:a eQF192:v eosc2:a eQV0QF192:t eoc1:s eYO0:v ey0:a eYO192:a eosc3:a eosc0:s eosc1:s ey1:s
+"""
+ORDER = """
+cUT0:a cNUL0:v cLI0:g cCT49:g cLI3:v cLI1:v cLI2:v cCT50:v cLANE0:v cRMK0:v cC40:g cPO0:g cPM0:g cLN200:g cLN220:g cC160:g cNIL0:g cLANE0':a cW88:a
+0LN256:a cCT48:v cW80:v cCT0:v cPU0:v cX704:s cX1216:s cX384:s cBT448:g cQW0:s cQWs0:s cVT0:s 0LN200:a cW816:a cCT28:v cCT28':a cQU0:v 0LN248:v cUU0:v
+cQS0:v cUUs0:a 0UU0QS0:t cUU128:v cLR0:v 0RMC0:v cZQ0:a cUUs128:a 0UU1QS0:t cLN192:g 0LN192:a cX0:g 0JI0:v cW80':a cZ20:v 0RMK80:v 0SGC0:a 0QK0:a
+cX160:g cED0:g 0CK3:v 0JI0':v 0W832:v 0SGK0:a 0W824:v 0W840:v 0TC0:a 0L10:v 0W848:v 0QX192:v 0L20:v 0X32:a 0JA0:v 0BT320:v 0BT0:a 0B00:v 0G0112:s
+0EH128:v 0QX0:v 0EH256:v 0G00:g cEDB0:g 0WA0:a 0CK4:a 0EB0:v 0JT0:a 0WA20:a 0WA80:v 0JY0:a 0CK10:a 0JA0':v 0EH384:v 0WA100:v 0LN128:v 0LN0:v 0JB0:a 0LN64:v
+0CK6:v 0WA40:a 0EH1QX0:t 0PL432:a 0WA120:a 0WA140:v 0CK5:a 0WA60:a 0MX0:v 0WA160:v 0EB256:v 0EB0QX192:t 0EH2QX0:t 0EB0QX0:t 0PL0:a 0PL192:a 0WA180:v
+0EB384:v 0EB128:v 0WA200:v 0G0s112:s 0EH3QX0:t 0PL1296:a 0PL864:a 0EB0G00:t 0PL320:a 0EH2G00:t 0EH1G00:t 0PL752:a 0G1112:s 0G2112:s 0G1s112:s
+0G2s112:s 0EH3G00:t 0PL1616:a 0SH0:v 0LA0:v 0QV0:v 0BB64:v 0SH64:v 0BB0:v 0PL1184:v 0AB640:a 0EB1QX0:t 0FP320:g 0FP0:g 0ZT0:v 0WO0:v 0ZT1:v 0ZT2:v
+0EB3QX0:t 0EB0QX192':t 0EB2QX0:t 0EB1QX192:t 0EB0QX0':t 0AB960:a 0ZT3:v 0ZT768:v 0QZ0:v 0AB832:a cCK15:a 0EB3QX192:t 0AB512:a 0ZT769:v 0EB2QX192:t
+0ZT770:v 0AB1152:a 0ZT771:v 0QW2QZ0:t 0YP640:a 0WO64:v 0QW0QZ0:t 0YP0:a 0QW1QZ0:t 0YP320:a 0QZ192:v 0QW2QZ192:t 0YP832:a 0QW0QZ192:t 0QW3QZ0:t
+0YP960:a 0WO128:v 0WO192:v 0YP192:v 0LO8:v 0LO0:v 0X706:a 0QW1QZ192:t 0YP512:v 0X705:a 0QW3QZ192:t 0YP1152:v 1X384:a 1X32:a 0X704:v 0X707:v 1QS0:v
+1UU0QS0:t 1X1216:v 1RMC0:v 1SGC0:a 1UU1QS0:t 1RMK80:v 1SGK0:a 1QX0:v 1EB0QX0:t 1CK3:v 1TC0:v 1W824:v 1QK0:a 1W832:v 1CK10:v 1W840:v 1L10:v 1W848:v
+1X1440:a 1QX192:v 1EB0QX192:t 1EH1QX0:t 1EH2QX0:t 1EH3QX0:t 1L20:v 1LN0:v 1BT320:v 1LN64:v 1BT0:a 1B10:v 1WA0:a 1CK4:a 1WA40:a 1WA20:a 1PL432:a
+1EB1QX192:t 1PL0:a 1LN128:v 1CK5:v 1WA80:v 1MX0:v 1WA100:v 1WA120:a 1CK6:v 1WA60:v 1SH0:v 1WA140:v 1PL192:a 1PL1296:a 1PL864:a 1BB0:v 1WA160:v 1BB64:v
+1WA180:v 1WO64:v 1WO0:v 1WA200:v 1SH64:v 1LA0:v 1WO128:v 1G10:g 1EB0G10:t cLF20:g 1FP0:g 1PL320:a 1ZT0:v 1ZT768:v 1EH2G10:t 1PL1184:a 1EH3G10:t
+1EB0QX0':t 1PL1616:a 1AB640:a 1ZT2:v 1EH1G10:t 1PL752:a 1FP320:g 1ZT1:v 1EB1QX0:t 1EB0QX192':t 1EB2QX0:t 1AB960:a 1ZT3:v 1QZ0:v 1EB2QX192:t 1EB3QX0:t
+1AB512:a 1AB832:a 1AB1152:a 1EB3QX192:t 1ZT770:v 1ZT771:v 1ZT769:v 1QW3QZ0:t 1YP960:a 1QW0QZ0:t 1QW1QZ0:t 1YP320:a 1QW2QZ0:t 1YP640:a 1WO192:v
+1QZ192:v 1QW3QZ192:t 1YP0:v 1LO8:v 1LO0:v 1QW0QZ192:t 1YP192:v 1YP1152:a 1X707:v 1QW1QZ192:t 1YP512:a 1QW2QZ192:t 1YP832:a 1X705:a 1X704:v 2X1440:v
+1X706:a 2QS0:v 2UU0QS0:t 2X32:v 2RMC0:v 2UU1QS0:t 2RMK80:v 2X384:a 2QX0:v 2EB0QX0:t 2SGC0:a 2CK3:v 2TC0:v 2SGK0:a 2W824:v 2QK0:a 2W832:v 2CK10:v
+2W840:v 2L10:v 2W848:v 2LN316:v 2L20:v 2X1216:a 2QX192:v 2CK4:a 2EH3QX0:t 2EB0QX192:t 2EH1QX0:t 2BT320:v 2LN296:v 2BT0:a 2B20:v 2LN276:v 2G20:g 2CK6:v
+2MX0:v 2WA0:a 2WA40:a 2WA20:a 2WA80:v 2PL0:a 2PL192:a 2EB0QX0':t 2EH2QX0:t 2FP0:g 2SH0:v 2WA100:v 2WA120:a 2CK5:v 2BB0:v 2BB20:v 2WA140:v 2WA60:a
+2PL432:a 2SH20:v 2WA160:v 2WO64:v 2WA180:v 2WO0:v 2WA200:v 2WO128:v 2LA0:v 2PL1296:a 2PL864:a 2EB0G20:t 2PL320:v 2WO192:v 2ZT768:v 2ZT0:v 2EH2G20:t
+2EB1QX192:t 2PL1184:a 2AB640:a 2ZT2:v 2EH3G20:t 2PL1616:a 2EB1QX0:t 2EH1G20:t 2PL752:a 2FP320:g 2ZT1:v 2AB960:a 2ZT3:v 2LF0:a 2LT0:v 2QZ0:v
+2EB0QX192':t 2EB2QX192:t 2EB2QX0:t 2EB3QX0:t 2AB832:a 2ZT770:v 2AB512:a 2ZT769:v 2AB1152:a 2EB3QX192:t 2ZT771:v 2QZ192:v 2QW1QZ0:t 2YP320:a 2QW0QZ0:t
+2YP0:a 2QW3QZ0:t 2YP960:v 2LO0:v 2QW2QZ0:t 2YP640:v 2QW0QZ192:t 2YP192:a 2X384':v 2QW1QZ192:t 2YP512:a 2QW3QZ192:t 2YP1152:a 2QW2QZ192:t 2YP832:v
+2X387:v eX1152:v 2X385:a 2lo3:s 2lo0:s 2lo6:s 2lo1:s 2lo2:s 2lo4:s 2lo7:s 2lo5:s 2X386:a eQF0:v eQV0QF0:t eoc0:s eX1154:a eX1153:a eX1155:v eQF192:v
+eosc0:s eQV0QF192:t eoc1:a eYO0:v ey0:a eosc3:s eosc2:a eosc1:a eYO192:v ey1:s
+"""
+ORDER = """
+cUT0:a cNUL0:v cLI0:g cLI3:v cLI2:v cLI1:v cCT48:v cPO0:g cC40:g cC160:g cCT49:g cNIL0:g cLN192:g cEDB0:g cLN200:g cLANE0:v cLANE0':a cPM0:g cLN220:g
+cW80:a cW88:a cZQ0:a cCT50:v cX160:v cPU0:v cCT28:v cRMK0:v cZ20:a 0LN256:a cX704:s cX1216:s cX384:s cQW0:s cQWs0:s cVT0:s cQU0:v cCT0:v cUU0:v cQS0:v
+cUU128:v cUUs0:a 0UU0QS0:t 0RMC0:v cUUs128:a cW816:a cLR0:v 0LN248:a 0EB0:v 0UU1QS0:t 0RMK80:v 0SGC0:a 0CK2:v 0CK3:v cCT28':a 0TC0:v 0W832:v cBT448:g
+0SGK0:a 0W824:v 0L10:v 0W840:v 0LN192:v 0X32:a 0LN200:a 0W848:v 0JI0:v 0L20:v cX0:g 0BT320:v 0BT0:a 0JI0':v 0CK5:a 0QK0:a cCK15:a 0WA0:a 0B00:v
+0G0112:s 0QX0:v 0QX192:v 0EB0QX192:t 0EB0QX0:t cED0:g 0EH128:v 0EH1QX0:t 0EH384:v 0EH3QX0:t 0CK4:a 0WA40:a 0WA20:a 0JY0:a 0CK10:a 0WA80:v 0G00:g
+0JT0:a 0JB0:a 0WA60:a 0PL192:a 0PL0:a 0EH256:v 0EB0QX0':t 0JA0:v 0WA100:v 0PL432:a 0WA120:a 0EB128:v 0LN0:v 0JA0':v 0LN64:v 0CK6:v 0LN128:v 0EB384:v
+0MX0:v 0EB1QX192:t 0FP320:a 0PL1296:a 0EH2QX0:t 0PL864:a 0WA140:v 0SH0:v 0WA160:v 0EB256:v 0WA180:v 0G0s112:s 0BB64:v 0WA200:v 0BB0:v 0LA0:v 0EH1G00:t
+0PL752:v 0EH2G00:t 0PL1184:a 0G1112:s 0G2112:s 0G1s112:s 0G2s112:s 0WO0:v cLF20:g 0FP0:g 0ZT1:v 0EB0G00:t 0PL320:a 0ZT0:v 0EH3G00:t 0PL1616:a 0AB640:a
+0ZT2:v 0AB960:a 0ZT3:v 0WO64:v 0QZ0:v 0EB0QX192':t 0EB1QX0:t 0EB2QX192:t 0EB3QX0:t 0AB1152:a 0AB832:a 0ZT768:v 0ZT770:v 0AB512:a 0EB2QX0:t 0EB3QX192:t
+0ZT771:v 0ZT769:v 0SH64:v 0QW0QZ0:t 0YP0:a 0QW1QZ0:t 0YP320:a 0QW2QZ0:t 0YP640:a 0QW3QZ0:t 0YP960:a 0QZ192:v 0QW1QZ192:t 0QW0QZ192:t 0YP192:a
+0QW2QZ192:t 0YP832:a 0WO128:v 0QV0:v 0WO192:v 0YP512:v 0LO0:v 0X705:a 0LO8:v 0QW3QZ192:t 0YP1152:v 0X704:v 0X706:a 0X707:v 1QS0:v 1X1216:v 1UU0QS0:t
+1RMC0:v 1UU1QS0:t 1RMK80:v 1X512:a 1X384:a 1QX0:v 1EB0QX0:t 1X32:a 1SGC0:a 1CK2:v 1CK3:v 1SGK0:a 1W824:v 1W832:v 1TC0:a 1L10:v 1W840:v 1QK0:a 1CK10:v
+1W848:v 1LN128:v 1L20:v 1X1440:a 1QX192:v 1EB0QX192:t 1EH1QX0:t 1EH3QX0:t 1EH2QX0:t 1BT320:v 1LN64:v 1BT0:a 1B10:v 1G10:g 1EH2G10:t 1WA0:a 1CK4:a
+1CK5:a 1WA20:a 1WA80:v 1LN0:v 1WA100:v 1MX0:v 1CK6:v 1PL192:a 1PL0:a 1WA40:a 1SH0:v 1WA120:a 1WA140:v 1PL1296:a 1WA60:a 1PL864:a 1PL432:a 1SH64:v
+1WA160:v 1BB0:v 1WA180:v 1WO64:v 1WA200:v 1BB64:v 1LA0:v 1EB0G10:t 1PL320:v 1WO0:v 1FP0:g 1ZT0:v 1PL1184:a 1AB640:a 1ZT2:v 1EH1G10:t 1EH3G10:t
+1EB1QX192:t 1EB0QX0':t 1EB1QX0:t 1EB0QX192':t 1PL1616:a 1PL752:a 1EB3QX0:t 1FP320:g 1ZT1:v 1EB2QX192:t 1EB2QX0:t 1AB960:a 1ZT3:v 1EB3QX192:t 1AB512:a
+1ZT769:v 1AB832:a 1AB1152:a 1QZ0:v 1QW3QZ0:t 1YP960:a 1QW1QZ0:t 1YP320:a 1QW2QZ0:t 1YP640:a 1QW0QZ0:t 1ZT770:v 1ZT768:v 1ZT771:v 1WO128:v 1QZ192:v
+1QW1QZ192:t 1YP512:a 1WO192:v 1YP0:v 1LO0:v 1LO8:v 1QW0QZ192:t 1YP192:v 1QW2QZ192:t 1YP832:a 1QW3QZ192:t 1YP1152:v 1X704:v 1X705:a 1X707:v 1X706:a
+2QS0:v 2UU0QS0:t 2X32:v 2RMC0:v 2UU1QS0:t 2RMK80:v 2X512:a 2X384:a 2QX0:v 2SGC0:a 2CK2:v 2CK3:v 2SGK0:a 2W824:v 2W832:v 2TC0:a 2L10:v 2W840:v 2QK0:a
+2CK10:v 2W848:v 2X1440:a 2LN276:v 2L20:v 2LN316:v 2BT320:v 2LN296:v 2BT0:a 2B20:v 2G20:g 2X1216:a 2QX192:v 2MX0:v 2CK4:a 2WA0:a 2WA40:a 2WA20:a
+2WA80:v 2SH0:v 2WA100:v 2EB0QX0:t 2WA60:v 2PL0:a 2CK5:a 2BB0:v 2CK6:v 2EB0QX192:t 2PL192:a 2FP0:g 2WA120:a 2WA140:v 2SH20:v 2WA160:v 2BB20:v 2WA180:v
+2WO64:v 2EH1QX0:t 2PL432:a 2FP320:g 2EH3QX0:t 2PL1296:a 2EH2QX0:t 2PL864:a 2WA200:v 2WO0:v 2LA0:v 2EB0G20:t 2PL320:v 2WO128:v 2ZT0:v 2ZT768:v
+2EH2G20:t 2PL1184:a 2EH3G20:t 2PL1616:a 2AB640:a 2ZT2:v 2EH1G20:t 2PL752:a 2EB0QX0':t 2ZT1:v 2EB1QX0:t 2EB3QX0:t 2EB1QX192:t 2EB0QX192':t 2AB960:a
+2ZT3:v 2WO192:v 2QZ0:v 2AB512:a 2ZT769:v 2AB832:a 2EB2QX0:t 2EB2QX192:t 2ZT770:v 2AB1152:a 2EB3QX192:t 2ZT771:v 2LO0:v 2QZ192:v 2LF0:a 2LT0:v 2lo1:s
+2lo2:s 2lo6:s 2lo7:s 2lo0:s 2lo4:s 2lo5:s 2lo3:s 2QW1QZ0:t 2YP320:a 2QW2QZ0:t 2YP640:a 2QW3QZ0:t 2YP960:v 2QW0QZ0:t 2YP0:a 2QW1QZ192:t 2QW0QZ192:t
+2YP192:v 2YP512:a 2QW2QZ192:t 2YP832:v 2QW3QZ192:t 2YP1152:a 2X385:a 2X384':v 2X387:v eX1152:v 2X386:a eQF0:v eQV0QF0:t eoc0:s eX1155:v eX1153:a
+eX1154:a eQF192:v eoc1:s eosc2:a eosc3:a eosc0:s eosc1:s eYO0:v ey0:a eQV0QF192:t eYO192:v ey1:s
 """
 
 
@@ -194,7 +281,10 @@ def rank_program(g, core, T, topo):
         mm(RBANK[h][b], hi - lo, w, 128 * b, x, lo, start, stop)
 
     def fill(r, value):
-        call({"v": lambda e: e.memset(ap(r), value)}, [r], [])
+        forms = {"v": lambda e: e.memset(ap(r), value)}
+        if value == int(value) and abs(value) < 256:
+            forms["g"] = lambda e: e.iota(ap(r), [[0, r[2] - r[1]]], int(value), 0, allow_small_or_imprecise_dtypes=True)
+        call(forms, [r], [])
 
     def iota(r, pattern, base, cm=0):
         more = {} if SCRATCH[r[0]][2] == I32 else {"allow_small_or_imprecise_dtypes": True}
@@ -216,14 +306,17 @@ def rank_program(g, core, T, topo):
 
     iota(col("LI", 0), [[0, 1]], 0, 1)
     iota(R("PO"), [[1, 2], [16, 8]], 0)
-    fill(R("HALF"), 0.5)
+    fill(R("NUL"), 0.0)
     iota(R("C4"), [[4, 28]], 0)
     iota(R("C16"), [[16, 20]], 0)
-    call({"g": lambda e: e.affine_select(T.ED[:], T.HALF[:], [[-1, 516]], Op.is_equal, 0.0, 3, 4)}, [R("ED")], [R("HALF")])
-    iota(R("JF", 0, 8), [[16, 8]], 80)
-    iota(R("JF", 8, 28), [[4, 20]], 0)
-    iota(R("JF", 28, 56), [[4, 28]], 208)
-    iota(R("IOT"), [[1, 320]], 0)
+    for name, value in (("ED", 0.5), ("EDB", 32.0)):
+        call({"g": lambda e, name=name, value=value: e.affine_select(T[name][:], T.NUL[:], [[-1, 516]], Op.not_equal, value, 3, 4)}, [R(name)], [R("NUL")])
+    JF = lambda lo=0, hi=W1 + W2: R("LN", 3 * W1 + lo, 3 * W1 + hi)
+    iota(JF(0, 8), [[16, 8]], 80)
+    iota(JF(8, 28), [[4, 20]], 0)
+    iota(JF(28, 56), [[4, 28]], 208)
+    iota(R("PM"), [[-2, 2]], 1)
+    fill(R("LF", 20, 32), 0.0)
     fill(R("NIL"), 0.0)
     fill(R("RMK", 0, 80), -1e29)
     ts(col("LI", 1), col("LI", 0), 15, Op.bitwise_and)
@@ -238,8 +331,6 @@ def rank_program(g, core, T, topo):
     fill(col("CT", 48), -31.875)
     fill(col("CT", 49), -192.0)
     fill(col("CT", 50), 127.5)
-    fill(col("PM", 0), 1.0)
-    fill(col("PM", 1), -1.0)
     lin("v", lq, lane, 0.0, 0.25)
     lin("a", R("W8", 0, 8), R("C4", 20, 28), l1)
     lin("a", R("W8", 8, 16), R("C4", 0, 8), l1)
@@ -263,22 +354,19 @@ def rank_program(g, core, T, topo):
         quant(name, 128 * b, 128 * b + 128, R({"EH": "ED", "EB": "EDB"}[name], 3 - b, 515 - b))
 
     def late_constants():
-        copy("a", R("EDB"), R("ED"), 64.0)
-        lin("a", R("JF", 0, 8), R("JF", 0, 8), lane)
-        lin("a", R("JF", 8, 56), R("JF", 8, 56), l1)
-        lin("a", R("JF", 64, 84), R("C16"), lane)
-        lin("a", R("JF", 56, 64), R("W8", 8, 16), 319.0, -1.0)
+        lin("a", JF(0, 8), JF(0, 8), lane)
+        lin("a", JF(8, 56), JF(8, 56), l1)
+        lin("a", JF(64, 84), R("C16"), lane)
+        lin("a", JF(56, 64), R("W8", 8, 16), 319.0, -1.0)
         for b in (2, 1, 3):
             unit("EH", b)
         unit("EB", 0)
-        cast(R("JI"), R("JF"))
-        lin("a", R("JY"), R("JF"), -160.125)
-        lin("a", R("JB"), R("JF"), -159.375)
-        lin("a", R("JT"), R("JF"), -160.0, 0.5)
+        cast(R("JI"), JF())
+        lin("a", R("JY"), JF(), -160.125)
+        lin("a", R("JB"), JF(), -159.375)
+        lin("a", R("JT"), JF(), -160.0, 0.5)
         unit("EB", 1)
         ts(R("JI"), R("JI"), 1, Op.bitwise_and)
-        copy("a", R("LN1", 3 * W1, 4 * W1), R("JF", 0, W1))
-        copy("a", R("LN2", 3 * W2, 4 * W2), R("JF", W1, 84))
         unit("EB", 2)
         ts(R("JA"), R("JI"), -0.25, Op.mult)
         unit("EB", 3)
@@ -356,9 +444,9 @@ def rank_program(g, core, T, topo):
             copy("a", X(208, 264), (R("YP"), LO(28, 42)))
             copy("a", X(264, 320), (R("YP"), LO(42, 56)))
 
-        j0, w, LN = (W1, W2, "LN2") if last else (0, W1, "LN1")
+        j0, w, at = (W1, W2, (1, 3, 2)) if last else (0, W1, (0, 1, 2))
         J = lambda n: R(n, j0, j0 + w)
-        ln = lambda i, e=None: R(LN, w * i, w * (e or i + 1))
+        ln = lambda i, e=None: R("LN", 4 * j0 + w * i, 4 * j0 + w * (e or i + 1))
         wo = lambda i: R("WO", 64 * i, 64 * i + w)
         quant("QX", 0, 192, X(0, 192))
         mm(0, 192, "EB", 0, "QX", 0)
@@ -367,9 +455,9 @@ def rank_program(g, core, T, topo):
         act(wa(2), R("QK", 0, 20), Fn.Abs, K, -1.0)
         lin("a", kh, K, 0.5, -1.0)
         lin("a", wa(3), wa(2), cm, -1.0)
-        ts(ln(0), J("JY"), akp, Op.add, 4.0 / 3.0, Op.mult)
-        ts(ln(1), J("JB"), akm, Op.add, 4.0, Op.mult)
-        ts(ln(2), J("JA"), K, Op.add, 4.0, Op.mult)
+        ts(ln(at[0]), J("JY"), akp, Op.add, 4.0 / 3.0, Op.mult)
+        ts(ln(at[1]), J("JB"), akm, Op.add, 4.0, Op.mult)
+        ts(ln(at[2]), J("JA"), K, Op.add, 4.0, Op.mult)
         quant("QX", 192, 320, X(192, 320))
         mm(4, 128, "EB", 0, "QX", 192)
         for b in (2, 1, 3):
@@ -438,8 +526,10 @@ def rank_program(g, core, T, topo):
         if t == 0:
             quant("QV", 0, 128, R("VT"))
         if last:
-            copy("a", R("LOR"), (R("IOT"), LO(0, 20)))
-            store("s", T.lo[:], T.LOR[0:128:16, :], R("LOR"), "lo")
+            lin("a", R("LF", 0, 20), wo(3), cp)
+            call({"v": lambda e: e.transpose(T.LT[:], T.LF[:])}, [R("LT")], [R("LF")])
+            for i in range(8):
+                store("s", T.lo[i:i + 1, :], T.LT[32 * (i // 2):32 * (i // 2) + 20, 16 * (i % 2):16 * (i % 2) + 16], R("LT"), "lo%d" % i)
         for b in range(4):
             copy("a", YP(b, 0, 192), bank(RBANK[0][b], 0, 192), 0.03125)
         for b in range(4):

@@ -4,156 +4,52 @@ PAD = 384
 XW = PAD + 1280
 WIN = PAD + 768
 PART = ((0, 192), (192, 320))
-W1, W2 = 64, 20
+SLOTS = 112
+GQ = 3 * SLOTS
+W1, W2, WS = 44, 20, 20
+HALVES = (1, 2, 3)
+FUSED = ((0, 0), (1, 0), (0, 1))
 BIG = 4096.0
+LEAF = 512
 
 F8, U8, BF, F32, I32, U16 = "float8_e4m3fn_x4", "uint8", "bfloat16", "float32", "int32", "uint16"
 SCRATCH = {"PS": ("psum", [128, 4096], F32)}
-for _n, _w in (("X", XW), ("UT", 512), ("VT", 512), ("BT", 512), ("ZT", 1280), ("PL", 1728), ("AB", 1280), ("FP", 640), ("YP", 1280),
+for _n, _w in (("X", XW), ("UT", 512), ("VT", 512), ("BT", 512), ("ZT", 1280), ("PL", 1728), ("AB", 1280), ("YP", 1280),
                ("ED", 516), ("EDB", 516), ("NUL", 516)):
     SCRATCH[_n] = ("sbuf", [128, _w], BF)
-for _n, _w in (("QU", 128), ("UU", 256), ("QV", 128), ("QW", 512), ("EH", 512), ("EB", 512), ("QS", 128), ("QX", 320), ("QZ", 320),
-               ("QF", 320), ("B0", 128), ("B1", 128), ("B2", 128), ("G0", 128), ("G1", 128), ("G2", 128)):
+for _n, _w in (("QU", 128), ("UU", 256), ("QV", 128), ("QW", 512), ("EH", 512), ("EB", 512), ("QS", 128), ("QX", GQ + 320), ("QZ", 320),
+               ("QF", 320), ("B0", 128), ("B1", 128), ("B2", 128)):
     SCRATCH[_n] = ("sbuf", [128, _w], F8)
     SCRATCH[_n + "s"] = ("sbuf", [128, _w], U8)
-for _n, _w in (("C4", 28), ("C16", 20), ("CT", 51), ("TC", 51), ("ZQ", 8), ("Z2", 8), ("LANE", 4), ("PM", 2), ("NIL", 65), ("JY", 84),
-               ("JB", 84), ("JA", 84), ("JT", 84), ("LN", 4 * W1 + 4 * W2), ("MX", 2 * W1), ("LF", 32), ("LT", 32), ("YO", 320),
-               ("RMC", 65), ("RMK", 105), ("SGC", 65), ("SGK", 105), ("CK", 16), ("QK", 21), ("W8", 64), ("WA", 320), ("WO", 256)):
+for _n, _w in (("RUN", 28), ("LANE", 16), ("CT", 54), ("TC", 54), ("ZQ", 8), ("ZN", 8), ("ZR", 8), ("PM", 2), ("K0", 2), ("NIL", 65),
+               ("J", 64), ("JY", 64), ("JB", 64), ("JA", 64), ("LN", 4 * W1 + 4 * W2), ("MX", 2 * W1), ("VF", W1), ("G1", WS + W1),
+               ("G2", WS + W1), ("LF", 32), ("LT", 32), ("YO", 320), ("RMC", 65), ("RMK", 25), ("SGC", 65), ("SGK", 25), ("CK", 8),
+               ("W8", 32), ("WA", 240)):
     SCRATCH[_n] = ("sbuf", [128, _w], F32)
-for _n, _w in (("LI", 4), ("JI", 84), ("PO", 16), ("SH", 2 * W1), ("BB", 2 * W1)):
+for _n, _w in (("LI", 6), ("PO", 16), ("L3", W1), ("SH", W1), ("VI", W1)):
     SCRATCH[_n] = ("sbuf", [128, _w], I32)
-for _n, _w in (("PU", 16), ("LR", 8), ("L1", 20), ("L2", 8), ("LA", 20), ("LO", W1)):
+for _n, _w in (("PU", 16), ("LR", 8), ("L1", 20), ("L2", 8), ("LA", 20), ("LO", WS + W1)):
     SCRATCH[_n] = ("sbuf", [128, _w], U16)
-DMAS = ["d%d" % i for i in range(16)]
+DMAS = ["d%d" % i for i in range(8)]
 SEMAPHORES = ["v", "a", "t", "g", "out", "arr0", "arr1", "arr2", "sent"] + DMAS
-RBANK = ((0, 7, 4, 5), (6, 1, 2, 3))
-GBANK = (6, 4, 7, 5)
 ORDER = """
-cUT0:a cX704:s cCT49:v cLI0:g cJF0:g cJF28:g cC160:g cC40:g cCT48:v cNIL0:v cLI1:v cLI3:v cLI2:v cX0:v cLANE0:v cCT50:v cW88:a cW80:a cZ20:a cW816:a
-cX160:v cX1216:s cX384:s cQW0:s cQWs0:s cVT0:s cLANE0':a cZQ0:a cCT28:v cHALF0:v cPO0:g cPU0:v cQU0:v cUUs0:a cLR0:v cUU0:v cQS0:v cUU128:v cCT0:v
-cUUs128:a cCT28':a 0JF0:a 0UU0QS0:t 0RMC0:v 0JF56:a cJF8:g 0JF8:a 0SGC0:a cRMK0:v cPM1:v 0UU1QS0:t 0RMK80:v 0JF64:a 0CK2:v 0CK3:v 0TC0:v 0W832:v
-0SGK0:a 0W824:v 0L10:v 0X32:a 0W840:v 0BT0:a 0CK4:a 0JB0:a 0JI0:v 0QK0:a 0JY0:a 0W848:v 0L20:v cBT448:v 0BT320:v cED0:g cPM0:v 0CK10:a 0B00:v 0G0112:s
-0G0s112:s 0G1112:s 0G2112:s 0G1s112:s 0G2s112:s 0JI0':v 0EH384:v 0QX192:v 0G00:g 0EH256:v 0EH128:v 0QX0:v 0EH1QX0:t 0EDB0:a 0JT0:a 0WA0:a 0WA20:a
-0LN10:v 0EB0:v 0WA40:a 0CK5:a 0EH3QX0:t 0EB0QX0:t 0LN164:v 0JA0:v 0EB128:v 0WA80:v 0WA60:a 0JA0':v 0WA100:v 0CK6:v 0PL432:a 0LN1192:a 0EB1QX192:t
-0EB0QX192:t 0PL0:a 0EB0QX0':t 0EH2QX0:t 0WA120:a 0QV0:v 0LN1128:v 0EB256:v 0WA140:v 0PL192:a 0EH1G00:t 0PL1296:a 0LN260:a 0MX0:v 0WA160:v 0SH0:v
-0WA180:v cIOT0:g 0FP320:g 0PL864:a cCK15:a 0PL752:a 0EB0G00:t 0PL320:a 0EH2G00:t 0PL1184:a 0EH3G00:t 0BB64:v 0SH64:v 0EB384:v 0WA200:v 0WO0:v 0LA0:v
-0AB640:a 0WO128:v 0ZT1:v 0PL1616:v 0FP0:g 0ZT0:v 0EB2QX0:t 0EB3QX0:t 0EB1QX0:t 0ZT2:v 0EB2QX192:t 0EB0QX192':t 0AB960:a 0ZT3:v 0EB3QX192:t 0BB0:v
-0QZ0:v 0QW3QZ0:t 0QW2QZ0:t 0QW1QZ0:t 0AB832:a 0AB1152:a 0AB512:a 0YP960:a 0YP640:a 0YP320:a 0QW0QZ0:t 0ZT770:v 0ZT768:v 0ZT769:v 0ZT771:v 0WO64:v
-0QZ192:v 0QW0QZ192:t 0YP192:a 0QW1QZ192:t 0YP512:a 0QW2QZ192:t 0YP832:a 0WO192:v 0YP0:v 0LO0:v 0X704:v 0X705:a 0QW3QZ192:t 0YP1152:v 0X706:a 0LO8:v
-0X707:v 1QS0:v 1UU0QS0:t 1X32:a 1X512:a 1X1216:v 1RMC0:v 1UU1QS0:t 1RMK80:v 1SGC0:a 1CK2:v 1CK3:v 1SGK0:a 1W824:v 1W832:v 1TC0:a 1L10:v 1W840:v 1CK4:v
-1W848:v 1LN1128:v 1L20:v 1X384:a 1QK0:a 1BT0:a 1BT320:v 1B10:v 1G10:g 1QX0:v 1EB0QX0:t 1X1440:a 1QX192:v 1EH1QX0:t 1WA40:a 1WA0:a 1CK10:a 1LN10:v
-1WA20:a 1WA80:v 1LN164:v 1WA60:a 1CK5:a 1WA100:v 1EB0QX192:t 1EH3QX0:t 1EH2QX0:t 1PL0:a 1CK6:v 1MX0:v 1WA120:a 1WA140:v 1PL432:a 1EB1QX192:t
-1EB0QX0':t 1PL192:a 1SH0:v 1WA160:v 1BB64:v 1WA180:v 1SH64:v 1BB0:v 1WO0:v 1PL1296:a 1WA200:v 1WO128:v 1PL864:a 1EH2G10:t 1PL1184:a 1LA0:v 1AB640:a
-1EB0G10:t 1PL320:v 1FP0:g 1ZT0:v 1EH1G10:t 1EH3G10:t 1PL1616:a 1ZT2:v 1FP320:g 1PL752:a 1ZT1:v 1EB1QX0:t 1EB0QX192':t 1EB2QX0:t 1EB3QX0:t 1EB2QX192:t
-1AB960:a 1ZT3:v 1EB3QX192:t 1WO64:v 1QZ0:v 1QW1QZ0:t 1ZT768:v 1AB832:a 1AB1152:a 1ZT771:v 1AB512:a 1ZT770:v 1ZT769:v 1QZ192:v 1YP320:a 1QW2QZ0:t
-1YP640:a 1QW3QZ0:t 1YP960:a 1WO192:v 1LO0:v 1QW0QZ0:t 1QW0QZ192:t 1YP192:v 1YP0:a 1X704:v 1QW1QZ192:t 1YP512:a 1QW2QZ192:t 1YP832:a 1X705:a
-1QW3QZ192:t 1YP1152:v 1LO8:v 1X706:a 1X707:v 2QS0:v 2X384:v 2UU0QS0:t 2RMC0:v 2UU1QS0:t 2RMK80:v 2X32:a 2X512:a 2QX0:v 2EB0QX0:t 2SGC0:a 2CK2:v 2CK3:v
-2SGK0:a 2W824:v 2W832:v 2QK0:a 2TC0:a 2L10:v 2X1440:a 2W840:v 2W848:v 2CK10:v 2L20:v 2CK4:v 2BT0:a 2BT320:v 2B20:v 2LN20:v 2LN220:v 2X1216:a 2QX192:v
-2EB0QX192:t 2EH1QX0:t 2EH3QX0:t 2WA0:a 2WA40:a 2WA20:a 2LN240:v 2WA80:v 2CK6:v 2PL0:a 2EB0QX0':t 2WA100:v 2WA60:a 2WA120:a 2PL192:a 2PL432:a 2PL1296:a
-2EH2QX0:t 2PL864:a 2MX0:v 2CK5:v 2SH0:v 2WA140:v 2BB0:v 2BB20:v 2WA160:v 2WO64:v 2WA180:v 2WO0:v 2SH20:v 2WA200:v 2WO128:v 2LA0:v 2G20:g 2EB0G20:t
-2PL320:v 2WO192:v 2FP0:g 2ZT0:v 2ZT768:v 2EH2G20:t 2PL1184:a 2AB640:a 2ZT2:v 2EH3G20:t 2PL1616:a 2EH1G20:t 2EB1QX192:t 2EB0QX192':t 2EB1QX0:t 2PL752:a
-2FP320:g 2ZT1:v 2EB2QX0:t 2EB3QX0:t 2EB2QX192:t 2AB960:a 2ZT3:v 2EB3QX192:t 2LO0:v 2QZ0:v 2QW0QZ0:t 2QW2QZ0:t 2QW3QZ0:t 2QW1QZ0:t 2AB512:a 2ZT769:v
-2AB832:a 2ZT770:v 2AB1152:a 2ZT771:v 2LOR0:a 2lo:s 2QZ192:v 2QW0QZ192:t 2YP0:v 2YP640:v 2YP320:v 2YP960:a 2YP192:a 2X384':v 2QW1QZ192:t 2YP512:a
-2QW3QZ192:t 2QW2QZ192:t 2YP832:v 2YP1152:a 2X387:v eX1152:v 2X385:a 2X386:a eQF0:v eQV0QF0:t eoc0:s eX1155:v eX1153:a eX1154:a eQF192:v eoc1:a
-eQV0QF192:t eYO0:v ey0:s eosc3:s eosc2:s eYO192:a eosc1:a eosc0:s ey1:s
-"""
-ORDER = """
-cUT0:a cNUL0:v cLI0:g cLI3:v cLI2:v cLI1:v cCT48:v cLANE0:v cCK15:a cPO0:g cC40:g cCT49:g cLN192:g cLN220:g 0LN192:a cW88:a cRMK0:v cX160:v cLANE0':v
-cX704:s cX1216:s cX384:s cPU0:v cC160:g cCT0:v cCT28:v cCT50:v cLN200:g cNIL0:g cW80:a cW816:a cZ20:a cZQ0:a cQW0:s cQWs0:s cVT0:s cED0:g cBT448:g
-cX0:g cPM0:g cQU0:v cUUs0:a cLR0:v cUU0:v cQS0:v cUU128:v 0LN256:v 0UU0QS0:t 0RMC0:v 0QX192:v cUUs128:a 0UU1QS0:t 0RMK80:v 0LN200:a 0LN248:a 0JI0:v
-0SGC0:a 0CK2:v 0CK3:v cCT28':a 0SGK0:a 0W824:v 0W832:v 0TC0:a 0L10:v 0W840:v 0CK4:v 0W848:v 0CK6:v 0L20:v 0JI0':v 0X32:a 0BT320:v 0QK0:a 0JA0:v 0BT0:a
-0B00:v 0G0112:s cEDB0:g 0G00:g 0EB0:v 0EB0QX192:t 0QX0:v 0EB0QX0:t 0EH128:v 0WA0:a 0WA40:a 0WA20:a 0WA80:v 0CK10:a 0JB0:a 0JT0:a 0JY0:a 0WA60:a
-0PL192:a 0LN64:v 0WA100:v 0WA120:a 0EH1QX0:t 0PL432:a 0CK5:a 0EH256:v 0JA0':v 0EH384:v 0LN0:v 0WA140:v 0EB256:v 0EB384:v 0LN128:v 0WA160:v 0EB128:v
-0MX0:v 0WA180:v 0EH2QX0:t 0EH3QX0:t 0PL0:a 0EB0QX0':t 0PL1296:a 0PL864:a 0G0s112:s 0EH1G00:t 0PL752:a 0G1112:s 0G2112:s 0G1s112:s 0G2s112:s 0EH2G00:t
-0PL1184:a 0SH0:v 0WA200:v 0BB0:v 0LA0:v 0BB64:v 0FP320:g 0ZT1:v 0EB0G00:t 0PL320:a 0EH3G00:t 0PL1616:a 0EB1QX192:t 0EB3QX0:t 0FP0:g 0ZT0:v 0WO64:v
-0AB640:a 0ZT2:v 0AB960:a 0ZT3:v 0SH64:v 0QZ0:v 0EB1QX0:t 0EB0QX192':t 0EB2QX192:t 0EB2QX0:t 0AB1152:a 0AB832:a 0ZT768:v 0ZT770:v 0EB3QX192:t 0AB512:a
-0ZT771:v 0ZT769:v 0QW2QZ0:t 0YP640:a 0QW0QZ0:t 0YP0:a 0QW3QZ0:t 0YP960:a 0QW1QZ0:t 0YP320:a 0WO0:v 0QZ192:v 0QW1QZ192:t 0QW0QZ192:t 0YP192:a
-0QW2QZ192:t 0YP832:a 0WO128:v 0WO192:v 0YP512:v 0LO0:v 0X705:a 0LO8:v 0QW3QZ192:t 0YP1152:v 0X704:v 0X706:a 0X707:v 1QS0:v 1UU0QS0:t 1X1216:v 1RMC0:v
-1UU1QS0:t 1RMK80:v 1X384:a 1X512:a 1QX0:v 1EB0QX0:t 1X32:a 1SGC0:a 1CK2:v 1CK3:v 1SGK0:a 1W824:v 1W832:v 1TC0:v 1W840:v 1L10:v 1W848:v 1CK4:v 1L20:v
-1QK0:a 1X1440:a 1QX192:v 1EB0QX192:t 1WA0:a 1BT320:v 1LN128:v 1BT0:a 1B10:v 1G10:g cLF20:g 1WA20:a 1WA80:v 1CK10:a 1LN0:v 1LN64:v 1WA100:v 1CK6:v
-1MX0:v 1PL192:a 1PL0:a 1FP0:g 1WA40:a 1WA120:a 1WA140:v 1WA60:v 1SH0:v 1WA160:v 1CK5:a 1EH1QX0:t 1EH3QX0:t 1PL1296:a 1PL432:a 1EH2QX0:t 1PL864:a
-1BB64:v 1WA180:v 1SH64:v 0QV0:v 1WA200:v 1WO0:v 1EH2G10:t 1PL1184:a 1LA0:v 1AB640:a 1EB0G10:t 1EH1G10:t 1EH3G10:t 1PL1616:a 1EB1QX192:t 1EB1QX0:t
-1WO128:v 1PL320:v 1BB0:v 1ZT0:v 1EB0QX192':t 1ZT2:v 1PL752:a 1FP320:g 1ZT1:v 1EB3QX0:t 1EB0QX0':t 1EB2QX192:t 1EB2QX0:t 1AB960:a 1ZT3:v 1EB3QX192:t
-1QZ0:v 1AB512:a 1ZT769:v 1AB1152:a 1ZT768:v 1ZT771:v 1AB832:a 1ZT770:v 1QW1QZ0:t 1QW3QZ0:t 1YP320:a 1QW0QZ0:t 1YP960:a 1YP0:a 1WO64:v 1QW2QZ0:t
-1QZ192:v 1WO192:v 1YP640:v 1QW0QZ192:t 1YP192:a 1LO0:v 1LO8:v 1X704:v 1QW1QZ192:t 1YP512:a 1QW2QZ192:t 1YP832:a 1X705:a 1QW3QZ192:t 1YP1152:v 1X707:v
-1X706:a 2QS0:v 2X32:a 2X384:v 2UU0QS0:t 2RMC0:v 2UU1QS0:t 2RMK80:v 2X512:a 2QX0:v 2SGC0:a 2CK2:v 2CK3:v 2SGK0:a 2W824:v 2W832:v 2TC0:a 2L10:v 2QK0:a
-2X1440:a 2W840:v 2LN296:v 2W848:v 2CK4:v 2L20:v 2CK10:v 2BT320:v 2LN276:v 2BT0:a 2B20:v 2G20:g 2LN316:v 2X1216:a 2QX192:v 2WA0:a 2WA20:a 2WA80:v
-2MX0:v 2WA100:v 2SH0:v 2CK6:v 2CK5:a 2WA40:a 2EB0QX0:t 2PL0:a 2BB0:v 2WA120:a 2WA140:v 2WO64:v 2WA60:v 2WA160:v 2SH20:v 2WA180:v 2BB20:v 2WA200:v
-2WO0:v 2EB0QX192:t 2PL192:a 2FP0:g 2EH1QX0:t 2PL432:a 2FP320:g 2EH3QX0:t 2PL1296:a 2EH2QX0:t 2PL864:a 2LA0:v 2EB0G20:t 2PL320:v 2WO128:v 2ZT0:v
-2ZT768:v 2EH2G20:t 2PL1184:a 2AB640:a 2ZT2:v 2EH1G20:t 2EH3G20:t 2EB1QX192:t 2EB0QX192':t 2EB0QX0':t 2PL1616:a 2PL752:a 2ZT1:v 2EB1QX0:t 2EB3QX0:t
-2AB960:a 2ZT3:v 2WO192:v 2QZ0:v 2EB2QX192:t 2EB2QX0:t 2AB832:a 2ZT770:v 2AB512:a 2ZT769:v 2EB3QX192:t 2AB1152:a 2ZT771:v 2LF0:a 2LT0:v 2lo0:s 2lo4:s
-2lo2:s 2lo5:s 2lo1:s 2lo7:s 2lo3:s 2lo6:s 2QZ192:v 2QW1QZ0:t 2YP320:a 2QW0QZ0:t 2YP0:a 2QW3QZ0:t 2YP960:v 2LO0:v 2QW2QZ0:t 2YP640:a 2QW0QZ192:t
-2YP192:v 2X384':v 2QW1QZ192:t 2YP512:a 2QW3QZ192:t 2QW2QZ192:t 2YP832:v 2YP1152:a 2X387:v eX1152:v 2X385:a 2X386:a eQF0:v eQV0QF0:t eoc0:s eX1154:a
-eX1155:v eX1153:a eQF192:v eosc2:a eQV0QF192:t eoc1:s eYO0:v ey0:a eYO192:a eosc3:a eosc0:s eosc1:s ey1:s
-"""
-ORDER = """
-cUT0:a cNUL0:v cLI0:g cCT49:g cLI3:v cLI1:v cLI2:v cCT50:v cLANE0:v cRMK0:v cC40:g cPO0:g cPM0:g cLN200:g cLN220:g cC160:g cNIL0:g cLANE0':a cW88:a
-0LN256:a cCT48:v cW80:v cCT0:v cPU0:v cX704:s cX1216:s cX384:s cBT448:g cQW0:s cQWs0:s cVT0:s 0LN200:a cW816:a cCT28:v cCT28':a cQU0:v 0LN248:v cUU0:v
-cQS0:v cUUs0:a 0UU0QS0:t cUU128:v cLR0:v 0RMC0:v cZQ0:a cUUs128:a 0UU1QS0:t cLN192:g 0LN192:a cX0:g 0JI0:v cW80':a cZ20:v 0RMK80:v 0SGC0:a 0QK0:a
-cX160:g cED0:g 0CK3:v 0JI0':v 0W832:v 0SGK0:a 0W824:v 0W840:v 0TC0:a 0L10:v 0W848:v 0QX192:v 0L20:v 0X32:a 0JA0:v 0BT320:v 0BT0:a 0B00:v 0G0112:s
-0EH128:v 0QX0:v 0EH256:v 0G00:g cEDB0:g 0WA0:a 0CK4:a 0EB0:v 0JT0:a 0WA20:a 0WA80:v 0JY0:a 0CK10:a 0JA0':v 0EH384:v 0WA100:v 0LN128:v 0LN0:v 0JB0:a 0LN64:v
-0CK6:v 0WA40:a 0EH1QX0:t 0PL432:a 0WA120:a 0WA140:v 0CK5:a 0WA60:a 0MX0:v 0WA160:v 0EB256:v 0EB0QX192:t 0EH2QX0:t 0EB0QX0:t 0PL0:a 0PL192:a 0WA180:v
-0EB384:v 0EB128:v 0WA200:v 0G0s112:s 0EH3QX0:t 0PL1296:a 0PL864:a 0EB0G00:t 0PL320:a 0EH2G00:t 0EH1G00:t 0PL752:a 0G1112:s 0G2112:s 0G1s112:s
-0G2s112:s 0EH3G00:t 0PL1616:a 0SH0:v 0LA0:v 0QV0:v 0BB64:v 0SH64:v 0BB0:v 0PL1184:v 0AB640:a 0EB1QX0:t 0FP320:g 0FP0:g 0ZT0:v 0WO0:v 0ZT1:v 0ZT2:v
-0EB3QX0:t 0EB0QX192':t 0EB2QX0:t 0EB1QX192:t 0EB0QX0':t 0AB960:a 0ZT3:v 0ZT768:v 0QZ0:v 0AB832:a cCK15:a 0EB3QX192:t 0AB512:a 0ZT769:v 0EB2QX192:t
-0ZT770:v 0AB1152:a 0ZT771:v 0QW2QZ0:t 0YP640:a 0WO64:v 0QW0QZ0:t 0YP0:a 0QW1QZ0:t 0YP320:a 0QZ192:v 0QW2QZ192:t 0YP832:a 0QW0QZ192:t 0QW3QZ0:t
-0YP960:a 0WO128:v 0WO192:v 0YP192:v 0LO8:v 0LO0:v 0X706:a 0QW1QZ192:t 0YP512:v 0X705:a 0QW3QZ192:t 0YP1152:v 1X384:a 1X32:a 0X704:v 0X707:v 1QS0:v
-1UU0QS0:t 1X1216:v 1RMC0:v 1SGC0:a 1UU1QS0:t 1RMK80:v 1SGK0:a 1QX0:v 1EB0QX0:t 1CK3:v 1TC0:v 1W824:v 1QK0:a 1W832:v 1CK10:v 1W840:v 1L10:v 1W848:v
-1X1440:a 1QX192:v 1EB0QX192:t 1EH1QX0:t 1EH2QX0:t 1EH3QX0:t 1L20:v 1LN0:v 1BT320:v 1LN64:v 1BT0:a 1B10:v 1WA0:a 1CK4:a 1WA40:a 1WA20:a 1PL432:a
-1EB1QX192:t 1PL0:a 1LN128:v 1CK5:v 1WA80:v 1MX0:v 1WA100:v 1WA120:a 1CK6:v 1WA60:v 1SH0:v 1WA140:v 1PL192:a 1PL1296:a 1PL864:a 1BB0:v 1WA160:v 1BB64:v
-1WA180:v 1WO64:v 1WO0:v 1WA200:v 1SH64:v 1LA0:v 1WO128:v 1G10:g 1EB0G10:t cLF20:g 1FP0:g 1PL320:a 1ZT0:v 1ZT768:v 1EH2G10:t 1PL1184:a 1EH3G10:t
-1EB0QX0':t 1PL1616:a 1AB640:a 1ZT2:v 1EH1G10:t 1PL752:a 1FP320:g 1ZT1:v 1EB1QX0:t 1EB0QX192':t 1EB2QX0:t 1AB960:a 1ZT3:v 1QZ0:v 1EB2QX192:t 1EB3QX0:t
-1AB512:a 1AB832:a 1AB1152:a 1EB3QX192:t 1ZT770:v 1ZT771:v 1ZT769:v 1QW3QZ0:t 1YP960:a 1QW0QZ0:t 1QW1QZ0:t 1YP320:a 1QW2QZ0:t 1YP640:a 1WO192:v
-1QZ192:v 1QW3QZ192:t 1YP0:v 1LO8:v 1LO0:v 1QW0QZ192:t 1YP192:v 1YP1152:a 1X707:v 1QW1QZ192:t 1YP512:a 1QW2QZ192:t 1YP832:a 1X705:a 1X704:v 2X1440:v
-1X706:a 2QS0:v 2UU0QS0:t 2X32:v 2RMC0:v 2UU1QS0:t 2RMK80:v 2X384:a 2QX0:v 2EB0QX0:t 2SGC0:a 2CK3:v 2TC0:v 2SGK0:a 2W824:v 2QK0:a 2W832:v 2CK10:v
-2W840:v 2L10:v 2W848:v 2LN316:v 2L20:v 2X1216:a 2QX192:v 2CK4:a 2EH3QX0:t 2EB0QX192:t 2EH1QX0:t 2BT320:v 2LN296:v 2BT0:a 2B20:v 2LN276:v 2G20:g 2CK6:v
-2MX0:v 2WA0:a 2WA40:a 2WA20:a 2WA80:v 2PL0:a 2PL192:a 2EB0QX0':t 2EH2QX0:t 2FP0:g 2SH0:v 2WA100:v 2WA120:a 2CK5:v 2BB0:v 2BB20:v 2WA140:v 2WA60:a
-2PL432:a 2SH20:v 2WA160:v 2WO64:v 2WA180:v 2WO0:v 2WA200:v 2WO128:v 2LA0:v 2PL1296:a 2PL864:a 2EB0G20:t 2PL320:v 2WO192:v 2ZT768:v 2ZT0:v 2EH2G20:t
-2EB1QX192:t 2PL1184:a 2AB640:a 2ZT2:v 2EH3G20:t 2PL1616:a 2EB1QX0:t 2EH1G20:t 2PL752:a 2FP320:g 2ZT1:v 2AB960:a 2ZT3:v 2LF0:a 2LT0:v 2QZ0:v
-2EB0QX192':t 2EB2QX192:t 2EB2QX0:t 2EB3QX0:t 2AB832:a 2ZT770:v 2AB512:a 2ZT769:v 2AB1152:a 2EB3QX192:t 2ZT771:v 2QZ192:v 2QW1QZ0:t 2YP320:a 2QW0QZ0:t
-2YP0:a 2QW3QZ0:t 2YP960:v 2LO0:v 2QW2QZ0:t 2YP640:v 2QW0QZ192:t 2YP192:a 2X384':v 2QW1QZ192:t 2YP512:a 2QW3QZ192:t 2YP1152:a 2QW2QZ192:t 2YP832:v
-2X387:v eX1152:v 2X385:a 2lo3:s 2lo0:s 2lo6:s 2lo1:s 2lo2:s 2lo4:s 2lo7:s 2lo5:s 2X386:a eQF0:v eQV0QF0:t eoc0:s eX1154:a eX1153:a eX1155:v eQF192:v
-eosc0:s eQV0QF192:t eoc1:a eYO0:v ey0:a eosc3:s eosc2:a eosc1:a eYO192:v ey1:s
-"""
-ORDER = """
-cUT0:a cNUL0:v cLI0:g cLI3:v cLI2:v cLI1:v cCT48:v cPO0:g cC40:g cC160:g cCT49:g cNIL0:g cLN192:g cEDB0:g cLN200:g cLANE0:v cLANE0':a cPM0:g cLN220:g
-cW80:a cW88:a cZQ0:a cCT50:v cX160:v cPU0:v cCT28:v cRMK0:v cZ20:a 0LN256:a cX704:s cX1216:s cX384:s cQW0:s cQWs0:s cVT0:s cQU0:v cCT0:v cUU0:v cQS0:v
-cUU128:v cUUs0:a 0UU0QS0:t 0RMC0:v cUUs128:a cW816:a cLR0:v 0LN248:a 0EB0:v 0UU1QS0:t 0RMK80:v 0SGC0:a 0CK2:v 0CK3:v cCT28':a 0TC0:v 0W832:v cBT448:g
-0SGK0:a 0W824:v 0L10:v 0W840:v 0LN192:v 0X32:a 0LN200:a 0W848:v 0JI0:v 0L20:v cX0:g 0BT320:v 0BT0:a 0JI0':v 0CK5:a 0QK0:a cCK15:a 0WA0:a 0B00:v
-0G0112:s 0QX0:v 0QX192:v 0EB0QX192:t 0EB0QX0:t cED0:g 0EH128:v 0EH1QX0:t 0EH384:v 0EH3QX0:t 0CK4:a 0WA40:a 0WA20:a 0JY0:a 0CK10:a 0WA80:v 0G00:g
-0JT0:a 0JB0:a 0WA60:a 0PL192:a 0PL0:a 0EH256:v 0EB0QX0':t 0JA0:v 0WA100:v 0PL432:a 0WA120:a 0EB128:v 0LN0:v 0JA0':v 0LN64:v 0CK6:v 0LN128:v 0EB384:v
-0MX0:v 0EB1QX192:t 0FP320:a 0PL1296:a 0EH2QX0:t 0PL864:a 0WA140:v 0SH0:v 0WA160:v 0EB256:v 0WA180:v 0G0s112:s 0BB64:v 0WA200:v 0BB0:v 0LA0:v 0EH1G00:t
-0PL752:v 0EH2G00:t 0PL1184:a 0G1112:s 0G2112:s 0G1s112:s 0G2s112:s 0WO0:v cLF20:g 0FP0:g 0ZT1:v 0EB0G00:t 0PL320:a 0ZT0:v 0EH3G00:t 0PL1616:a 0AB640:a
-0ZT2:v 0AB960:a 0ZT3:v 0WO64:v 0QZ0:v 0EB0QX192':t 0EB1QX0:t 0EB2QX192:t 0EB3QX0:t 0AB1152:a 0AB832:a 0ZT768:v 0ZT770:v 0AB512:a 0EB2QX0:t 0EB3QX192:t
-0ZT771:v 0ZT769:v 0SH64:v 0QW0QZ0:t 0YP0:a 0QW1QZ0:t 0YP320:a 0QW2QZ0:t 0YP640:a 0QW3QZ0:t 0YP960:a 0QZ192:v 0QW1QZ192:t 0QW0QZ192:t 0YP192:a
-0QW2QZ192:t 0YP832:a 0WO128:v 0QV0:v 0WO192:v 0YP512:v 0LO0:v 0X705:a 0LO8:v 0QW3QZ192:t 0YP1152:v 0X704:v 0X706:a 0X707:v 1QS0:v 1X1216:v 1UU0QS0:t
-1RMC0:v 1UU1QS0:t 1RMK80:v 1X512:a 1X384:a 1QX0:v 1EB0QX0:t 1X32:a 1SGC0:a 1CK2:v 1CK3:v 1SGK0:a 1W824:v 1W832:v 1TC0:a 1L10:v 1W840:v 1QK0:a 1CK10:v
-1W848:v 1LN128:v 1L20:v 1X1440:a 1QX192:v 1EB0QX192:t 1EH1QX0:t 1EH3QX0:t 1EH2QX0:t 1BT320:v 1LN64:v 1BT0:a 1B10:v 1G10:g 1EH2G10:t 1WA0:a 1CK4:a
-1CK5:a 1WA20:a 1WA80:v 1LN0:v 1WA100:v 1MX0:v 1CK6:v 1PL192:a 1PL0:a 1WA40:a 1SH0:v 1WA120:a 1WA140:v 1PL1296:a 1WA60:a 1PL864:a 1PL432:a 1SH64:v
-1WA160:v 1BB0:v 1WA180:v 1WO64:v 1WA200:v 1BB64:v 1LA0:v 1EB0G10:t 1PL320:v 1WO0:v 1FP0:g 1ZT0:v 1PL1184:a 1AB640:a 1ZT2:v 1EH1G10:t 1EH3G10:t
-1EB1QX192:t 1EB0QX0':t 1EB1QX0:t 1EB0QX192':t 1PL1616:a 1PL752:a 1EB3QX0:t 1FP320:g 1ZT1:v 1EB2QX192:t 1EB2QX0:t 1AB960:a 1ZT3:v 1EB3QX192:t 1AB512:a
-1ZT769:v 1AB832:a 1AB1152:a 1QZ0:v 1QW3QZ0:t 1YP960:a 1QW1QZ0:t 1YP320:a 1QW2QZ0:t 1YP640:a 1QW0QZ0:t 1ZT770:v 1ZT768:v 1ZT771:v 1WO128:v 1QZ192:v
-1QW1QZ192:t 1YP512:a 1WO192:v 1YP0:v 1LO0:v 1LO8:v 1QW0QZ192:t 1YP192:v 1QW2QZ192:t 1YP832:a 1QW3QZ192:t 1YP1152:v 1X704:v 1X705:a 1X707:v 1X706:a
-2QS0:v 2UU0QS0:t 2X32:v 2RMC0:v 2UU1QS0:t 2RMK80:v 2X512:a 2X384:a 2QX0:v 2SGC0:a 2CK2:v 2CK3:v 2SGK0:a 2W824:v 2W832:v 2TC0:a 2L10:v 2W840:v 2QK0:a
-2CK10:v 2W848:v 2X1440:a 2LN276:v 2L20:v 2LN316:v 2BT320:v 2LN296:v 2BT0:a 2B20:v 2G20:g 2X1216:a 2QX192:v 2MX0:v 2CK4:a 2WA0:a 2WA40:a 2WA20:a
-2WA80:v 2SH0:v 2WA100:v 2EB0QX0:t 2WA60:v 2PL0:a 2CK5:a 2BB0:v 2CK6:v 2EB0QX192:t 2PL192:a 2FP0:g 2WA120:a 2WA140:v 2SH20:v 2WA160:v 2BB20:v 2WA180:v
-2WO64:v 2EH1QX0:t 2PL432:a 2FP320:g 2EH3QX0:t 2PL1296:a 2EH2QX0:t 2PL864:a 2WA200:v 2WO0:v 2LA0:v 2EB0G20:t 2PL320:v 2WO128:v 2ZT0:v 2ZT768:v
-2EH2G20:t 2PL1184:a 2EH3G20:t 2PL1616:a 2AB640:a 2ZT2:v 2EH1G20:t 2PL752:a 2EB0QX0':t 2ZT1:v 2EB1QX0:t 2EB3QX0:t 2EB1QX192:t 2EB0QX192':t 2AB960:a
-2ZT3:v 2WO192:v 2QZ0:v 2AB512:a 2ZT769:v 2AB832:a 2EB2QX0:t 2EB2QX192:t 2ZT770:v 2AB1152:a 2EB3QX192:t 2ZT771:v 2LO0:v 2QZ192:v 2LF0:a 2LT0:v 2lo1:s
-2lo2:s 2lo6:s 2lo7:s 2lo0:s 2lo4:s 2lo5:s 2lo3:s 2QW1QZ0:t 2YP320:a 2QW2QZ0:t 2YP640:a 2QW3QZ0:t 2YP960:v 2QW0QZ0:t 2YP0:a 2QW1QZ192:t 2QW0QZ192:t
-2YP192:v 2YP512:a 2QW2QZ192:t 2YP832:v 2QW3QZ192:t 2YP1152:a 2X385:a 2X384':v 2X387:v eX1152:v 2X386:a eQF0:v eQV0QF0:t eoc0:s eX1155:v eX1153:a
-eX1154:a eQF192:v eoc1:s eosc2:a eosc3:a eosc0:s eosc1:s eYO0:v ey0:a eQV0QF192:t eYO192:v ey1:s
+.u:a .xm:s .xh:s .xl:s .w:s .ws:s .v:s .p:g .nil:v .x1:v .nul:v .x0:v .i2:v .i3:v .i1:v .i4:v .lane:v xl1:a .run:g .o3:a .po:g .ct5:a .o2:a .op0:v .k0:a .ct6:a .ct4:a .zr:v .ct2:v .bt:v .o1:a xh1:a .pu:v .edb:g .o4:v .o0:v .qu:v .uc1:v .uc0:v .ct0:a qs:v .us0:a .us1:a .ed:g .ct3:v .o8:v .j2:v sc:t .zn:a sk:t .zq:a xl0:v .ct1:a .ct7:a .pm:v mc:v c:a mk:v k:a .lr:v tc:a fj:v xt:a b0:v a0:a b1:v b2:v l1:v b3:v k2:v l2:v a1:v bm:a bt:v a3:v qb:v qx0:v a4:v xh0:a .j1:v a2:a .eb0:v .op2:v e00:t .j0:a qx1:v .jf0:v ak:a .eb1:v .jy:v e01:t a7:a .qv:v send:g .op1:a .ja0:v p00:a .jb:a n0:v .eh2:v .ja1:v a5:v .eh3:v n2:v a6:a n3:v e10:t t00:g h2:t p01:a e11:t .ja2:v .eb2:v p10:a h3:t n1:v g2:t t01:g n4:v a8:v p2:a g0:t n5:v a9:v p11:v aa:v g1:t .eb3:v t11:g p3:a n6:v pg0:a ab:v g3:t n7:v pg2:v pg3:a la:v o0:t f1:t f2:t pg1:v y02:a z00:v y03:a z01:v z02:v y13:a f3:t z03:v t10:g y12:a n8:a .gs:a n9:a z11:v d2:t f0:t d3:t qz0:v o1:t lf:a w03:t w00:t w02:t z10:v r03:a w01:t z12:v z13:v lt:v qz1:v so6:s w10:t r00:a lo:v r02:a r01:v w11:t w12:t r11:a w13:t r10:v r12:v so0:s !x10:a so3:s r13:a !x00:v so2:s so4:s !x01:v !x12:a !x03:a !x02:v so5:s !x11:a !x13:a !q0:v .jf1:v so1:s so7:s !q1:v xm0:a !v0:t .lf:v !oc0:s !v1:t !y0:v !oc1:a !os0:s !os1:s !y1:v !os3:s !os2:s xm1:v !sy0:a !sy1:a
 """
 
 
-def rank_program(g, core, T, topo):
-    rank = T.rank_of(core)
-    if rank is None:
-        return
-    N = len(T.cores)
+ORDER = """
+.u:a .xm:s .xh:s .xl:s .w:s .ws:s .v:s .p:g .x0:v .nil:v .bt:v .nul:v .i2:v .i3:v xh1:a .run:g .ct4:a .i1:v .x1:v .i4:v .po:g .k0:a .pu:v .lane:v .qu:v .o0:a .ct7:a .j2:a .o1:v .uc0:v .o2:a .o3:a .edb:g .us0:a qs:v .us1:a .pm:a .uc1:v .ct0:a .ct1:v xl0:v sc:t xl1:v .ed:g .zr:v .ct2:a .ct5:a .eb1:v mc:v sk:t .zn:a .lr:v mk:v qx0:v xh0:a .zq:a qx1:v .ct6:a .ct3:a c:a fj:v k:a b0:v .o4:a k2:v tc:a xt:a b1:v b2:v l1:v a1:a e01:t b3:v a0:a .j1:a a3:v l2:v bm:a .j0:v a4:v bt:v p01:a ak:a a5:v a2:a qb:v .jy:v .eb0:v e00:t e11:t .jb:v send:g .op2:v a6:a .eh2:v p00:a .eb2:v n0:v p11:v .eh3:v .op0:a n2:v .eb3:v h2:t .o8:v e10:t p10:a .ja0:a .ja2:v h3:t a8:v t01:g .op1:a .jf0:a n1:v p2:a .ja1:a n3:v g0:t a7:v t00:v a9:v n4:v g1:t p3:a .qv:v aa:v .gs:a n5:v t10:g t11:g g2:t ab:v pg2:a n6:v g3:t pg3:a la:v y02:a n7:v o1:t pg0:v y03:a f2:t y13:a o0:t pg1:v z00:v z01:v z11:v f3:t z02:v f1:t z03:v f0:t d2:t d3:t z10:v y12:a n8:a qz0:v w00:t z12:v z13:v n9:a w02:t lo:v lf:a qz1:v lt:v r02:a w01:t w03:t so5:a r00:v w10:t w11:t r01:v r10:v so4:s w12:t r03:a r12:v so3:s !x00:v .lf:v r11:a !x02:v so6:s w13:t r13:a !x01:a !x10:v .jf1:a so0:s !x03:a !x11:a !q0:v so7:s so1:s !x12:a !x13:v !q1:v !v0:t xm1:v !v1:t !y0:v !oc0:s !y1:v so2:a !os0:a !oc1:s !os1:a !sy0:s xm0:a !os3:s !os2:a !sy1:s
+"""
+
+
+ORDER = """
+.u:a .xm:s .xh:s .xl:s .w:s .ws:s .v:s xh1:a xl1:v .x0:v .p:g .nul:v .i2:v .i3:v .po:g .run:g .nil:v .x1:v .i1:v .i4:v .ct7:v .ct5:a .lane:v .j3:a .pu:v .o3:a .zr:a .k0:v .ed:g .qu:v xh0:a .ct2:a .bt:v .o2:v .uc0:v .us0:a qs:v sc:t .o1:a .uc1:v .ct1:v .us1:a .j1:a .ct3:v xl0:v .zq:a .lr:v .ct6:v .o0:a .o4:a sk:t .op1:a mc:v .ct0:v .ct4:a mk:v qx0:v qx1:v .j2:a c:a .pm:a k:a fj:v tc:a .zn:a xt:a b0:v a0:a k2:v l1:v .edb:g b1:v b2:v .eh1:v a1:a h1:t b3:v a3:v ak:v bm:a l2:v bu:a a4:v bt:v .j0:a .jf0:a a5:v a2:a .o8:v .jb:a qb:v a6:a .ja1:a .eb0:v e10:t e00:t .eh2:v .op2:a .lf:v .jy:v .eb3:v .eh3:v h3:t n2:v h2:t .op0:a p00:a .qv:v send:g .ja0:a o0:t p10:a g2:t n0:v .ja2:v a8:v .eb1:v n3:v g0:t n1:v a9:v .eb2:v g1:t n4:v a7:a t00:v aa:v g3:t n5:v ab:v p1:a p2:a n6:v .gs:a p3:a d1:t pg2:a pg3:a t10:v la:v t01:v n7:v pg0:v pg1:v z00:v z01:v y02:a f0:t z02:v y03:a y11:a f2:t y12:a f1:t f3:t d2:t z03:v z10:v qz0:v z11:v d3:t y13:a z12:v n8:a n9:a z13:v lf:v w00:t qz1:v r00:a lm:v w03:t w01:t lo:v w02:t w10:t r01:a lt:v so7:s so4:s so6:s so1:s w11:t w12:t r02:v so3:a r03:a r10:v r11:a w13:t r13:a !x01:a r12:v !x03:a xm1:a !x11:a so5:s xm3:a !x00:v !x02:v so2:s !x10:v so0:s !q0:v !x13:v !x12:a xm0:v !v0:t !oc0:a xm2:v !q1:v !y0:v !v1:t !os0:a !y1:v !oc1:s !os2:a !os1:a !os3:s !sy0:s .jf1:a !sy1:s
+"""
+
+
+def plan(core, T, topo):
+    rank, N = T.rank_of(core), len(T.cores)
     prev, nxt = T.cores[(rank - 1) % N], T.cores[(rank + 1) % N]
-    queue = {"v": g.vector, "a": g.scalar, "t": g.tensor, "g": g, "s": g.sync}
-    total, seen, clock, uses, free = {}, {q: {} for q in queue}, {}, {}, list(DMAS)
     calls, stage = {}, ["c"]
 
     def R(name, lo=0, hi=None, step=1):
@@ -177,16 +73,346 @@ def rank_program(g, core, T, topo):
                 out += list(r) if len(r) == 2 else [r]
         return out
 
-    def call(forms, outs, ins, kind="run", name=None):
-        outs, ins = pieces(outs), pieces(ins)
-        name = stage[0] + (name or outs[0][0] + str(outs[0][1]))
-        while name in calls:
-            name += "'"
-        calls[name] = (forms, outs, ins, kind)
+    def call(name, forms, outs, ins, kind="run"):
+        calls[stage[0] + name] = (forms, pieces(outs), pieces(ins), kind)
 
-    def wait(q, deps):
+    def load(name, r, src, cast=None):
+        call(name, {q: lambda e: e.dma_start(ap(r, cast), src) for q in "sa"}, [r], [], "dma")
+
+    def store(name, dst, src, r):
+        call(name, {q: lambda e: e.dma_start(dst, src) for q in "sa"}, [], [r], "out")
+
+    def ts_form(out, in0, s1, op0, s2=None, op1=None):
+        if op1 is None:
+            return lambda e: e.tensor_scalar(ap(out), ap(in0), ap(s1), None, op0)
+        return lambda e: e.tensor_scalar(ap(out), ap(in0), ap(s1), ap(s2), op0, op1)
+
+    def ts(name, out, in0, s1, op0, s2=None, op1=None):
+        call(name, {"v": ts_form(out, in0, s1, op0, s2, op1)}, [out], [in0, s1, s2])
+
+    def tt(name, out, a, b, op):
+        call(name, {"v": lambda e: e.tensor_tensor(ap(out), ap(a), ap(b), op)}, [out], [a, b])
+
+    def act(name, out, in_, fn, bias=0.0, scale=1.0, accum=None):
+        more = {} if accum is None else {"accum_out": ap(accum)}
+        call(name, {"a": lambda e: e.activation(ap(out), ap(in_), fn, bias=ap(bias), scale=ap(scale), **more)}, [out, accum], [in_, bias, scale])
+
+    def lin(name, out, in_, bias, scale=1.0):
+        call(name, {"a": lambda e: e.activation(ap(out), ap(in_), Fn.Identity, bias=ap(bias), scale=ap(scale)),
+                    "v": ts_form(out, in_, scale, Op.mult, bias, Op.add)}, [out], [in_, bias, scale])
+
+    def copy(name, out, in_, scale=None):
+        if scale is None:
+            forms = {"a": lambda e: e.activation(ap(out), ap(in_), Fn.Copy), "v": lambda e: e.tensor_copy(ap(out), ap(in_))}
+        else:
+            forms = {"a": lambda e: e.activation(ap(out), ap(in_), Fn.Copy, scale=scale), "v": ts_form(out, in_, scale, Op.mult)}
+        call(name, forms, [out], [in_])
+
+    def twin(name, out, in_):
+        call(name, {"g": lambda e: e.affine_select(ap(out), ap(in_), [[0, out[2] - out[1]]], Op.is_ge, 0.0, 0, 0),
+                    "v": lambda e: e.tensor_copy(ap(out), ap(in_))}, [out], [in_])
+
+    def cast(name, out, in_, as_=None):
+        call(name, {"v": lambda e: e.tensor_copy(ap(out, as_), ap(in_, as_))}, [out], [in_])
+
+    def quant(name, q, lo, hi, in_):
+        c, s = R(q, lo, hi), R(q + "s", lo, hi)
+        call(name, {"v": lambda e: e.quantize_mx(ap(c), ap(s), ap(in_))}, [c, s], [in_])
+
+    def bank(b, lo, hi):
+        return ("PS", 512 * b + lo, 512 * b + hi, 1)
+
+    def mm(name, b, n, w, wlo, x, xlo, start=True, stop=True):
+        ins = [R(w, wlo, wlo + 128), R(w + "s", wlo, wlo + 128), R(x, xlo, xlo + n), R(x + "s", xlo, xlo + n)]
+        call(name, {"t": lambda e: e.matmul_mx(ap(bank(b, 0, n)), *[ap(r) for r in ins], start, stop)}, [bank(b, 0, n)], ins)
+
+    def fill(name, r, value):
+        call(name, {"v": lambda e: e.memset(ap(r), value)}, [r], [])
+
+    def iota(name, r, pattern, base, cm=0):
+        more = {} if SCRATCH[r[0]][2] == I32 else {"allow_small_or_imprecise_dtypes": True}
+        call(name, {"g": lambda e: e.iota(ap(r), pattern, base, cm, **more)}, [r], [])
+
+    def scan(name, out, scores):
+        zero = R("NIL", 0, out[2] - out[1])
+        call(name, {"v": lambda e: e.tensor_tensor_scan(ap(out), ap(zero), ap(scores), -1e29, Op.add, Op.max)}, [out], [zero, scores])
+
+    X = lambda lo, hi, b=None: R("X", PAD + 4 * lo, PAD + 4 * hi) if b is None else R("X", PAD + 4 * lo + b, PAD + 4 * hi, 4)
+    HEAD = R("X", 32, 160)
+
+    load("u", R("UT"), T.u[:])
+    load("xm", X(80, 208), T.x[:, 320:832])
+    load("xh", X(208, 320), T.x[:, 832:1280])
+    load("xl", X(0, 80), T.x[:, 0:320])
+    load("w", R("QW"), T.wc[:], dt.uint8)
+    load("ws", R("QWs"), T.ws[:])
+    load("v", R("VT"), T.v[:])
+
+    iota("p", col("LI", 0), [[0, 1]], 0, 1)
+    iota("run", R("RUN"), [[1, 28]], 0)
+    iota("po", R("PO"), [[1, 2], [16, 8]], 0)
+    fill("nul", R("NUL"), 0.0)
+    for name, value in (("EDB", 32.0), ("ED", 0.5)):
+        call(name.lower(), {"g": lambda e, name=name, value=value: e.affine_select(T[name][:], T.NUL[:], [[-1, 516]], Op.not_equal, value, 3, 4)},
+             [R(name)], [R("NUL")])
+    run = lambda n, lo=0: R("RUN", lo, lo + n)
+
+    def const(name, r, value):
+        lin(name, r, run(r[2] - r[1]), value, 0.0)
+
+    ts("i1", col("LI", 1), col("LI", 0), 15, Op.bitwise_and)
+    ts("i2", col("LI", 2), col("LI", 0), 2, Op.logical_shift_right, 3, Op.bitwise_and)
+    ts("i3", col("LI", 3), col("LI", 0), 3, Op.bitwise_and)
+    ts("i4", R("LI", 4, 6), R("LI", 2, 4), 1, Op.bitwise_and)
+    cast("lane", R("LANE", 0, 6), R("LI"))
+    cast("pu", R("PU"), R("PO"))
+    lane, l1, lb, par1, par = (col("LANE", i) for i in range(1, 6))
+    own = lambda i: col("LANE", 6 + i)
+    fill("x0", R("X", 0, 32), 0.0)
+    fill("x1", R("X", 160, PAD), 0.0)
+    fill("bt", R("BT", 4 * SLOTS, 512), 0.0)
+    fill("nil", R("NIL"), 0.0)
+    lin("o0", own(0), lane, PAD / 4 + 48.0, 0.25)
+    lin("ct0", R("CT", 0, 28), run(28), own(0), 4.0)
+    lin("o1", own(1), lane, 127.5, -1.0)
+    lin("ct1", R("CT", 28, 48), run(20), own(1), -16.0)
+    const("ct2", col("CT", 48), -31.875)
+    const("ct3", col("CT", 49), -192.0)
+    const("ct4", col("CT", 50), 127.5)
+    const("ct5", col("CT", 51), 127.5 + LEAF / 2)
+    lin("ct6", col("CT", 52), lb, 127.5 + LEAF / 2, 320.0)
+    const("ct7", col("CT", 53), 128.0)
+    lin("zr", R("ZR"), run(8), l1, 4.0)
+    lin("zq", R("ZQ"), R("ZR"), 0.5)
+    lin("o2", own(2), lb, PAD / 4 - 1.125, 0.25)
+    lin("zn", R("ZN"), R("ZR"), own(2), -1.0)
+    lin("o3", own(3), lb, 124.0)
+    ts("lr", R("LR"), R("ZR"), -4.0, Op.mult, own(3), Op.add)
+    quant("qu", "QU", 0, 128, R("UT"))
+    for h in range(2):
+        pick = R("PU", 8 * h, 8 * h + 8)
+        cast("uc%d" % h, R("UU", 128 * h, 128 * h + 128), (R("QU"), pick), dt.uint32)
+        copy("us%d" % h, R("UUs", 128 * h, 128 * h + 128), (R("QUs"), pick))
+    for b in range(4):
+        quant("eb%d" % b, "EB", 128 * b, 128 * b + 128, R("EDB", 3 - b, 515 - b))
+    for b in HALVES:
+        quant("eh%d" % b, "EH", 128 * b, 128 * b + 128, R("ED", 3 - b, 515 - b))
+    lin("pm", R("PM"), run(2), 1.0, -2.0)
+    lin("k0", R("K0"), run(2), 80.0, -float(LEAF))
+    lin("o4", own(4), l1, 208.0)
+    lin("j0", R("J", 0, 28), run(28), own(4), 4.0)
+    lin("j1", R("J", 28, 36), R("ZR"), 319.0, -1.0)
+    lin("j2", R("J", 44, 64), run(20), lane, 16.0)
+    lin("j3", R("J", 36, 44), run(8, 5), lane, 16.0)
+    lin("jy", R("JY"), R("J"), -80.125)
+    lin("jb", R("JB"), R("J"), -239.375)
+    for i, (lo, hi, odd, base, step) in enumerate(((0, 28, par1, -80.0, -0.25), (28, 36, par1, -80.25, 0.25), (36, 64, par, -80.0, -0.25))):
+        lin("op%d" % i, own(5 + i), odd, base, step)
+        lin("ja%d" % i, R("JA", lo, hi), R("J", lo, hi), own(5 + i), 0.5)
+    lin("jf0", R("LN", 3 * W1, 4 * W1), R("J", 0, W1), 0.0, 4.0 * LEAF + 1)
+    lin("jf1", R("LN", 4 * W1 + 3 * W2, 4 * W1 + 4 * W2), R("J", W1, W1 + W2), 0.0, 4.0 * LEAF + 1)
+    lin("o8", own(8), l1, 0.5 - 1.5 * LEAF, float(LEAF))
+    act("gs", R("G1", 0, WS), run(WS), Fn.Abs, own(8))
+    fill("lf", R("LF", W2, 32), 0.0)
+    quant("qv", "QV", 0, 128, R("VT"))
+
+    C, K, fj, akp, akm, k2, kl = (col("CK", i) for i in range(7))
+    ak, right, cp, cq, cqb, left = (col("TC", 48 + i) for i in range(6))
+    w8 = lambda i: R("W8", 8 * i, 8 * i + 8)
+    wa = lambda i: R("WA", 20 * i, 20 * i + 20)
+    PL = lambda b, lo=0, hi=432: R("PL", 432 * b + lo, 432 * b + hi)
+    YP = lambda b, lo=0, hi=320: R("YP", 320 * b + lo, 320 * b + hi)
+    AB = lambda b, lo, hi: R("AB", 320 * b + lo, 320 * b + hi)
+    LO = lambda lo, hi: R("LO", lo, hi)
+    other = list(HALVES) + [b for b in range(4) if b not in HALVES]
+    result = lambda h, b: b if (b in HALVES) == (h == 1) else 4 + other.index(b)
+    engines = topo.engines(core, prev)
+    mask = sum(1 << e for e in engines)
+    rid, pid = topo.addr(prev)[:2]
+
+    def send(t):
+        lo = GQ - SLOTS * (t + 1)
+
+        def form(e):
+            for name, as_ in (("", dt.uint8), ("s", None)):
+                e.remote_dma(ap(R("QX" + name, lo, lo + SLOTS), as_), ap(R("B%d%s" % (t, name), 0, SLOTS), as_), T.sem["arr%d" % t], T.sem.sent, pid, rid, mask)
+            return 2 * len(engines), ("arr%d" % t, 2 * len(topo.engines(nxt, core)))
+        call("send", {"g": form}, [R("QX", lo, lo + SLOTS), R("QXs", lo, lo + SLOTS)], [R("B%d" % t), R("B%ds" % t)], "far")
+        return lo
+
+    def big(name, h, b, to, stop):
+        lo, hi = PART[h]
+        mm(name, to, hi - lo, "EB", 128 * b, "QX", GQ + lo, True, stop)
+
+    for t in range(3):
+        last = t == 2
+        stage[0] = str(t)
+        quant("qs", "QS", 0, 128, X(80, 208))
+        mm("sc", 6, 128, "UU", 0, "QS", 0)
+        mm("sk", 7, 128, "UU", 128, "QS", 0)
+        if t == 0:
+            copy("xt", HEAD, (X(288, 320), R("LR")))
+        else:
+            copy("xt", HEAD, (R("YP"), LO(48, 56)))
+            copy("xl0", X(0, 40), (R("YP"), LO(0, 10)))
+            copy("xl1", X(40, 80), (R("YP"), LO(10, 20)))
+        scan("mc", R("RMC"), bank(6, 48, 113))
+        scan("mk", R("RMK"), bank(7, 0, 25))
+        act("c", R("SGC"), R("RMC"), Fn.Sign, col("RMC", 64), -1.0, C)
+        act("k", R("SGK"), R("RMK"), Fn.Sign, col("RMK", 24), -1.0, K)
+        act("tc", R("TC"), R("CT"), Fn.Abs, C)
+        ts("fj", fj, C, 32.0, Op.is_lt, 8.25 - PAD / 4, Op.mult)
+        ts("b0", w8(0), R("ZQ"), K, Op.subtract, -BIG, Op.mult)
+        ts("b1", w8(1), R("ZN"), ak, Op.add, fj, Op.add)
+        ts("l1", R("L1"), R("TC", 0, 20), K, Op.subtract, 4.0, Op.mult)
+        tt("b2", w8(2), w8(0), R("TC", 20, 28), Op.min)
+        tt("b3", w8(3), w8(2), w8(1), Op.max)
+        ts("l2", R("L2"), w8(3), K, Op.subtract, 4.0, Op.mult)
+        copy("bm", R("BT", 0, 320), (R("X", 0, WIN), R("L1")))
+        copy("bt", R("BT", 320, 384), (R("X", 0, WIN), R("L2", 0, 4)))
+        copy("bu", R("BT", 384, 448), (R("X", 0, WIN), R("L2", 4, 8)))
+        quant("qb", "B%d" % t, 0, 128, R("BT"))
+        came = send(t)
+        if t:
+            copy("xh0", X(208, 264), (R("YP"), LO(20, 34)))
+            copy("xh1", X(264, 320), (R("YP"), LO(34, 48)))
+        for h, (lo, hi) in enumerate(PART):
+            quant("qx%d" % h, "QX", GQ + lo, GQ + hi, X(lo, hi))
+        for b in range(4):
+            if b in HALVES:
+                mm("h%d" % b, b, 320, "EH", 128 * b, "QX", GQ)
+                copy("p%d" % b, PL(b, 0, 320), bank(b, 0, 320))
+            else:
+                for h in range(2):
+                    big("e%d%d" % (h, b), h, b, result(h, b), True)
+                    copy("p%d%d" % (h, b), PL(b, *PART[h]), bank(result(h, b), 0, PART[h][1] - PART[h][0]), 1.0 / 64.0)
+                big("o%d" % b, 0, b, b, False)
+        for b, h in FUSED:
+            twin("t%d%d" % (h, b), AB(b, *PART[h]), PL(b, *PART[h]))
+        ts("k2", R("CK", 5, 7), R("K0"), K, Op.add, 2.0, Op.mult)
+        lin("a0", wa(0), R("CT", 28, 48), C)
+        lin("a1", wa(1), R("TC", 28, 48), k2, -2.0)
+        act("a2", wa(2), R("TC", 28, 48), Fn.Abs, k2, -2.0)
+        tt("a3", wa(3), wa(0), wa(1), Op.mult)
+        ts("a4", wa(4), wa(3), 0.0, Op.is_lt, k2, Op.mult)
+        tt("a5", wa(5), wa(4), wa(0), Op.add)
+        act("a6", wa(6), wa(5), Fn.Sign, right, -1.0)
+        lin("a7", wa(7), wa(2), right, 0.5)
+        tt("a8", wa(8), wa(5), wa(6), Op.mult)
+        ts("a9", wa(9), wa(8), left, Op.add, -BIG, Op.mult)
+        tt("aa", wa(10), wa(9), wa(7), Op.min)
+        tt("ab", wa(11), wa(10), wa(8), Op.max)
+        ts("la", R("LA"), wa(11), cp, Op.add)
+        j0, w = (W1, W2) if last else (0, W1)
+        J = lambda n: R(n, j0, j0 + w)
+        ln = lambda i, e=None: R("LN", 4 * j0 + w * i, 4 * j0 + w * (e or i + 1))
+        lin("ak", R("CK", 3, 5), R("PM"), ak, K)
+        ts("n0", R("L3", 0, w), J("JY"), akp, Op.add, 4.0 / 3.0, Op.mult)
+        ts("n1", ln(0), R("L3", 0, w), 4.0 * LEAF + 1, Op.mult)
+        ts("n2", ln(1), J("JB"), akm, Op.add, 16.0 * LEAF + 4, Op.mult)
+        ts("n3", ln(2), J("JA"), K, Op.add, 16.0 * LEAF + 4, Op.mult)
+        tt("n4", R("MX", 0, 2 * w), ln(0, 2), ln(2, 4), Op.max)
+        tt("n5", R("SH", 0, w), R("MX", 0, w), R("MX", w, 2 * w), Op.max)
+        ts("n6", R("VI", 0, w), R("SH", 0, w), 2, Op.logical_shift_right, 4 * LEAF - 1, Op.bitwise_and)
+        ts("n7", R("VF", 0, w), R("VI", 0, w), 0.5 - 1.5 * LEAF, Op.add)
+        act("n8", R("G1", WS, WS + w), R("VF", 0, w), Fn.Abs)
+        g0 = WS if last else 0
+        g2 = R("G2", g0, WS + w)
+        act("n9", g2, R("G1", g0, WS + w), Fn.Abs, kl, 2.0)
+        if last:
+            ts("lm", LO(0, W2), g2, -0.5, Op.mult, cq, Op.add)
+        else:
+            ts("lm", LO(56, 64), R("G2", 56, 64), -0.5, Op.mult, cq, Op.add)
+            ts("lo", LO(0, 56), R("G2", 0, 56), -0.5, Op.mult, cqb, Op.add)
+        la = lambda h: R("LA", PART[h][0] // 16, PART[h][1] // 16)
+        zt = lambda b, h: R("ZT", 4 * PART[h][0] + b, 4 * PART[h][1], 4)
+        for b in range(4):
+            mm("g%d" % b, 4 + b, 128, "EH" if b in HALVES else "EB", 128 * b, "QX", came)
+            copy("pg%d" % b, PL(b, 320, 432), bank(4 + b, 0, SLOTS), None if b in HALVES else 1.0 / 64.0)
+        for b in range(4):
+            big("f%d" % b, int(b not in HALVES), b, 4 + other.index(b), False)
+        for h in range(2):
+            for b in range(4):
+                if (b, h) in FUSED:
+                    tt("z%d%d" % (h, b), zt(b, h), (PL(b), la(h)), AB(b, *PART[h]), Op.add)
+                else:
+                    copy("y%d%d" % (h, b), AB(b, *PART[h]), (PL(b), la(h)))
+                    tt("z%d%d" % (h, b), zt(b, h), bank(b, *PART[h]), AB(b, *PART[h]), Op.add)
+                if h == 0 and b in HALVES:
+                    big("d%d" % b, 1, b, b, False)
+            quant("qz%d" % h, "QZ", PART[h][0], PART[h][1], R("ZT", 4 * PART[h][0], 4 * PART[h][1]))
+        if last:
+            lin("lf", R("LF", 0, W2), g2, cq, -0.5)
+            call("lt", {"v": lambda e: e.transpose(T.LT[:], T.LF[:])}, [R("LT")], [R("LF")])
+            for i in range(8):
+                store("so%d" % i, T.lo[i:i + 1, :], T.LT[32 * (i // 2):32 * (i // 2) + 20, 16 * (i % 2):16 * (i % 2) + 16], R("LT"))
+        for h, (lo, hi) in enumerate(PART):
+            for b in range(4):
+                mm("w%d%d" % (h, b), result(h, b), hi - lo, "QW", 128 * b, "QZ", lo, False, True)
+                copy("r%d%d" % (h, b), YP(b, lo, hi), bank(result(h, b), 0, hi - lo), 0.03125)
+        if not last:
+            for b in range(4):
+                copy("xm%d" % b, X(80, 208, b), (YP(b), LO(56, 64)))
+
+    stage[0] = "e"
+    for h, (lo, hi) in enumerate(PART):
+        for b in range(4):
+            copy("x%d%d" % (h, b), X(lo, hi, b), (YP(b), LO(lo // 16, hi // 16)))
+        quant("q%d" % h, "QF", lo, hi, X(lo, hi))
+        store("oc%d" % h, T.oc[:, 4 * lo:4 * hi], T.QF[:, lo:hi].bitcast(dt.uint8), R("QF", lo, hi))
+        mm("v%d" % h, 2 + h, hi - lo, "QV", 0, "QF", lo)
+        copy("y%d" % h, R("YO", lo, hi), bank(2 + h, 0, hi - lo))
+        store("sy%d" % h, T.y[:, lo:hi], T.YO[:, lo:hi], R("YO", lo, hi))
+    for i in range(4):
+        store("os%d" % i, T.osc[4 * i:4 * i + 4, :], T.QFs[32 * i:32 * i + 4, :], R("QFs"))
+    return calls
+
+
+def before(calls):
+    uses, deps = {}, {}
+    for name, (forms, outs, ins, kind) in calls.items():
+        deps[name] = {}
+        for rs, writes in ((ins, False), (outs if kind != "far" else [], True)):
+            for r in rs:
+                cols = set(range(*r[1:]))
+                for w2, cols2, other in uses.get(r[0], []):
+                    if (writes or w2) and not cols.isdisjoint(cols2):
+                        deps[name][other] = True
+                    elif r[0] == "PS" and r[1] // 512 == min(cols2) // 512:
+                        deps[name].setdefault(other, False)
+        for rs, writes in ((ins if kind != "far" else [], False), (outs, True)):
+            for r in rs:
+                cols = set(range(*r[1:]))
+                old = uses.get(r[0], [])
+                if writes:
+                    old = [e for e in old if not e[1] <= cols]
+                uses[r[0]] = old + [(writes, cols, name)]
+    return deps
+
+
+def spread(calls, words):
+    order = []
+    for t in "012":
+        for name, q in words:
+            for full in ("c" + name[1:] if name[0] == "." and t == "0" else t + name, "e" + name[1:] if name[0] == "!" and t == "2" else ""):
+                if full in calls:
+                    order.append((full, q))
+    return order
+
+
+def rank_program(g, core, T, topo):
+    if T.rank_of(core) is None:
+        return
+    calls = plan(core, T, topo)
+    order = spread(calls, [word.split(":") for word in ORDER.split()])
+    where = dict(order)
+    deps = before(calls)
+    queue = {"v": g.vector, "a": g.scalar, "t": g.tensor, "g": g, "s": g.sync}
+    total, seen, clock, token, free = {}, {q: {} for q in queue}, {}, {}, list(DMAS)
+
+    def wait(q, tokens):
         need = {}
-        for s, n in deps:
+        for s, n in tokens:
             need[s] = max(need.get(s, 0), n)
         for s, n in sorted(need.items(), key=lambda e: -len(clock.get(e, {}))):
             if seen[q].get(s, 0) < n:
@@ -194,364 +420,17 @@ def rank_program(g, core, T, topo):
                 for s2, n2 in list(clock.get((s, n), {}).items()) + [(s, n)]:
                     seen[q][s2] = max(seen[q].get(s2, 0), n2)
 
-    def issue(name, q):
+    for name, q in order:
         forms, outs, ins, kind = calls[name]
-        deps, who = [], q if kind == "run" else "dma"
-        for rs, writes in ((ins, False), (outs if kind != "far" else [], True)):
-            for r in rs:
-                cols = set(range(*r[1:]))
-                for w2, cols2, q2, tok in uses.get(r[0], []):
-                    if seen[q].get(tok[0], 0) >= tok[1]:
-                        hit = False
-                    elif r[0] == "PS" and q2 != who:
-                        hit = r[1] // 512 == min(cols2) // 512
-                    else:
-                        hit = (writes or w2) and not (who == q2 == "t") and not cols.isdisjoint(cols2)
-                    if hit:
-                        deps.append(tok)
-        wait(q, deps)
+        wait(q, [token[d] for d, sure in deps[name].items() if where[d] != q or sure and q != "t"])
         if kind == "far":
-            tok = forms[q](queue[q])
-            ins = []
+            n, token[name] = forms[q](queue[q])
+            total["sent"] = total.get("sent", 0) + n
+            total[token[name][0]] = token[name][1]
         else:
             sem, n = (q, 1) if kind == "run" else ("out" if kind == "out" else free.pop(0), 16)
             forms[q](queue[q]).then_inc(T.sem[sem], n)
             total[sem] = total.get(sem, 0) + n
-            tok = (sem, total[sem])
-            clock[tok] = dict(seen[q])
-        for rs, writes in ((ins, False), (outs, True)):
-            for r in rs:
-                cols = set(range(*r[1:]))
-                old = uses.get(r[0], [])
-                if writes and r[0] != "PS":
-                    old = [e for e in old if not e[1] <= cols]
-                uses[r[0]] = old + [(writes, cols, who, tok)]
-
-    def load(q, r, src, cast=None, ins=()):
-        call({q: lambda e: e.dma_start(ap(r, cast), src)}, [r], ins, "dma")
-
-    def store(qs, dst, src, r, name):
-        call({q: lambda e: e.dma_start(dst, src) for q in qs}, [], [r], "out", name)
-
-    def ts_form(out, in0, s1, op0, s2=None, op1=None):
-        if op1 is None:
-            return lambda e: e.tensor_scalar(ap(out), ap(in0), ap(s1), None, op0)
-        return lambda e: e.tensor_scalar(ap(out), ap(in0), ap(s1), ap(s2), op0, op1)
-
-    def ts(out, in0, s1, op0, s2=None, op1=None):
-        call({"v": ts_form(out, in0, s1, op0, s2, op1)}, [out], [in0, s1, s2])
-
-    def tt(out, a, b, op):
-        call({"v": lambda e: e.tensor_tensor(ap(out), ap(a), ap(b), op)}, [out], [a, b])
-
-    def act(out, in_, fn, bias=0.0, scale=1.0, accum=None):
-        more = {} if accum is None else {"accum_out": ap(accum)}
-        call({"a": lambda e: e.activation(ap(out), ap(in_), fn, bias=ap(bias), scale=ap(scale), **more)}, [out, accum], [in_, bias, scale])
-
-    def either(q, forms):
-        return {p: forms[p] for p in q + "".join(p for p in forms if p != q)}
-
-    def lin(q, out, in_, bias, scale=1.0):
-        call(either(q, {"v": ts_form(out, in_, scale, Op.mult, bias, Op.add),
-                        "a": lambda e: e.activation(ap(out), ap(in_), Fn.Identity, bias=ap(bias), scale=ap(scale))}), [out], [in_, bias, scale])
-
-    def copy(q, out, in_, scale=None, more=None):
-        if scale is None:
-            forms = {"v": lambda e: e.tensor_copy(ap(out), ap(in_)), "a": lambda e: e.activation(ap(out), ap(in_), Fn.Copy)}
-        else:
-            forms = {"v": ts_form(out, in_, scale, Op.mult), "a": lambda e: e.activation(ap(out), ap(in_), Fn.Copy, scale=scale)}
-        call(either(q, dict(forms, **(more or {}))), [out], [in_])
-
-    def cast(out, in_, as_=None):
-        call({"v": lambda e: e.tensor_copy(ap(out, as_), ap(in_, as_))}, [out], [in_])
-
-    def quant(name, lo, hi, in_):
-        c, s = R(name, lo, hi), R(name + "s", lo, hi)
-        call({"v": lambda e: e.quantize_mx(ap(c), ap(s), ap(in_))}, [c, s], [in_])
-
-    def bank(b, lo, hi):
-        return ("PS", 512 * b + lo, 512 * b + hi, 1)
-
-    def mm(b, n, w, wlo, x, xlo, start=True, stop=True):
-        ins = [R(w, wlo, wlo + 128), R(w + "s", wlo, wlo + 128), R(x, xlo, xlo + n), R(x + "s", xlo, xlo + n)]
-        call({"t": lambda e: e.matmul_mx(ap(bank(b, 0, n)), *[ap(r) for r in ins], start, stop)}, [bank(b, 0, n)], ins, name=w + str(wlo // 128) + x + str(xlo))
-
-    def part(h, b, w, x, start, stop):
-        lo, hi = PART[h]
-        mm(RBANK[h][b], hi - lo, w, 128 * b, x, lo, start, stop)
-
-    def fill(r, value):
-        forms = {"v": lambda e: e.memset(ap(r), value)}
-        if value == int(value) and abs(value) < 256:
-            forms["g"] = lambda e: e.iota(ap(r), [[0, r[2] - r[1]]], int(value), 0, allow_small_or_imprecise_dtypes=True)
-        call(forms, [r], [])
-
-    def iota(r, pattern, base, cm=0):
-        more = {} if SCRATCH[r[0]][2] == I32 else {"allow_small_or_imprecise_dtypes": True}
-        call({"g": lambda e: e.iota(ap(r), pattern, base, cm, **more)}, [r], [])
-
-    def scan(out, scores):
-        zero = R("NIL", 0, out[2] - out[1])
-        call({"v": lambda e: e.tensor_tensor_scan(ap(out), ap(zero), ap(scores), -1e29, Op.add, Op.max)}, [out], [zero, scores])
-
-    X = lambda lo, hi, b=None: R("X", PAD + 4 * lo, PAD + 4 * hi) if b is None else R("X", PAD + 4 * lo + b, PAD + 4 * hi, 4)
-
-    load("a", R("UT"), T.u[:])
-    load("s", X(80, 208), T.x[:, 320:832])
-    load("s", X(208, 320), T.x[:, 832:1280])
-    load("s", X(0, 80), T.x[:, 0:320])
-    load("s", R("QW"), T.wc[:], dt.uint8)
-    load("s", R("QWs"), T.ws[:])
-    load("s", R("VT"), T.v[:])
-
-    iota(col("LI", 0), [[0, 1]], 0, 1)
-    iota(R("PO"), [[1, 2], [16, 8]], 0)
-    fill(R("NUL"), 0.0)
-    iota(R("C4"), [[4, 28]], 0)
-    iota(R("C16"), [[16, 20]], 0)
-    for name, value in (("ED", 0.5), ("EDB", 32.0)):
-        call({"g": lambda e, name=name, value=value: e.affine_select(T[name][:], T.NUL[:], [[-1, 516]], Op.not_equal, value, 3, 4)}, [R(name)], [R("NUL")])
-    JF = lambda lo=0, hi=W1 + W2: R("LN", 3 * W1 + lo, 3 * W1 + hi)
-    iota(JF(0, 8), [[16, 8]], 80)
-    iota(JF(8, 28), [[4, 20]], 0)
-    iota(JF(28, 56), [[4, 28]], 208)
-    iota(R("PM"), [[-2, 2]], 1)
-    fill(R("LF", 20, 32), 0.0)
-    fill(R("NIL"), 0.0)
-    fill(R("RMK", 0, 80), -1e29)
-    ts(col("LI", 1), col("LI", 0), 15, Op.bitwise_and)
-    ts(col("LI", 2), col("LI", 0), 2, Op.logical_shift_right, 3, Op.bitwise_and)
-    ts(col("LI", 3), col("LI", 0), 3, Op.bitwise_and)
-    cast(R("PU"), R("PO"))
-    cast(R("LANE"), R("LI"))
-    lane, l1, lb, lq = col("LANE", 1), col("LANE", 2), col("LANE", 3), col("LANE", 0)
-    fill(R("X", 0, 32), 0.0)
-    fill(R("X", 160, PAD), 0.0)
-    fill(R("BT", 448, 512), 0.0)
-    fill(col("CT", 48), -31.875)
-    fill(col("CT", 49), -192.0)
-    fill(col("CT", 50), 127.5)
-    lin("v", lq, lane, 0.0, 0.25)
-    lin("a", R("W8", 0, 8), R("C4", 20, 28), l1)
-    lin("a", R("W8", 8, 16), R("C4", 0, 8), l1)
-    ts(R("CT", 28, 48), R("C16"), lane, Op.add, -127.5, Op.add)
-    ts(R("CT", 0, 28), R("C4"), lq, Op.add, PAD / 4 + 128, Op.add)
-    lin("a", R("ZQ"), R("C4", 20, 28), lq)
-    lin("a", R("Z2"), R("W8", 0, 8), 63.0, -2.0)
-    lin("a", R("W8", 16, 24), R("W8", 8, 16), 124.0, -4.0)
-    lin("v", R("CT", 28, 48), R("CT", 28, 48), 0.0, -1.0)
-    ts(R("LR"), R("W8", 16, 24), lb, Op.add)
-    cb = col("CK", 15)
-    lin("a", cb, lb, 127.5, 320.0)
-    quant("QU", 0, 128, R("UT"))
-    quant("QS", 0, 128, X(80, 208))
-    for h in range(2):
-        pick = R("PU", 8 * h, 8 * h + 8)
-        cast(R("UU", 128 * h, 128 * h + 128), (R("QU"), pick), dt.uint32)
-        copy("a", R("UUs", 128 * h, 128 * h + 128), (R("QUs"), pick))
-
-    def unit(name, b):
-        quant(name, 128 * b, 128 * b + 128, R({"EH": "ED", "EB": "EDB"}[name], 3 - b, 515 - b))
-
-    def late_constants():
-        lin("a", JF(0, 8), JF(0, 8), lane)
-        lin("a", JF(8, 56), JF(8, 56), l1)
-        lin("a", JF(64, 84), R("C16"), lane)
-        lin("a", JF(56, 64), R("W8", 8, 16), 319.0, -1.0)
-        for b in (2, 1, 3):
-            unit("EH", b)
-        unit("EB", 0)
-        cast(R("JI"), JF())
-        lin("a", R("JY"), JF(), -160.125)
-        lin("a", R("JB"), JF(), -159.375)
-        lin("a", R("JT"), JF(), -160.0, 0.5)
-        unit("EB", 1)
-        ts(R("JI"), R("JI"), 1, Op.bitwise_and)
-        unit("EB", 2)
-        ts(R("JA"), R("JI"), -0.25, Op.mult)
-        unit("EB", 3)
-        tt(R("JA"), R("JA"), R("JT"), Op.add)
-
-    C, K, rr, fj, k2, kh, mn = (col("CK", i) for i in range(7))
-    akp, akm, ak = col("CK", 10), col("CK", 11), col("QK", 20)
-    TN, cm, cp = R("TC", 28, 48), col("TC", 49), col("TC", 50)
-    w8 = lambda i: R("W8", 24 + 8 * i, 32 + 8 * i)
-    wa = lambda i: R("WA", 20 * i, 20 * i + 20)
-    PL = lambda b, lo=0, hi=432: R("PL", 432 * b + lo, 432 * b + hi)
-    YP = lambda b, lo=0, hi=320: R("YP", 320 * b + lo, 320 * b + hi)
-    AB = lambda b, lo, hi: R("AB", 320 * b + lo, 320 * b + hi)
-    FP = lambda b, lo, hi: R("FP", 320 * b + lo, 320 * b + hi)
-    LO = lambda lo, hi: R("LO", lo, hi)
-    engines = topo.engines(core, prev)[:8]
-    mask = sum(1 << e for e in engines)
-    rid, pid = topo.addr(prev)[:2]
-
-    def send(t):
-        def form(e):
-            for name, as_ in (("", dt.uint8), ("s", None)):
-                e.remote_dma(ap(R("G%d%s" % (t, name), 0, 112), as_), ap(R("B%d%s" % (t, name), 0, 112), as_), T.sem["arr%d" % t], T.sem.sent, pid, rid, mask)
-                total["sent"] = total.get("sent", 0) + len(engines)
-            total["arr%d" % t] = 2 * len(topo.engines(nxt, core)[:8])
-            return ("arr%d" % t, total["arr%d" % t])
-        call({"g": form}, [R("G%d" % t, 0, 112), R("G%ds" % t, 0, 112)], [R("B%d" % t), R("B%ds" % t)], "far")
-
-    def twin(b, n):
-        out, in_ = FP(b, 0, n), PL(b, 0, n)
-        copy("g", out, in_, more={"g": lambda e: e.affine_select(ap(out), ap(in_), [[0, n]], Op.is_ge, 0.0, 0, 0)})
-
-    for t in range(3):
-        last = t == 2
-        stage[0] = str(t)
-        if t:
-            quant("QS", 0, 128, X(80, 208))
-        mm(6, 128, "UU", 0, "QS", 0)
-        mm(7, 128, "UU", 128, "QS", 0)
-        if t == 0:
-            copy("a", R("X", 32, 160), (X(288, 320), R("LR")))
-        else:
-            copy("a", R("X", 32, 160), (R("YP"), LO(56, 64)))
-            copy("v", X(0, 32), (R("YP"), LO(8, 16)))
-            copy("a", X(32, 80), (R("YP"), LO(16, 28)))
-        scan(R("RMC"), bank(6, 48, 113))
-        scan(R("RMK", 80, 105), bank(7, 0, 25))
-        act(R("SGC"), R("RMC"), Fn.Sign, col("RMC", 64), -1.0, C)
-        act(R("SGK"), R("RMK"), Fn.Sign, col("RMK", 104), -1.0, K)
-        ts(rr, C, 32.0, Op.min, -2.0, Op.mult)
-        ts(fj, C, 32.0, Op.is_lt, -88.0, Op.mult)
-        lin("v", R("TC"), R("CT"), C)
-        act(R("QK"), R("CT", 28, 49), Fn.Abs, C)
-        ts(w8(1), R("Z2"), rr, Op.add, fj, Op.add)
-        ts(w8(0), R("ZQ"), K, Op.is_ge)
-        ts(R("L1"), R("TC", 0, 20), K, Op.subtract, 4.0, Op.mult)
-        tt(w8(2), w8(0), w8(1), Op.mult)
-        copy("a", R("BT", 0, 320), (R("X", 0, WIN), R("L1")))
-        lin("v", R("CK", 10, 12), R("PM"), ak, K)
-        tt(w8(3), w8(2), R("TC", 20, 28), Op.add)
-        lin("v", k2, K, 0.0, 2.0)
-        ts(R("L2"), w8(3), K, Op.subtract, 4.0, Op.mult)
-        ts(mn, C, 128.0, Op.add, k2, Op.min)
-        copy("v", R("BT", 320, 448), (R("X", 0, WIN), R("L2")))
-        B, G = "B%d" % t, "G%d" % t
-        quant(B, 0, 128, R("BT"))
-        send(t)
-        if t == 0:
-            for i in range(3):
-                for name, as_ in (("", dt.uint8), ("s", None)):
-                    src = R("B0" + name, 112, 128)
-                    load("s", R("G%d%s" % (i, name), 112, 128), ap(src, as_), as_, [src])
-            late_constants()
-        else:
-            copy("a", X(208, 264), (R("YP"), LO(28, 42)))
-            copy("a", X(264, 320), (R("YP"), LO(42, 56)))
-
-        j0, w, at = (W1, W2, (1, 3, 2)) if last else (0, W1, (0, 1, 2))
-        J = lambda n: R(n, j0, j0 + w)
-        ln = lambda i, e=None: R("LN", 4 * j0 + w * i, 4 * j0 + w * (e or i + 1))
-        wo = lambda i: R("WO", 64 * i, 64 * i + w)
-        quant("QX", 0, 192, X(0, 192))
-        mm(0, 192, "EB", 0, "QX", 0)
-        act(wa(0), TN, Fn.Abs, K, -2.0)
-        act(wa(1), wa(0), Fn.Abs, k2, -1.0)
-        act(wa(2), R("QK", 0, 20), Fn.Abs, K, -1.0)
-        lin("a", kh, K, 0.5, -1.0)
-        lin("a", wa(3), wa(2), cm, -1.0)
-        ts(ln(at[0]), J("JY"), akp, Op.add, 4.0 / 3.0, Op.mult)
-        ts(ln(at[1]), J("JB"), akm, Op.add, 4.0, Op.mult)
-        ts(ln(at[2]), J("JA"), K, Op.add, 4.0, Op.mult)
-        quant("QX", 192, 320, X(192, 320))
-        mm(4, 128, "EB", 0, "QX", 192)
-        for b in (2, 1, 3):
-            mm(b, 320, "EH", 128 * b, "QX", 0)
-        tt(R("MX", 0, 2 * w), ln(0, 2), ln(2, 4), Op.max)
-        ts(wa(4), wa(1), K, Op.is_lt, k2, Op.mult)
-        tt(R("SH", 0, w), R("MX", 0, w), R("MX", w, 2 * w), Op.max)
-        tt(wa(5), wa(4), TN, Op.add)
-        ts(R("BB", w, 2 * w), R("SH", 0, w), 1, Op.logical_shift_right, 1, Op.bitwise_and)
-        copy("a", PL(0, 0, 192), bank(0, 0, 192), 1.0 / 64.0)
-        copy("a", PL(0, 192, 320), bank(4, 0, 128), 1.0 / 64.0)
-        twin(0, 320)
-        act(wa(6), wa(5), Fn.Sign, cm)
-        for b in (2, 1, 3):
-            copy("a", PL(b, 0, 320), bank(b, 0, 320))
-        twin(1, 192)
-        ts(R("BB", 0, w), R("SH", 0, w), 1, Op.bitwise_and)
-        ts(R("SH", w, 2 * w), R("SH", 0, w), 2, Op.logical_shift_right)
-        tt(wa(7), wa(5), wa(6), Op.mult)
-        ts(wo(0), R("BB", w, 2 * w), k2, Op.mult, kh, Op.add)
-        ts(wa(8), wa(7), mn, Op.subtract, -BIG, Op.mult)
-        ts(wo(1), R("BB", 0, w), -2.0, Op.mult, 1.0, Op.add)
-        tt(wa(9), wa(8), wa(3), Op.max)
-        tt(wo(2), wo(0), R("SH", w, 2 * w), Op.add)
-        tt(wa(10), wa(9), wa(7), Op.min)
-        tt(wo(3), wo(2), wo(1), Op.mult)
-        ts(R("LA"), wa(10), -1.0, Op.mult, cp, Op.add)
-        la = lambda h: R("LA", PART[h][0] // 16, PART[h][1] // 16)
-        zt = lambda b, h: R("ZT", 4 * PART[h][0] + b, 4 * PART[h][1], 4)
-        fused = lambda b, h: tt(zt(b, h), (PL(b), la(h)), FP(b, *PART[h]), Op.add)
-        gather = lambda b, h: copy("a", AB(b, *PART[h]), (PL(b), la(h)))
-        add = lambda b, h: tt(zt(b, h), bank(b, *PART[h]), AB(b, *PART[h]), Op.add)
-        part(0, 0, "EB", "QX", True, False)
-        for b in (0, 2, 1, 3):
-            mm(GBANK[b], 128, "EH" if b else "EB", 128 * b, G, 0)
-        part(1, 1, "EB", "QX", True, False)
-        for b in (0, 2, 1, 3):
-            copy("vvaa"[b], PL(b, 320, 432), bank(GBANK[b], 0, 112), None if b else 1.0 / 64.0)
-        fused(0, 0)
-        gather(2, 0)
-        gather(3, 0)
-        for h, b in ((1, 0), (0, 1), (0, 2), (0, 3)):
-            part(h, b, "EB", "QX", True, False)
-        add(2, 0)
-        part(1, 2, "EB", "QX", True, False)
-        fused(1, 0)
-        add(3, 0)
-        part(1, 3, "EB", "QX", True, False)
-        for b in (1, 2, 3):
-            gather(b, 1)
-        if last:
-            ts(LO(0, 20), wo(3), C, Op.add, 127.5, Op.add)
-        else:
-            ts(LO(0, 8), R("WO", 192, 200), C, Op.add, 127.5, Op.add)
-        quant("QZ", 0, 192, R("ZT", 0, 768))
-        for b in range(4):
-            part(0, b, "QW", "QZ", False, True)
-        fused(0, 1)
-        for b in (1, 2, 3):
-            add(b, 1)
-        if not last:
-            ts(LO(8, 64), R("WO", 200, 256), C, Op.add, cb, Op.add)
-        quant("QZ", 192, 320, R("ZT", 768, 1280))
-        for b in range(4):
-            part(1, b, "QW", "QZ", False, True)
-        if t == 0:
-            quant("QV", 0, 128, R("VT"))
-        if last:
-            lin("a", R("LF", 0, 20), wo(3), cp)
-            call({"v": lambda e: e.transpose(T.LT[:], T.LF[:])}, [R("LT")], [R("LF")])
-            for i in range(8):
-                store("s", T.lo[i:i + 1, :], T.LT[32 * (i // 2):32 * (i // 2) + 20, 16 * (i % 2):16 * (i % 2) + 16], R("LT"), "lo%d" % i)
-        for b in range(4):
-            copy("a", YP(b, 0, 192), bank(RBANK[0][b], 0, 192), 0.03125)
-        for b in range(4):
-            copy("vaav"[b], YP(b, 192, 320), bank(RBANK[1][b], 0, 128), 0.03125)
-        for b in range(4):
-            if last:
-                copy("vaav"[b], X(0, 192, b), (YP(b), LO(0, 12)))
-            else:
-                copy("vaav"[b], X(80, 208, b), (YP(b), LO(0, 8)))
-
-    stage[0] = "e"
-    for b in range(4):
-        copy("vaav"[b], X(192, 320, b), (YP(b), LO(12, 20)))
-    for h, (lo, hi) in enumerate(PART):
-        quant("QF", lo, hi, X(lo, hi))
-        store("sa", T.oc[:, 4 * lo:4 * hi], T.QF[:, lo:hi].bitcast(dt.uint8), R("QF", lo, hi), "oc%d" % h)
-        mm(2 + h, hi - lo, "QV", 0, "QF", lo)
-        copy("av"[h], R("YO", lo, hi), bank(2 + h, 0, hi - lo))
-        store("as", T.y[:, lo:hi], T.YO[:, lo:hi], R("YO", lo, hi), "y%d" % h)
-    for i in range(4):
-        store("sa", T.osc[4 * i:4 * i + 4, :], T.QFs[32 * i:32 * i + 4, :], R("QFs"), "osc%d" % i)
-
-    for name, q in [e.split(":") for e in ORDER.split()] or [(name, list(c[0])[0]) for name, c in calls.items()]:
-        issue(name, q)
+            token[name] = (sem, total[sem])
+            clock[token[name]] = dict(seen[q])
     wait("g", list(total.items()))

@@ -1,49 +1,47 @@
 from concourse.mybir import AluOpType as Op, ActivationFunctionType as Fn, dt
 
-PAD = 384
+PAD = 880
 XW = PAD + 1280
 WIN = PAD + 768
 PART = ((0, 192), (192, 320))
+RUNS = ((0, 112, 208), (192, 320, 80), (112, 192, 0))
+ZPART = ((48, 192, 4), (192, 320, 14), (0, 48, 0))
+NA = 22
 SLOTS = 112
-GQ = 3 * SLOTS
+GQ = 3 * SLOTS + 16
 W1, W2, WS = 44, 20, 20
-HALVES = (1, 2, 3)
-FUSED = ((0, 0), (1, 0), (0, 1))
-BIG = 4096.0
+FUSED = ((0, 0), (1, 0), (0, 1), (0, 2), (1, 2))
+LAST = ((0, 0, 320), (1, 0, 320), (2, 0, 192), (3, 0, 192), (2, 192, 320), (3, 192, 256), (3, 256, 320))
+BIG = 8192.0
 LEAF = 512
 
 F8, U8, BF, F32, I32, U16 = "float8_e4m3fn_x4", "uint8", "bfloat16", "float32", "int32", "uint16"
 SCRATCH = {"PS": ("psum", [128, 4096], F32)}
 for _n, _w in (("X", XW), ("UT", 512), ("VT", 512), ("BT", 512), ("ZT", 1280), ("PL", 1728), ("AB", 1280), ("YP", 1280),
-               ("ED", 516), ("EDB", 516), ("NUL", 516)):
+               ("ED", 516), ("EDB", 516)):
     SCRATCH[_n] = ("sbuf", [128, _w], BF)
-for _n, _w in (("QU", 128), ("UU", 256), ("QV", 128), ("QW", 512), ("EH", 512), ("EB", 512), ("QS", 128), ("QX", GQ + 320), ("QZ", 320),
+for _n, _w in (("QU", 128), ("UU", 256), ("QV", 128), ("QW", 512), ("EH", 512), ("EB", 512), ("QX", GQ + 320), ("QZ", 320),
                ("QF", 320), ("B0", 128), ("B1", 128), ("B2", 128)):
     SCRATCH[_n] = ("sbuf", [128, _w], F8)
     SCRATCH[_n + "s"] = ("sbuf", [128, _w], U8)
-for _n, _w in (("RUN", 28), ("LANE", 16), ("CT", 54), ("TC", 54), ("ZQ", 8), ("ZN", 8), ("ZR", 8), ("PM", 2), ("K0", 2), ("NIL", 65),
-               ("J", 64), ("JY", 64), ("JB", 64), ("JA", 64), ("LN", 4 * W1 + 4 * W2), ("MX", 2 * W1), ("VF", W1), ("G1", WS + W1),
-               ("G2", WS + W1), ("LF", 32), ("LT", 32), ("YO", 320), ("RMC", 65), ("RMK", 25), ("SGC", 65), ("SGK", 25), ("CK", 8),
-               ("W8", 32), ("WA", 240)):
+for _n, _w in (("RUN", 28), ("LANE", 3), ("M", 28), ("N4", 8), ("CT", 49 + NA), ("TC", 49 + NA), ("ZR", 28), ("PM", 2), ("K0", 2),
+               ("J", W1 + W2), ("JY", W1 + W2), ("JB", W1 + W2), ("JA", W1 + W2), ("LN", 4 * W1 + 4 * W2), ("MX", 2 * W1), ("VF", W1),
+               ("G1", WS + W1), ("G2", WS + W1), ("LF", 32), ("LT", 32), ("YO", 320), ("RMC", 65), ("RMK", 25), ("SGC", 65), ("SGK", 25),
+               ("CK", 7), ("BD", 24), ("BR", 24), ("WA", 5 * NA), ("AD", 4 * NA), ("AE", 4 * NA), ("AR", 4 * NA)):
     SCRATCH[_n] = ("sbuf", [128, _w], F32)
-for _n, _w in (("LI", 6), ("PO", 16), ("L3", W1), ("SH", W1), ("VI", W1)):
+for _n, _w in (("LI", 4), ("PO", 16), ("JI", W1 + W2), ("L3", W1), ("SH", W1), ("VI", W1)):
     SCRATCH[_n] = ("sbuf", [128, _w], I32)
-for _n, _w in (("PU", 16), ("LR", 8), ("L1", 20), ("L2", 8), ("LA", 20), ("LO", WS + W1)):
+for _n, _w in (("PU", 16), ("LR", 8), ("L1", 20), ("L2", 8), ("LA", NA), ("LO", WS + W1)):
     SCRATCH[_n] = ("sbuf", [128, _w], U16)
 DMAS = ["d%d" % i for i in range(8)]
 SEMAPHORES = ["v", "a", "t", "g", "out", "arr0", "arr1", "arr2", "sent"] + DMAS
 ORDER = """
-.u:a .xm:s .xh:s .xl:s .w:s .ws:s .v:s .p:g .nil:v .x1:v .nul:v .x0:v .i2:v .i3:v .i1:v .i4:v .lane:v xl1:a .run:g .o3:a .po:g .ct5:a .o2:a .op0:v .k0:a .ct6:a .ct4:a .zr:v .ct2:v .bt:v .o1:a xh1:a .pu:v .edb:g .o4:v .o0:v .qu:v .uc1:v .uc0:v .ct0:a qs:v .us0:a .us1:a .ed:g .ct3:v .o8:v .j2:v sc:t .zn:a sk:t .zq:a xl0:v .ct1:a .ct7:a .pm:v mc:v c:a mk:v k:a .lr:v tc:a fj:v xt:a b0:v a0:a b1:v b2:v l1:v b3:v k2:v l2:v a1:v bm:a bt:v a3:v qb:v qx0:v a4:v xh0:a .j1:v a2:a .eb0:v .op2:v e00:t .j0:a qx1:v .jf0:v ak:a .eb1:v .jy:v e01:t a7:a .qv:v send:g .op1:a .ja0:v p00:a .jb:a n0:v .eh2:v .ja1:v a5:v .eh3:v n2:v a6:a n3:v e10:t t00:g h2:t p01:a e11:t .ja2:v .eb2:v p10:a h3:t n1:v g2:t t01:g n4:v a8:v p2:a g0:t n5:v a9:v p11:v aa:v g1:t .eb3:v t11:g p3:a n6:v pg0:a ab:v g3:t n7:v pg2:v pg3:a la:v o0:t f1:t f2:t pg1:v y02:a z00:v y03:a z01:v z02:v y13:a f3:t z03:v t10:g y12:a n8:a .gs:a n9:a z11:v d2:t f0:t d3:t qz0:v o1:t lf:a w03:t w00:t w02:t z10:v r03:a w01:t z12:v z13:v lt:v qz1:v so6:s w10:t r00:a lo:v r02:a r01:v w11:t w12:t r11:a w13:t r10:v r12:v so0:s !x10:a so3:s r13:a !x00:v so2:s so4:s !x01:v !x12:a !x03:a !x02:v so5:s !x11:a !x13:a !q0:v .jf1:v so1:s so7:s !q1:v xm0:a !v0:t .lf:v !oc0:s !v1:t !y0:v !oc1:a !os0:s !os1:s !y1:v !os3:s !os2:s xm1:v !sy0:a !sy1:a
+.u:a .xm:s .xh:s .xl:s .w:s .ws:s .v:s .x0:v .p:g .p4:g xh1:a .run:g .ct4:a .i1:v .lane:v .m:a .po:g .pu:v .bd:v .qu:v .ct6:a .n4:v .uc0:v .ctb:a .ct5:g qs:v .ct3:a .us0:a .uc1:v xl0:v .us1:a .ct7:a .ct8:v sc:t .k0:g .ct0:v sk:t xt1:a mc:v .ct2:v .ed:g xt3:g mk:v .ctc:a xt0:v .ct1:a .pm:g c:a xt2:g qx0:v k:a tc:a b1:a a0:a .ad:g qx1:v b0:v k2:v ak:a l1:v b2:v .eh2:v .bt:g a1:a l2:v bm:a bn:v bu:a bt:v a3:v .j2:a qb:v .zr:v send:g .eh0:v .j3:a h0:t .j0:a .o8:a .eh1:v .jf0:a .eh3:v .jb:a a4:v .ja0:a .jy:v p00:a .edb:v .ji:v n0:v .eb0:v h1:t h3:t .ja1:v a5:v n2:v h2:t d0:t p01:a t10:v .eb1:v g2:t n3:v a6:a a2:a t00:v a8:v n1:v p02:a t01:v a7:a .gs:a a9:v n4:v ab:v g1:t .eb2:v n5:v p03:a p13:a p12:a la:v g3:t y23:a .qv:v n6:v .eb3:v z20:v t11:g g0:t y22:a n7:v z23:v pg2:a pg1:a pg3:a f2:t d1:t .lf:g f3:t f1:t y02:a z21:v z22:v pg0:v y03:a z01:v n8:a y12:a y13:a f0:t z00:v z02:v z03:v y11:a z10:v d2:t qz0:v z12:v d3:t w03:t z13:v z11:v n9:a .jf1:a lm:v w02:t qz1:v w01:t w00:t r03:a lf:a r02:v w10:t lt:v r00:v r20:v so5:s r23:a so4:s w11:t w12:t r01:a lo:v w13:t r21:a so0:s r11:v r22:a r10:a r12:a so1:s r13:v xm1:v !x1:a xm0:a so2:s !x0:v xm3:v !x3:a !x5:a !x4:a so7:a so3:s !x2:v !x6:v !q0:v !oc0:a !q1:v !oc1:a !os1:a so6:s !os0:s !os2:a !v0:t xm2:a !v1:t !y0:v !os3:a !sy0:s !y1:v !sy1:s
 """
 
 
 ORDER = """
-.u:a .xm:s .xh:s .xl:s .w:s .ws:s .v:s .p:g .x0:v .nil:v .bt:v .nul:v .i2:v .i3:v xh1:a .run:g .ct4:a .i1:v .x1:v .i4:v .po:g .k0:a .pu:v .lane:v .qu:v .o0:a .ct7:a .j2:a .o1:v .uc0:v .o2:a .o3:a .edb:g .us0:a qs:v .us1:a .pm:a .uc1:v .ct0:a .ct1:v xl0:v sc:t xl1:v .ed:g .zr:v .ct2:a .ct5:a .eb1:v mc:v sk:t .zn:a .lr:v mk:v qx0:v xh0:a .zq:a qx1:v .ct6:a .ct3:a c:a fj:v k:a b0:v .o4:a k2:v tc:a xt:a b1:v b2:v l1:v a1:a e01:t b3:v a0:a .j1:a a3:v l2:v bm:a .j0:v a4:v bt:v p01:a ak:a a5:v a2:a qb:v .jy:v .eb0:v e00:t e11:t .jb:v send:g .op2:v a6:a .eh2:v p00:a .eb2:v n0:v p11:v .eh3:v .op0:a n2:v .eb3:v h2:t .o8:v e10:t p10:a .ja0:a .ja2:v h3:t a8:v t01:g .op1:a .jf0:a n1:v p2:a .ja1:a n3:v g0:t a7:v t00:v a9:v n4:v g1:t p3:a .qv:v aa:v .gs:a n5:v t10:g t11:g g2:t ab:v pg2:a n6:v g3:t pg3:a la:v y02:a n7:v o1:t pg0:v y03:a f2:t y13:a o0:t pg1:v z00:v z01:v z11:v f3:t z02:v f1:t z03:v f0:t d2:t d3:t z10:v y12:a n8:a qz0:v w00:t z12:v z13:v n9:a w02:t lo:v lf:a qz1:v lt:v r02:a w01:t w03:t so5:a r00:v w10:t w11:t r01:v r10:v so4:s w12:t r03:a r12:v so3:s !x00:v .lf:v r11:a !x02:v so6:s w13:t r13:a !x01:a !x10:v .jf1:a so0:s !x03:a !x11:a !q0:v so7:s so1:s !x12:a !x13:v !q1:v !v0:t xm1:v !v1:t !y0:v !oc0:s !y1:v so2:a !os0:a !oc1:s !os1:a !sy0:s xm0:a !os3:s !os2:a !sy1:s
-"""
-
-
-ORDER = """
-.u:a .xm:s .xh:s .xl:s .w:s .ws:s .v:s xh1:a xl1:v .x0:v .p:g .nul:v .i2:v .i3:v .po:g .run:g .nil:v .x1:v .i1:v .i4:v .ct7:v .ct5:a .lane:v .j3:a .pu:v .o3:a .zr:a .k0:v .ed:g .qu:v xh0:a .ct2:a .bt:v .o2:v .uc0:v .us0:a qs:v sc:t .o1:a .uc1:v .ct1:v .us1:a .j1:a .ct3:v xl0:v .zq:a .lr:v .ct6:v .o0:a .o4:a sk:t .op1:a mc:v .ct0:v .ct4:a mk:v qx0:v qx1:v .j2:a c:a .pm:a k:a fj:v tc:a .zn:a xt:a b0:v a0:a k2:v l1:v .edb:g b1:v b2:v .eh1:v a1:a h1:t b3:v a3:v ak:v bm:a l2:v bu:a a4:v bt:v .j0:a .jf0:a a5:v a2:a .o8:v .jb:a qb:v a6:a .ja1:a .eb0:v e10:t e00:t .eh2:v .op2:a .lf:v .jy:v .eb3:v .eh3:v h3:t n2:v h2:t .op0:a p00:a .qv:v send:g .ja0:a o0:t p10:a g2:t n0:v .ja2:v a8:v .eb1:v n3:v g0:t n1:v a9:v .eb2:v g1:t n4:v a7:a t00:v aa:v g3:t n5:v ab:v p1:a p2:a n6:v .gs:a p3:a d1:t pg2:a pg3:a t10:v la:v t01:v n7:v pg0:v pg1:v z00:v z01:v y02:a f0:t z02:v y03:a y11:a f2:t y12:a f1:t f3:t d2:t z03:v z10:v qz0:v z11:v d3:t y13:a z12:v n8:a n9:a z13:v lf:v w00:t qz1:v r00:a lm:v w03:t w01:t lo:v w02:t w10:t r01:a lt:v so7:s so4:s so6:s so1:s w11:t w12:t r02:v so3:a r03:a r10:v r11:a w13:t r13:a !x01:a r12:v !x03:a xm1:a !x11:a so5:s xm3:a !x00:v !x02:v so2:s !x10:v so0:s !q0:v !x13:v !x12:a xm0:v !v0:t !oc0:a xm2:v !q1:v !y0:v !v1:t !os0:a !y1:v !oc1:s !os2:a !os1:a !os3:s !sy0:s .jf1:a !sy1:s
+.u:a .xm:s .xh:s .xl:s .w:s .ws:s .v:s .p:g .p4:g .x0:v .i1:v .lane:v .run:g .po:g .pu:v .qu:v .ae:v .ct4:a .m:a .ct6:a .n4:v .uc0:v .ctc:a .us0:a qs:v .ed:g .uc1:v .us1:a .ct5:g .lr:v .ct8:a xl0:v xl1:v .eh1:v .ct0:a xh1:a .k0:g sc:t .ctb:v sk:t .bd:g .ct3:a .ct1:v .ct2:a mc:v .ct7:a xt:a c:a .ad:g .eh2:v mk:v k:a .j3:a qx0:v tc:a .pm:g .bt:g a0:a .zr:v qx1:v b1:v b0:v .j1:a .edb:g .j0:v k2:v ak:a l1:v b2:v a2:a a1:v k3:v bm:a l2:v bn:v bt:v .eh0:v a3:v bu:a .j2:a qb:v .eb3:v .eh3:v .o8:a .jf0:a .jy:v h2:t .jb:a h0:t p02:a .gs:a h1:t .lf:v .ja0:v send:g p12:a .ji:v a4:v n0:v a7:v p00:a .eb0:v .ja1:v a5:v n1:v p01:a n2:v n3:v aa:v .eb2:v a9:v h3:t p10:a a8:v a6:a d0:t n4:v p03:a t00:g p11:a p13:a ab:v .jf1:a t01:v n5:v t11:a la:v .eb1:v g2:t n6:v y23:a y22:v t10:g g1:t z20:v g3:t z21:v n7:v z22:v pg2:a z23:v g0:t d1:t pg1:a pg0:v pg3:a y02:a z01:v f1:t f2:t z00:v y03:a f3:t z02:v z03:v f0:t y11:a y12:a d2:t d3:t z10:v y13:a n8:a qz0:v z11:v z12:v z13:v n9:a .qv:v w03:t w00:t qz1:v r03:a lm:v lf:v lo:v r00:v w01:t w02:t r01:a r20:v w10:t r02:v w11:t lt:v r23:a so5:s r21:a r22:v r10:a w12:t so1:s r12:a r11:v !x1:a w13:t r13:v xm0:a so7:s xm2:a !x0:v !x3:a so6:s !x5:a !x4:a so3:s !x2:v !x6:v !q0:v xm1:v !v0:t !oc0:s !q1:v so2:s !os0:a so0:s !v1:t so4:s !os3:a !os2:a !os1:s !y0:v !oc1:s !y1:v !sy0:a !sy1:s xm3:v
 """
 
 
@@ -63,7 +61,7 @@ def plan(core, T, topo):
             return r
         if len(r) == 2:
             return ap(r[0], cast).indirect(ap(r[1]))
-        view = T[r[0]][:, r[1]:r[2]:r[3]] if r[3] > 1 else T[r[0]][:, r[1]:r[2]]
+        view = T[r[0]][:, r[1]:r[2]:r[3]] if r[3] != 1 else T[r[0]][:, r[1]:r[2]]
         return view.bitcast(cast) if cast is not None else view
 
     def pieces(rs):
@@ -109,8 +107,8 @@ def plan(core, T, topo):
         call(name, forms, [out], [in_])
 
     def twin(name, out, in_):
-        call(name, {"g": lambda e: e.affine_select(ap(out), ap(in_), [[0, out[2] - out[1]]], Op.is_ge, 0.0, 0, 0),
-                    "v": lambda e: e.tensor_copy(ap(out), ap(in_))}, [out], [in_])
+        call(name, {"g": lambda e: e.affine_select(ap(out), ap(in_), [[0, len(range(*out[1:]))]], Op.is_ge, 0.0, 0, 0),
+                    "v": lambda e: e.tensor_copy(ap(out), ap(in_)), "a": lambda e: e.activation(ap(out), ap(in_), Fn.Copy)}, [out], [in_])
 
     def cast(name, out, in_, as_=None):
         call(name, {"v": lambda e: e.tensor_copy(ap(out, as_), ap(in_, as_))}, [out], [in_])
@@ -127,18 +125,21 @@ def plan(core, T, topo):
         call(name, {"t": lambda e: e.matmul_mx(ap(bank(b, 0, n)), *[ap(r) for r in ins], start, stop)}, [bank(b, 0, n)], ins)
 
     def fill(name, r, value):
-        call(name, {"v": lambda e: e.memset(ap(r), value)}, [r], [])
+        call(name, {"v": lambda e: e.memset(ap(r), value),
+                    "g": lambda e: e.iota(ap(r), [[0, r[2] - r[1]]], int(value), 0, allow_small_or_imprecise_dtypes=True)}, [r], [])
 
     def iota(name, r, pattern, base, cm=0):
         more = {} if SCRATCH[r[0]][2] == I32 else {"allow_small_or_imprecise_dtypes": True}
         call(name, {"g": lambda e: e.iota(ap(r), pattern, base, cm, **more)}, [r], [])
 
     def scan(name, out, scores):
-        zero = R("NIL", 0, out[2] - out[1])
+        zero = R("X", 0, out[2] - out[1])
         call(name, {"v": lambda e: e.tensor_tensor_scan(ap(out), ap(zero), ap(scores), -1e29, Op.add, Op.max)}, [out], [zero, scores])
 
+    def chain(name, out, up, down):
+        call(name, {"v": lambda e: e.tensor_tensor_scan(ap(out), ap(up), ap(down), 0.0, Op.max, Op.min)}, [out], [up, down])
+
     X = lambda lo, hi, b=None: R("X", PAD + 4 * lo, PAD + 4 * hi) if b is None else R("X", PAD + 4 * lo + b, PAD + 4 * hi, 4)
-    HEAD = R("X", 32, 160)
 
     load("u", R("UT"), T.u[:])
     load("xm", X(80, 208), T.x[:, 320:832])
@@ -149,45 +150,33 @@ def plan(core, T, topo):
     load("v", R("VT"), T.v[:])
 
     iota("p", col("LI", 0), [[0, 1]], 0, 1)
-    iota("run", R("RUN"), [[1, 28]], 0)
+    iota("p4", col("LI", 1), [[0, 1]], 0, 4)
+    iota("run", R("RUN"), [[4, 28]], 0)
     iota("po", R("PO"), [[1, 2], [16, 8]], 0)
-    fill("nul", R("NUL"), 0.0)
-    for name, value in (("EDB", 32.0), ("ED", 0.5)):
-        call(name.lower(), {"g": lambda e, name=name, value=value: e.affine_select(T[name][:], T.NUL[:], [[-1, 516]], Op.not_equal, value, 3, 4)},
-             [R(name)], [R("NUL")])
-    run = lambda n, lo=0: R("RUN", lo, lo + n)
-
-    def const(name, r, value):
-        lin(name, r, run(r[2] - r[1]), value, 0.0)
-
-    ts("i1", col("LI", 1), col("LI", 0), 15, Op.bitwise_and)
-    ts("i2", col("LI", 2), col("LI", 0), 2, Op.logical_shift_right, 3, Op.bitwise_and)
-    ts("i3", col("LI", 3), col("LI", 0), 3, Op.bitwise_and)
-    ts("i4", R("LI", 4, 6), R("LI", 2, 4), 1, Op.bitwise_and)
-    cast("lane", R("LANE", 0, 6), R("LI"))
+    fill("x0", R("X", 0, PAD), 0.0)
+    call("ed", {"g": lambda e: e.affine_select(T.ED[:], T.X[:, 0:516], [[-1, 516]], Op.not_equal, 0.5, 3, 4)}, [R("ED")], [R("X", 0, 516)])
+    call("edb", {"g": lambda e: e.affine_select(T.EDB[:], T.X[:, 0:516], [[-1, 516]], Op.not_equal, 32.0, 3, 4)}, [R("EDB")], [R("X", 0, 516)])
+    ts("i1", R("LI", 2, 4), R("LI", 0, 2), 15, Op.bitwise_and)
+    ts("lane", R("LANE", 0, 2), R("LI", 2, 4), 0.25, Op.mult)
     cast("pu", R("PU"), R("PO"))
-    lane, l1, lb, par1, par = (col("LANE", i) for i in range(1, 6))
-    own = lambda i: col("LANE", 6 + i)
-    fill("x0", R("X", 0, 32), 0.0)
-    fill("x1", R("X", 160, PAD), 0.0)
+    lq, lb, l4 = col("LANE", 0), col("LANE", 1), col("ZR", 0)
+    M = lambda lo, hi: R("M", lo, hi)
+    lin("m", R("M"), R("RUN"), lq)
+    ts("n4", R("N4"), M(0, 8), 2.0, Op.mult, lb, Op.subtract)
     fill("bt", R("BT", 4 * SLOTS, 512), 0.0)
-    fill("nil", R("NIL"), 0.0)
-    lin("o0", own(0), lane, PAD / 4 + 48.0, 0.25)
-    lin("ct0", R("CT", 0, 28), run(28), own(0), 4.0)
-    lin("o1", own(1), lane, 127.5, -1.0)
-    lin("ct1", R("CT", 28, 48), run(20), own(1), -16.0)
-    const("ct2", col("CT", 48), -31.875)
-    const("ct3", col("CT", 49), -192.0)
-    const("ct4", col("CT", 50), 127.5)
-    const("ct5", col("CT", 51), 127.5 + LEAF / 2)
-    lin("ct6", col("CT", 52), lb, 127.5 + LEAF / 2, 320.0)
-    const("ct7", col("CT", 53), 128.0)
-    lin("zr", R("ZR"), run(8), l1, 4.0)
-    lin("zq", R("ZQ"), R("ZR"), 0.5)
-    lin("o2", own(2), lb, PAD / 4 - 1.125, 0.25)
-    lin("zn", R("ZN"), R("ZR"), own(2), -1.0)
-    lin("o3", own(3), lb, 124.0)
-    ts("lr", R("LR"), R("ZR"), -4.0, Op.mult, own(3), Op.add)
+    fill("bd", R("BD"), BIG)
+    fill("ad", R("AD"), BIG)
+    fill("ae", R("AE"), BIG)
+    ts("lr", R("LR"), R("N4"), -2.0, Op.mult, 124.0, Op.add)
+    lin("ct0", R("CT", 0, 20), M(0, 20), PAD / 4 + 48.0)
+    lin("ct1", R("CT", 20, 44, 3), R("N4"), -163.0, 0.5)
+    lin("ct2", R("CT", 21, 44, 3), R("N4"), PAD / 4 - 33.0, -0.5)
+    lin("ct3", R("CT", 22, 44, 3), M(20, 28), PAD / 4 + 48.0)
+    lin("ct4", R("CT", 44, 46), R("RUN", 0, 2), -31.875, (159.375 + LEAF / 2) / 4)
+    iota("ct5", R("CT", 46, 48), [[320, 2]], -192)
+    lin("ct6", col("CT", 48), lb, 127.5 + LEAF / 2, 320.0)
+    for name, at, lo, hi in (("ct7", 0, 13, 17), ("ct8", 4, 16, 20), ("ctb", 8, 0, 6), ("ctc", 14, 5, 13)):
+        lin(name, R("CT", 49 + at, 49 + at + hi - lo), M(lo, hi), 127.5, -4.0)
     quant("qu", "QU", 0, 128, R("UT"))
     for h in range(2):
         pick = R("PU", 8 * h, 8 * h + 8)
@@ -195,152 +184,146 @@ def plan(core, T, topo):
         copy("us%d" % h, R("UUs", 128 * h, 128 * h + 128), (R("QUs"), pick))
     for b in range(4):
         quant("eb%d" % b, "EB", 128 * b, 128 * b + 128, R("EDB", 3 - b, 515 - b))
-    for b in HALVES:
         quant("eh%d" % b, "EH", 128 * b, 128 * b + 128, R("ED", 3 - b, 515 - b))
-    lin("pm", R("PM"), run(2), 1.0, -2.0)
-    lin("k0", R("K0"), run(2), 80.0, -float(LEAF))
-    lin("o4", own(4), l1, 208.0)
-    lin("j0", R("J", 0, 28), run(28), own(4), 4.0)
-    lin("j1", R("J", 28, 36), R("ZR"), 319.0, -1.0)
-    lin("j2", R("J", 44, 64), run(20), lane, 16.0)
-    lin("j3", R("J", 36, 44), run(8, 5), lane, 16.0)
+    iota("pm", R("PM"), [[-2, 2]], 1)
+    iota("k0", R("K0"), [[-LEAF, 2]], 80)
+    ts("zr", R("ZR"), R("M"), 4.0, Op.mult, lb, Op.subtract)
+    lin("j0", R("J", 0, 28), R("ZR"), 208.0, 0.25)
+    lin("j1", R("J", 28, 36), R("ZR", 0, 8), 319.0, -0.25)
+    lin("j2", R("J", 36, 44), M(5, 13), 0.0, 4.0)
+    lin("j3", R("J", 44, 64), M(0, 20), 0.0, 4.0)
     lin("jy", R("JY"), R("J"), -80.125)
     lin("jb", R("JB"), R("J"), -239.375)
-    for i, (lo, hi, odd, base, step) in enumerate(((0, 28, par1, -80.0, -0.25), (28, 36, par1, -80.25, 0.25), (36, 64, par, -80.0, -0.25))):
-        lin("op%d" % i, own(5 + i), odd, base, step)
-        lin("ja%d" % i, R("JA", lo, hi), R("J", lo, hi), own(5 + i), 0.5)
+    ts("ji", R("JI"), R("J"), 0.5, Op.mult, -0.25, Op.add)
+    lin("ja0", R("JA"), R("J"), -320.0, 0.5)
+    tt("ja1", R("JA"), R("JA"), R("JI"), Op.add)
     lin("jf0", R("LN", 3 * W1, 4 * W1), R("J", 0, W1), 0.0, 4.0 * LEAF + 1)
     lin("jf1", R("LN", 4 * W1 + 3 * W2, 4 * W1 + 4 * W2), R("J", W1, W1 + W2), 0.0, 4.0 * LEAF + 1)
-    lin("o8", own(8), l1, 0.5 - 1.5 * LEAF, float(LEAF))
-    act("gs", R("G1", 0, WS), run(WS), Fn.Abs, own(8))
+    lin("o8", col("LANE", 2), l4, 0.5 - 1.5 * LEAF, LEAF / 4)
+    act("gs", R("G1", 0, WS), R("RUN", 0, WS), Fn.Abs, col("LANE", 2), 0.25)
     fill("lf", R("LF", W2, 32), 0.0)
     quant("qv", "QV", 0, 128, R("VT"))
 
-    C, K, fj, akp, akm, k2, kl = (col("CK", i) for i in range(7))
-    ak, right, cp, cq, cqb, left = (col("TC", 48 + i) for i in range(6))
-    w8 = lambda i: R("W8", 8 * i, 8 * i + 8)
-    wa = lambda i: R("WA", 20 * i, 20 * i + 20)
+    C, K, akp, akm, k2, kl, most = (col("CK", i) for i in range(7))
+    ak, cq, right, left, cqb = (col("TC", 44 + i) for i in range(5))
+    wa = lambda i: R("WA", NA * i, NA * i + NA)
+    nth = lambda name, i, n: R(name, i, None, n)
     PL = lambda b, lo=0, hi=432: R("PL", 432 * b + lo, 432 * b + hi)
     YP = lambda b, lo=0, hi=320: R("YP", 320 * b + lo, 320 * b + hi)
     AB = lambda b, lo, hi: R("AB", 320 * b + lo, 320 * b + hi)
     LO = lambda lo, hi: R("LO", lo, hi)
-    other = list(HALVES) + [b for b in range(4) if b not in HALVES]
-    result = lambda h, b: b if (b in HALVES) == (h == 1) else 4 + other.index(b)
-    engines = topo.engines(core, prev)
-    mask = sum(1 << e for e in engines)
+    result = lambda h, b: b if h else 4 + b
     rid, pid = topo.addr(prev)[:2]
 
     def send(t):
-        lo = GQ - SLOTS * (t + 1)
+        lo = SLOTS * (2 - t)
 
         def form(e):
             for name, as_ in (("", dt.uint8), ("s", None)):
-                e.remote_dma(ap(R("QX" + name, lo, lo + SLOTS), as_), ap(R("B%d%s" % (t, name), 0, SLOTS), as_), T.sem["arr%d" % t], T.sem.sent, pid, rid, mask)
-            return 2 * len(engines), ("arr%d" % t, 2 * len(topo.engines(nxt, core)))
+                e.remote_dma(ap(R("QX" + name, lo, lo + SLOTS), as_), ap(R("B%d%s" % (t, name), 0, SLOTS), as_), T.sem["arr%d" % t], T.sem.sent,
+                             pid, rid, topo.mask(core, prev))
+            return 2 * len(topo.engines(core, prev)), ("arr%d" % t, 2 * len(topo.engines(nxt, core)))
         call("send", {"g": form}, [R("QX", lo, lo + SLOTS), R("QXs", lo, lo + SLOTS)], [R("B%d" % t), R("B%ds" % t)], "far")
         return lo
 
-    def big(name, h, b, to, stop):
+    def start(name, h, b):
         lo, hi = PART[h]
-        mm(name, to, hi - lo, "EB", 128 * b, "QX", GQ + lo, True, stop)
+        mm(name, result(h, b), hi - lo, "EB", 128 * b, "QX", GQ + lo, True, False)
+
+    def contacts(h, b):
+        lo, hi, at = ZPART[h]
+        found, out = (PL(b, 0, 320 if h == 2 else 432), R("LA", at, at + (hi - lo) // 16)), R("ZT", 4 * lo + b, 4 * hi, 4)
+        if (b, h) in FUSED:
+            tt("z%d%d" % (h, b), out, found, AB(b, lo, hi), Op.add)
+        else:
+            copy("y%d%d" % (h, b), AB(b, lo, hi), found)
+            tt("z%d%d" % (h, b), out, bank(b, lo, hi), AB(b, lo, hi), Op.add)
 
     for t in range(3):
         last = t == 2
         stage[0] = str(t)
-        quant("qs", "QS", 0, 128, X(80, 208))
-        mm("sc", 6, 128, "UU", 0, "QS", 0)
-        mm("sk", 7, 128, "UU", 128, "QS", 0)
-        if t == 0:
-            copy("xt", HEAD, (X(288, 320), R("LR")))
-        else:
-            copy("xt", HEAD, (R("YP"), LO(48, 56)))
+        quant("qs", "QX", GQ + 192, GQ + 320, X(80, 208))
+        mm("sc", 6, 128, "UU", 0, "QX", GQ + 192)
+        mm("sk", 7, 128, "UU", 128, "QX", GQ + 192)
+        if t:
             copy("xl0", X(0, 40), (R("YP"), LO(0, 10)))
             copy("xl1", X(40, 80), (R("YP"), LO(10, 20)))
+            copy("xh1", X(208, 320), (R("YP"), LO(20, 48)))
+        copy("xt", R("X", 528, 656), (R("YP"), LO(48, 56)) if t else (X(288, 320), R("LR")))
         scan("mc", R("RMC"), bank(6, 48, 113))
         scan("mk", R("RMK"), bank(7, 0, 25))
         act("c", R("SGC"), R("RMC"), Fn.Sign, col("RMC", 64), -1.0, C)
         act("k", R("SGK"), R("RMK"), Fn.Sign, col("RMK", 24), -1.0, K)
         act("tc", R("TC"), R("CT"), Fn.Abs, C)
-        ts("fj", fj, C, 32.0, Op.is_lt, 8.25 - PAD / 4, Op.mult)
-        ts("b0", w8(0), R("ZQ"), K, Op.subtract, -BIG, Op.mult)
-        ts("b1", w8(1), R("ZN"), ak, Op.add, fj, Op.add)
+        lin("b1", nth("BD", 1, 3), nth("BD", 0, 3), 0.0, col("SGC", 31))
+        ts("b0", nth("BD", 2, 3), M(0, 8), K, Op.subtract, -BIG, Op.mult)
         ts("l1", R("L1"), R("TC", 0, 20), K, Op.subtract, 4.0, Op.mult)
-        tt("b2", w8(2), w8(0), R("TC", 20, 28), Op.min)
-        tt("b3", w8(3), w8(2), w8(1), Op.max)
-        ts("l2", R("L2"), w8(3), K, Op.subtract, 4.0, Op.mult)
-        copy("bm", R("BT", 0, 320), (R("X", 0, WIN), R("L1")))
+        chain("b2", R("BR"), R("BD"), R("TC", 20, 44))
+        ts("l2", R("L2"), nth("BR", 2, 3), K, Op.subtract, 4.0, Op.mult)
+        copy("bm", R("BT", 0, 192), (R("X", 0, WIN), R("L1", 0, 12)))
+        copy("bn", R("BT", 192, 320), (R("X", 0, WIN), R("L1", 12, 20)))
         copy("bt", R("BT", 320, 384), (R("X", 0, WIN), R("L2", 0, 4)))
         copy("bu", R("BT", 384, 448), (R("X", 0, WIN), R("L2", 4, 8)))
         quant("qb", "B%d" % t, 0, 128, R("BT"))
         came = send(t)
-        if t:
-            copy("xh0", X(208, 264), (R("YP"), LO(20, 34)))
-            copy("xh1", X(264, 320), (R("YP"), LO(34, 48)))
-        for h, (lo, hi) in enumerate(PART):
-            quant("qx%d" % h, "QX", GQ + lo, GQ + hi, X(lo, hi))
+        quant("qx0", "QX", GQ + 112, GQ + 240, X(0, 128))
+        quant("qx1", "QX", GQ - 16, GQ + 112, X(192, 320))
         for b in range(4):
-            if b in HALVES:
-                mm("h%d" % b, b, 320, "EH", 128 * b, "QX", GQ)
-                copy("p%d" % b, PL(b, 0, 320), bank(b, 0, 320))
-            else:
-                for h in range(2):
-                    big("e%d%d" % (h, b), h, b, result(h, b), True)
-                    copy("p%d%d" % (h, b), PL(b, *PART[h]), bank(result(h, b), 0, PART[h][1] - PART[h][0]), 1.0 / 64.0)
-                big("o%d" % b, 0, b, b, False)
-        for b, h in FUSED:
-            twin("t%d%d" % (h, b), AB(b, *PART[h]), PL(b, *PART[h]))
-        ts("k2", R("CK", 5, 7), R("K0"), K, Op.add, 2.0, Op.mult)
-        lin("a0", wa(0), R("CT", 28, 48), C)
-        lin("a1", wa(1), R("TC", 28, 48), k2, -2.0)
-        act("a2", wa(2), R("TC", 28, 48), Fn.Abs, k2, -2.0)
+            mm("h%d" % b, b, 320, "EH", 128 * b, "QX", GQ)
+            copy("p0%d" % b, PL(b, 208, 320), bank(b, 0, 112))
+            copy("p1%d" % b, PL(b, 0, 208), bank(b, 112, 320))
+            if (b, 0) in FUSED:
+                twin("t0%d" % b, AB(b, 0, 112), PL(b, 208, 320))
+                twin("t1%d" % b, AB(b, 112, 320 if (b, 1) in FUSED else 192), PL(b, 0, 208 if (b, 1) in FUSED else 80))
+        ts("k2", R("CK", 4, 6), R("K0"), K, Op.add, 2.0, Op.mult)
+        lin("a0", wa(0), R("CT", 49), C)
+        lin("a1", wa(1), R("TC", 49), k2, -2.0)
         tt("a3", wa(3), wa(0), wa(1), Op.mult)
         ts("a4", wa(4), wa(3), 0.0, Op.is_lt, k2, Op.mult)
-        tt("a5", wa(5), wa(4), wa(0), Op.add)
-        act("a6", wa(6), wa(5), Fn.Sign, right, -1.0)
-        lin("a7", wa(7), wa(2), right, 0.5)
-        tt("a8", wa(8), wa(5), wa(6), Op.mult)
-        ts("a9", wa(9), wa(8), left, Op.add, -BIG, Op.mult)
-        tt("aa", wa(10), wa(9), wa(7), Op.min)
-        tt("ab", wa(11), wa(10), wa(8), Op.max)
-        ts("la", R("LA"), wa(11), cp, Op.add)
+        act("a2", wa(2), R("TC", 49), Fn.Abs, k2, -2.0)
+        lin("k3", most, ak, 160.0)
+        mate = nth("AE", 1, 4)
+        tt("a5", mate, wa(4), wa(0), Op.add)
+        lin("a6", nth("AE", 0, 4), mate, 0.0, -1.0)
+        lin("a7", nth("AE", 3, 4), wa(2), right, 0.5)
+        ts("a8", nth("AD", 1, 4), mate, right, Op.subtract, -BIG, Op.mult)
+        ts("a9", nth("AD", 2, 4), mate, left, Op.add, -BIG, Op.mult)
+        ts("aa", nth("AD", 3, 4), mate, most, Op.subtract, BIG, Op.mult)
+        chain("ab", R("AR"), R("AD"), R("AE"))
+        ts("la", R("LA"), nth("AR", 3, 4), left, Op.add, -0.5, Op.add)
         j0, w = (W1, W2) if last else (0, W1)
         J = lambda n: R(n, j0, j0 + w)
         ln = lambda i, e=None: R("LN", 4 * j0 + w * i, 4 * j0 + w * (e or i + 1))
-        lin("ak", R("CK", 3, 5), R("PM"), ak, K)
+        lin("ak", R("CK", 2, 4), R("PM"), ak, K)
         ts("n0", R("L3", 0, w), J("JY"), akp, Op.add, 4.0 / 3.0, Op.mult)
         ts("n1", ln(0), R("L3", 0, w), 4.0 * LEAF + 1, Op.mult)
         ts("n2", ln(1), J("JB"), akm, Op.add, 16.0 * LEAF + 4, Op.mult)
-        ts("n3", ln(2), J("JA"), K, Op.add, 16.0 * LEAF + 4, Op.mult)
+        ts("n3", ln(2), J("JA"), k2, Op.add, 8.0 * LEAF + 2, Op.mult)
         tt("n4", R("MX", 0, 2 * w), ln(0, 2), ln(2, 4), Op.max)
         tt("n5", R("SH", 0, w), R("MX", 0, w), R("MX", w, 2 * w), Op.max)
         ts("n6", R("VI", 0, w), R("SH", 0, w), 2, Op.logical_shift_right, 4 * LEAF - 1, Op.bitwise_and)
         ts("n7", R("VF", 0, w), R("VI", 0, w), 0.5 - 1.5 * LEAF, Op.add)
         act("n8", R("G1", WS, WS + w), R("VF", 0, w), Fn.Abs)
-        g0 = WS if last else 0
-        g2 = R("G2", g0, WS + w)
-        act("n9", g2, R("G1", g0, WS + w), Fn.Abs, kl, 2.0)
+        g2 = R("G2", WS if last else 0, WS + w)
+        act("n9", g2, R("G1", WS if last else 0, WS + w), Fn.Abs, kl, 2.0)
         if last:
             ts("lm", LO(0, W2), g2, -0.5, Op.mult, cq, Op.add)
         else:
             ts("lm", LO(56, 64), R("G2", 56, 64), -0.5, Op.mult, cq, Op.add)
             ts("lo", LO(0, 56), R("G2", 0, 56), -0.5, Op.mult, cqb, Op.add)
-        la = lambda h: R("LA", PART[h][0] // 16, PART[h][1] // 16)
-        zt = lambda b, h: R("ZT", 4 * PART[h][0] + b, 4 * PART[h][1], 4)
         for b in range(4):
-            mm("g%d" % b, 4 + b, 128, "EH" if b in HALVES else "EB", 128 * b, "QX", came)
-            copy("pg%d" % b, PL(b, 320, 432), bank(4 + b, 0, SLOTS), None if b in HALVES else 1.0 / 64.0)
+            contacts(2, b)
         for b in range(4):
-            big("f%d" % b, int(b not in HALVES), b, 4 + other.index(b), False)
-        for h in range(2):
+            mm("g%d" % b, 4 + b, 128, "EH", 128 * b, "QX", came)
+            copy("pg%d" % b, PL(b, 320, 432), bank(4 + b, 0, SLOTS))
+        for b in range(4):
+            start("f%d" % b, 0, b)
+        for h, (lo, hi) in enumerate(PART):
             for b in range(4):
-                if (b, h) in FUSED:
-                    tt("z%d%d" % (h, b), zt(b, h), (PL(b), la(h)), AB(b, *PART[h]), Op.add)
-                else:
-                    copy("y%d%d" % (h, b), AB(b, *PART[h]), (PL(b), la(h)))
-                    tt("z%d%d" % (h, b), zt(b, h), bank(b, *PART[h]), AB(b, *PART[h]), Op.add)
-                if h == 0 and b in HALVES:
-                    big("d%d" % b, 1, b, b, False)
-            quant("qz%d" % h, "QZ", PART[h][0], PART[h][1], R("ZT", 4 * PART[h][0], 4 * PART[h][1]))
+                contacts(h, b)
+                if h == 0:
+                    start("d%d" % b, 1, b)
+            quant("qz%d" % h, "QZ", lo, hi, R("ZT", 4 * lo, 4 * hi))
         if last:
             lin("lf", R("LF", 0, W2), g2, cq, -0.5)
             call("lt", {"v": lambda e: e.transpose(T.LT[:], T.LF[:])}, [R("LT")], [R("LF")])
@@ -349,15 +332,17 @@ def plan(core, T, topo):
         for h, (lo, hi) in enumerate(PART):
             for b in range(4):
                 mm("w%d%d" % (h, b), result(h, b), hi - lo, "QW", 128 * b, "QZ", lo, False, True)
-                copy("r%d%d" % (h, b), YP(b, lo, hi), bank(result(h, b), 0, hi - lo), 0.03125)
+                for i, (first, end, place) in enumerate(RUNS):
+                    if lo <= first < hi:
+                        copy("r%d%d" % (i, b), YP(b, place, place + end - first), bank(result(h, b), first - lo, end - lo), 0.03125)
         if not last:
             for b in range(4):
                 copy("xm%d" % b, X(80, 208, b), (YP(b), LO(56, 64)))
 
     stage[0] = "e"
+    for i, (b, lo, hi) in enumerate(LAST):
+        copy("x%d" % i, X(lo, hi, b), (YP(b), LO(lo // 16, hi // 16)))
     for h, (lo, hi) in enumerate(PART):
-        for b in range(4):
-            copy("x%d%d" % (h, b), X(lo, hi, b), (YP(b), LO(lo // 16, hi // 16)))
         quant("q%d" % h, "QF", lo, hi, X(lo, hi))
         store("oc%d" % h, T.oc[:, 4 * lo:4 * hi], T.QF[:, lo:hi].bitcast(dt.uint8), R("QF", lo, hi))
         mm("v%d" % h, 2 + h, hi - lo, "QV", 0, "QF", lo)

from concourse.mybir import AluOpType as Op, ActivationFunctionType as Fn, dt

PAD = 880
XW = PAD + 1280
WIN = PAD + 768
PART = ((0, 192), (192, 320))
RUNS = ((0, 112, 208), (192, 320, 80), (112, 192, 0))
ZPART = ((48, 192, 4), (192, 320, 14), (0, 48, 0))
NA = 22
SLOTS = 112
GQ = 3 * SLOTS + 16
W1, W2, WS = 44, 20, 20
FUSED = ((0, 0), (1, 0), (0, 1), (0, 2), (1, 2))
LAST = ((0, 0, 320), (1, 0, 320), (2, 0, 192), (3, 0, 192), (2, 192, 320), (3, 192, 256), (3, 256, 320))
BIG = 8192.0
LEAF = 512

F8, U8, BF, F32, I32, U16 = "float8_e4m3fn_x4", "uint8", "bfloat16", "float32", "int32", "uint16"
SCRATCH = {"PS": ("psum", [128, 4096], F32)}
for _n, _w in (("X", XW), ("UT", 512), ("VT", 512), ("BT", 512), ("ZT", 1280), ("PL", 1728), ("AB", 1280), ("YP", 1280),
               ("ED", 516), ("EDB", 516)):
    SCRATCH[_n] = ("sbuf", [128, _w], BF)
for _n, _w in (("QU", 128), ("UU", 256), ("QV", 128), ("QW", 512), ("EH", 512), ("EB", 512), ("QX", GQ + 320), ("QZ", 320),
               ("QF", 320), ("B0", 128), ("B1", 128), ("B2", 128)):
    SCRATCH[_n] = ("sbuf", [128, _w], F8)
    SCRATCH[_n + "s"] = ("sbuf", [128, _w], U8)
for _n, _w in (("RUN", 28), ("LANE", 3), ("M", 28), ("N4", 8), ("CT", 49 + NA), ("TC", 49 + NA), ("ZR", 28), ("PM", 2), ("K0", 2),
               ("J", W1 + W2), ("JY", W1 + W2), ("JB", W1 + W2), ("JA", W1 + W2), ("LN", 4 * W1 + 4 * W2), ("MX", 2 * W1), ("VF", W1),
               ("G1", WS + W1), ("G2", WS + W1), ("LF", 32), ("LT", 32), ("YO", 320), ("RMC", 65), ("RMK", 25), ("SGC", 65), ("SGK", 25),
               ("CK", 7), ("BD", 24), ("BR", 24), ("WA", 5 * NA), ("AD", 4 * NA), ("AE", 4 * NA), ("AR", 4 * NA)):
    SCRATCH[_n] = ("sbuf", [128, _w], F32)
for _n, _w in (("LI", 4), ("PO", 16), ("JI", W1 + W2), ("L3", W1), ("SH", W1), ("VI", W1)):
    SCRATCH[_n] = ("sbuf", [128, _w], I32)
for _n, _w in (("PU", 16), ("LR", 8), ("L1", 20), ("L2", 8), ("LA", NA), ("LO", WS + W1)):
    SCRATCH[_n] = ("sbuf", [128, _w], U16)
DMAS = ["d%d" % i for i in range(8)]
SEMAPHORES = ["v", "a", "t", "g", "out", "arr0", "arr1", "arr2", "sent"] + DMAS
ORDER = """
.u:a .xm:s .xh:s .xl:s .w:s .ws:s .v:s .x0:v .p:g .p4:g xh1:a .run:g .ct4:a .i1:v .lane:v .m:a .po:g .pu:v .bd:v .qu:v .ct6:a .n4:v .uc0:v .ctb:a .ct5:g qs:v .ct3:a .us0:a .uc1:v xl0:v .us1:a .ct7:a .ct8:v sc:t .k0:g .ct0:v sk:t xt1:a mc:v .ct2:v .ed:g xt3:g mk:v .ctc:a xt0:v .ct1:a .pm:g c:a xt2:g qx0:v k:a tc:a b1:a a0:a .ad:g qx1:v b0:v k2:v ak:a l1:v b2:v .eh2:v .bt:g a1:a l2:v bm:a bn:v bu:a bt:v a3:v .j2:a qb:v .zr:v send:g .eh0:v .j3:a h0:t .j0:a .o8:a .eh1:v .jf0:a .eh3:v .jb:a a4:v .ja0:a .jy:v p00:a .edb:v .ji:v n0:v .eb0:v h1:t h3:t .ja1:v a5:v n2:v h2:t d0:t p01:a t10:v .eb1:v g2:t n3:v a6:a a2:a t00:v a8:v n1:v p02:a t01:v a7:a .gs:a a9:v n4:v ab:v g1:t .eb2:v n5:v p03:a p13:a p12:a la:v g3:t y23:a .qv:v n6:v .eb3:v z20:v t11:g g0:t y22:a n7:v z23:v pg2:a pg1:a pg3:a f2:t d1:t .lf:g f3:t f1:t y02:a z21:v z22:v pg0:v y03:a z01:v n8:a y12:a y13:a f0:t z00:v z02:v z03:v y11:a z10:v d2:t qz0:v z12:v d3:t w03:t z13:v z11:v n9:a .jf1:a lm:v w02:t qz1:v w01:t w00:t r03:a lf:a r02:v w10:t lt:v r00:v r20:v so5:s r23:a so4:s w11:t w12:t r01:a lo:v w13:t r21:a so0:s r11:v r22:a r10:a r12:a so1:s r13:v xm1:v !x1:a xm0:a so2:s !x0:v xm3:v !x3:a !x5:a !x4:a so7:a so3:s !x2:v !x6:v !q0:v !oc0:a !q1:v !oc1:a !os1:a so6:s !os0:s !os2:a !v0:t xm2:a !v1:t !y0:v !os3:a !sy0:s !y1:v !sy1:s
"""


ORDER = """
.u:a .xm:s .xh:s .xl:s .w:s .ws:s .v:s .p:g .p4:g .x0:v .i1:v .lane:v .run:g .po:g .pu:v .qu:v .ae:v .ct4:a .m:a .ct6:a .n4:v .uc0:v .ctc:a .us0:a qs:v .ed:g .uc1:v .us1:a .ct5:g .lr:v .ct8:a xl0:v xl1:v .eh1:v .ct0:a xh1:a .k0:g sc:t .ctb:v sk:t .bd:g .ct3:a .ct1:v .ct2:a mc:v .ct7:a xt:a c:a .ad:g .eh2:v mk:v k:a .j3:a qx0:v tc:a .pm:g .bt:g a0:a .zr:v qx1:v b1:v b0:v .j1:a .edb:g .j0:v k2:v ak:a l1:v b2:v a2:a a1:v k3:v bm:a l2:v bn:v bt:v .eh0:v a3:v bu:a .j2:a qb:v .eb3:v .eh3:v .o8:a .jf0:a .jy:v h2:t .jb:a h0:t p02:a .gs:a h1:t .lf:v .ja0:v send:g p12:a .ji:v a4:v n0:v a7:v p00:a .eb0:v .ja1:v a5:v n1:v p01:a n2:v n3:v aa:v .eb2:v a9:v h3:t p10:a a8:v a6:a d0:t n4:v p03:a t00:g p11:a p13:a ab:v .jf1:a t01:v n5:v t11:a la:v .eb1:v g2:t n6:v y23:a y22:v t10:g g1:t z20:v g3:t z21:v n7:v z22:v pg2:a z23:v g0:t d1:t pg1:a pg0:v pg3:a y02:a z01:v f1:t f2:t z00:v y03:a f3:t z02:v z03:v f0:t y11:a y12:a d2:t d3:t z10:v y13:a n8:a qz0:v z11:v z12:v z13:v n9:a .qv:v w03:t w00:t qz1:v r03:a lm:v lf:v lo:v r00:v w01:t w02:t r01:a r20:v w10:t r02:v w11:t lt:v r23:a so5:s r21:a r22:v r10:a w12:t so1:s r12:a r11:v !x1:a w13:t r13:v xm0:a so7:s xm2:a !x0:v !x3:a so6:s !x5:a !x4:a so3:s !x2:v !x6:v !q0:v xm1:v !v0:t !oc0:s !q1:v so2:s !os0:a so0:s !v1:t so4:s !os3:a !os2:a !os1:s !y0:v !oc1:s !y1:v !sy0:a !sy1:s xm3:v
"""


def plan(core, T, topo):
    rank, N = T.rank_of(core), len(T.cores)
    prev, nxt = T.cores[(rank - 1) % N], T.cores[(rank + 1) % N]
    calls, stage = {}, ["c"]

    def R(name, lo=0, hi=None, step=1):
        return (name, lo, SCRATCH[name][1][1] if hi is None else hi, step)

    def col(name, i):
        return (name, i, i + 1, 1)

    def ap(r, cast=None):
        if not isinstance(r, tuple):
            return r
        if len(r) == 2:
            return ap(r[0], cast).indirect(ap(r[1]))
        view = T[r[0]][:, r[1]:r[2]:r[3]] if r[3] != 1 else T[r[0]][:, r[1]:r[2]]
        return view.bitcast(cast) if cast is not None else view

    def pieces(rs):
        out = []
        for r in rs:
            if isinstance(r, tuple):
                out += list(r) if len(r) == 2 else [r]
        return out

    def call(name, forms, outs, ins, kind="run"):
        calls[stage[0] + name] = (forms, pieces(outs), pieces(ins), kind)

    def load(name, r, src, cast=None):
        call(name, {q: lambda e: e.dma_start(ap(r, cast), src) for q in "sa"}, [r], [], "dma")

    def store(name, dst, src, r):
        call(name, {q: lambda e: e.dma_start(dst, src) for q in "sa"}, [], [r], "out")

    def ts_form(out, in0, s1, op0, s2=None, op1=None):
        if op1 is None:
            return lambda e: e.tensor_scalar(ap(out), ap(in0), ap(s1), None, op0)
        return lambda e: e.tensor_scalar(ap(out), ap(in0), ap(s1), ap(s2), op0, op1)

    def ts(name, out, in0, s1, op0, s2=None, op1=None):
        call(name, {"v": ts_form(out, in0, s1, op0, s2, op1)}, [out], [in0, s1, s2])

    def tt(name, out, a, b, op):
        call(name, {"v": lambda e: e.tensor_tensor(ap(out), ap(a), ap(b), op)}, [out], [a, b])

    def act(name, out, in_, fn, bias=0.0, scale=1.0, accum=None):
        more = {} if accum is None else {"accum_out": ap(accum)}
        call(name, {"a": lambda e: e.activation(ap(out), ap(in_), fn, bias=ap(bias), scale=ap(scale), **more)}, [out, accum], [in_, bias, scale])

    def lin(name, out, in_, bias, scale=1.0):
        call(name, {"a": lambda e: e.activation(ap(out), ap(in_), Fn.Identity, bias=ap(bias), scale=ap(scale)),
                    "v": ts_form(out, in_, scale, Op.mult, bias, Op.add)}, [out], [in_, bias, scale])

    def copy(name, out, in_, scale=None):
        if scale is None:
            forms = {"a": lambda e: e.activation(ap(out), ap(in_), Fn.Copy), "v": lambda e: e.tensor_copy(ap(out), ap(in_))}
        else:
            forms = {"a": lambda e: e.activation(ap(out), ap(in_), Fn.Copy, scale=scale), "v": ts_form(out, in_, scale, Op.mult)}
        call(name, forms, [out], [in_])

    def twin(name, out, in_):
        call(name, {"g": lambda e: e.affine_select(ap(out), ap(in_), [[0, len(range(*out[1:]))]], Op.is_ge, 0.0, 0, 0),
                    "v": lambda e: e.tensor_copy(ap(out), ap(in_)), "a": lambda e: e.activation(ap(out), ap(in_), Fn.Copy)}, [out], [in_])

    def cast(name, out, in_, as_=None):
        call(name, {"v": lambda e: e.tensor_copy(ap(out, as_), ap(in_, as_))}, [out], [in_])

    def quant(name, q, lo, hi, in_):
        c, s = R(q, lo, hi), R(q + "s", lo, hi)
        call(name, {"v": lambda e: e.quantize_mx(ap(c), ap(s), ap(in_))}, [c, s], [in_])

    def bank(b, lo, hi):
        return ("PS", 512 * b + lo, 512 * b + hi, 1)

    def mm(name, b, n, w, wlo, x, xlo, start=True, stop=True):
        ins = [R(w, wlo, wlo + 128), R(w + "s", wlo, wlo + 128), R(x, xlo, xlo + n), R(x + "s", xlo, xlo + n)]
        call(name, {"t": lambda e: e.matmul_mx(ap(bank(b, 0, n)), *[ap(r) for r in ins], start, stop)}, [bank(b, 0, n)], ins)

    def fill(name, r, value):
        call(name, {"v": lambda e: e.memset(ap(r), value),
                    "g": lambda e: e.iota(ap(r), [[0, r[2] - r[1]]], int(value), 0, allow_small_or_imprecise_dtypes=True)}, [r], [])

    def iota(name, r, pattern, base, cm=0):
        more = {} if SCRATCH[r[0]][2] == I32 else {"allow_small_or_imprecise_dtypes": True}
        call(name, {"g": lambda e: e.iota(ap(r), pattern, base, cm, **more)}, [r], [])

    def scan(name, out, scores):
        zero = R("X", 0, out[2] - out[1])
        call(name, {"v": lambda e: e.tensor_tensor_scan(ap(out), ap(zero), ap(scores), -1e29, Op.add, Op.max)}, [out], [zero, scores])

    def chain(name, out, up, down):
        call(name, {"v": lambda e: e.tensor_tensor_scan(ap(out), ap(up), ap(down), 0.0, Op.max, Op.min)}, [out], [up, down])

    X = lambda lo, hi, b=None: R("X", PAD + 4 * lo, PAD + 4 * hi) if b is None else R("X", PAD + 4 * lo + b, PAD + 4 * hi, 4)

    load("u", R("UT"), T.u[:])
    load("xm", X(80, 208), T.x[:, 320:832])
    load("xh", X(208, 320), T.x[:, 832:1280])
    load("xl", X(0, 80), T.x[:, 0:320])
    load("w", R("QW"), T.wc[:], dt.uint8)
    load("ws", R("QWs"), T.ws[:])
    load("v", R("VT"), T.v[:])

    iota("p", col("LI", 0), [[0, 1]], 0, 1)
    iota("p4", col("LI", 1), [[0, 1]], 0, 4)
    iota("run", R("RUN"), [[4, 28]], 0)
    iota("po", R("PO"), [[1, 2], [16, 8]], 0)
    fill("x0", R("X", 0, PAD), 0.0)
    call("ed", {"g": lambda e: e.affine_select(T.ED[:], T.X[:, 0:516], [[-1, 516]], Op.not_equal, 0.5, 3, 4)}, [R("ED")], [R("X", 0, 516)])
    call("edb", {"g": lambda e: e.affine_select(T.EDB[:], T.X[:, 0:516], [[-1, 516]], Op.not_equal, 32.0, 3, 4)}, [R("EDB")], [R("X", 0, 516)])
    ts("i1", R("LI", 2, 4), R("LI", 0, 2), 15, Op.bitwise_and)
    ts("lane", R("LANE", 0, 2), R("LI", 2, 4), 0.25, Op.mult)
    cast("pu", R("PU"), R("PO"))
    lq, lb, l4 = col("LANE", 0), col("LANE", 1), col("ZR", 0)
    M = lambda lo, hi: R("M", lo, hi)
    lin("m", R("M"), R("RUN"), lq)
    ts("n4", R("N4"), M(0, 8), 2.0, Op.mult, lb, Op.subtract)
    fill("bt", R("BT", 4 * SLOTS, 512), 0.0)
    fill("bd", R("BD"), BIG)
    fill("ad", R("AD"), BIG)
    fill("ae", R("AE"), BIG)
    ts("lr", R("LR"), R("N4"), -2.0, Op.mult, 124.0, Op.add)
    lin("ct0", R("CT", 0, 20), M(0, 20), PAD / 4 + 48.0)
    lin("ct1", R("CT", 20, 44, 3), R("N4"), -163.0, 0.5)
    lin("ct2", R("CT", 21, 44, 3), R("N4"), PAD / 4 - 33.0, -0.5)
    lin("ct3", R("CT", 22, 44, 3), M(20, 28), PAD / 4 + 48.0)
    lin("ct4", R("CT", 44, 46), R("RUN", 0, 2), -31.875, (159.375 + LEAF / 2) / 4)
    iota("ct5", R("CT", 46, 48), [[320, 2]], -192)
    lin("ct6", col("CT", 48), lb, 127.5 + LEAF / 2, 320.0)
    for name, at, lo, hi in (("ct7", 0, 13, 17), ("ct8", 4, 16, 20), ("ctb", 8, 0, 6), ("ctc", 14, 5, 13)):
        lin(name, R("CT", 49 + at, 49 + at + hi - lo), M(lo, hi), 127.5, -4.0)
    quant("qu", "QU", 0, 128, R("UT"))
    for h in range(2):
        pick = R("PU", 8 * h, 8 * h + 8)
        cast("uc%d" % h, R("UU", 128 * h, 128 * h + 128), (R("QU"), pick), dt.uint32)
        copy("us%d" % h, R("UUs", 128 * h, 128 * h + 128), (R("QUs"), pick))
    for b in range(4):
        quant("eb%d" % b, "EB", 128 * b, 128 * b + 128, R("EDB", 3 - b, 515 - b))
        quant("eh%d" % b, "EH", 128 * b, 128 * b + 128, R("ED", 3 - b, 515 - b))
    iota("pm", R("PM"), [[-2, 2]], 1)
    iota("k0", R("K0"), [[-LEAF, 2]], 80)
    ts("zr", R("ZR"), R("M"), 4.0, Op.mult, lb, Op.subtract)
    lin("j0", R("J", 0, 28), R("ZR"), 208.0, 0.25)
    lin("j1", R("J", 28, 36), R("ZR", 0, 8), 319.0, -0.25)
    lin("j2", R("J", 36, 44), M(5, 13), 0.0, 4.0)
    lin("j3", R("J", 44, 64), M(0, 20), 0.0, 4.0)
    lin("jy", R("JY"), R("J"), -80.125)
    lin("jb", R("JB"), R("J"), -239.375)
    ts("ji", R("JI"), R("J"), 0.5, Op.mult, -0.25, Op.add)
    lin("ja0", R("JA"), R("J"), -320.0, 0.5)
    tt("ja1", R("JA"), R("JA"), R("JI"), Op.add)
    lin("jf0", R("LN", 3 * W1, 4 * W1), R("J", 0, W1), 0.0, 4.0 * LEAF + 1)
    lin("jf1", R("LN", 4 * W1 + 3 * W2, 4 * W1 + 4 * W2), R("J", W1, W1 + W2), 0.0, 4.0 * LEAF + 1)
    lin("o8", col("LANE", 2), l4, 0.5 - 1.5 * LEAF, LEAF / 4)
    act("gs", R("G1", 0, WS), R("RUN", 0, WS), Fn.Abs, col("LANE", 2), 0.25)
    fill("lf", R("LF", W2, 32), 0.0)
    quant("qv", "QV", 0, 128, R("VT"))

    C, K, akp, akm, k2, kl, most = (col("CK", i) for i in range(7))
    ak, cq, right, left, cqb = (col("TC", 44 + i) for i in range(5))
    wa = lambda i: R("WA", NA * i, NA * i + NA)
    nth = lambda name, i, n: R(name, i, None, n)
    PL = lambda b, lo=0, hi=432: R("PL", 432 * b + lo, 432 * b + hi)
    YP = lambda b, lo=0, hi=320: R("YP", 320 * b + lo, 320 * b + hi)
    AB = lambda b, lo, hi: R("AB", 320 * b + lo, 320 * b + hi)
    LO = lambda lo, hi: R("LO", lo, hi)
    result = lambda h, b: b if h else 4 + b
    rid, pid = topo.addr(prev)[:2]

    def send(t):
        lo = SLOTS * (2 - t)

        def form(e):
            for name, as_ in (("", dt.uint8), ("s", None)):
                e.remote_dma(ap(R("QX" + name, lo, lo + SLOTS), as_), ap(R("B%d%s" % (t, name), 0, SLOTS), as_), T.sem["arr%d" % t], T.sem.sent,
                             pid, rid, topo.mask(core, prev))
            return 2 * len(topo.engines(core, prev)), ("arr%d" % t, 2 * len(topo.engines(nxt, core)))
        call("send", {"g": form}, [R("QX", lo, lo + SLOTS), R("QXs", lo, lo + SLOTS)], [R("B%d" % t), R("B%ds" % t)], "far")
        return lo

    def start(name, h, b):
        lo, hi = PART[h]
        mm(name, result(h, b), hi - lo, "EB", 128 * b, "QX", GQ + lo, True, False)

    def contacts(h, b):
        lo, hi, at = ZPART[h]
        found, out = (PL(b, 0, 320 if h == 2 else 432), R("LA", at, at + (hi - lo) // 16)), R("ZT", 4 * lo + b, 4 * hi, 4)
        if (b, h) in FUSED:
            tt("z%d%d" % (h, b), out, found, AB(b, lo, hi), Op.add)
        else:
            copy("y%d%d" % (h, b), AB(b, lo, hi), found)
            tt("z%d%d" % (h, b), out, bank(b, lo, hi), AB(b, lo, hi), Op.add)

    for t in range(3):
        last = t == 2
        stage[0] = str(t)
        quant("qs", "QX", GQ + 192, GQ + 320, X(80, 208))
        mm("sc", 6, 128, "UU", 0, "QX", GQ + 192)
        mm("sk", 7, 128, "UU", 128, "QX", GQ + 192)
        if t:
            copy("xl0", X(0, 40), (R("YP"), LO(0, 10)))
            copy("xl1", X(40, 80), (R("YP"), LO(10, 20)))
            copy("xh1", X(208, 320), (R("YP"), LO(20, 48)))
        copy("xt", R("X", 528, 656), (R("YP"), LO(48, 56)) if t else (X(288, 320), R("LR")))
        scan("mc", R("RMC"), bank(6, 48, 113))
        scan("mk", R("RMK"), bank(7, 0, 25))
        act("c", R("SGC"), R("RMC"), Fn.Sign, col("RMC", 64), -1.0, C)
        act("k", R("SGK"), R("RMK"), Fn.Sign, col("RMK", 24), -1.0, K)
        act("tc", R("TC"), R("CT"), Fn.Abs, C)
        lin("b1", nth("BD", 1, 3), nth("BD", 0, 3), 0.0, col("SGC", 31))
        ts("b0", nth("BD", 2, 3), M(0, 8), K, Op.subtract, -BIG, Op.mult)
        ts("l1", R("L1"), R("TC", 0, 20), K, Op.subtract, 4.0, Op.mult)
        chain("b2", R("BR"), R("BD"), R("TC", 20, 44))
        ts("l2", R("L2"), nth("BR", 2, 3), K, Op.subtract, 4.0, Op.mult)
        copy("bm", R("BT", 0, 192), (R("X", 0, WIN), R("L1", 0, 12)))
        copy("bn", R("BT", 192, 320), (R("X", 0, WIN), R("L1", 12, 20)))
        copy("bt", R("BT", 320, 384), (R("X", 0, WIN), R("L2", 0, 4)))
        copy("bu", R("BT", 384, 448), (R("X", 0, WIN), R("L2", 4, 8)))
        quant("qb", "B%d" % t, 0, 128, R("BT"))
        came = send(t)
        quant("qx0", "QX", GQ + 112, GQ + 240, X(0, 128))
        quant("qx1", "QX", GQ - 16, GQ + 112, X(192, 320))
        for b in range(4):
            mm("h%d" % b, b, 320, "EH", 128 * b, "QX", GQ)
            copy("p0%d" % b, PL(b, 208, 320), bank(b, 0, 112))
            copy("p1%d" % b, PL(b, 0, 208), bank(b, 112, 320))
            if (b, 0) in FUSED:
                twin("t0%d" % b, AB(b, 0, 112), PL(b, 208, 320))
                twin("t1%d" % b, AB(b, 112, 320 if (b, 1) in FUSED else 192), PL(b, 0, 208 if (b, 1) in FUSED else 80))
        ts("k2", R("CK", 4, 6), R("K0"), K, Op.add, 2.0, Op.mult)
        lin("a0", wa(0), R("CT", 49), C)
        lin("a1", wa(1), R("TC", 49), k2, -2.0)
        tt("a3", wa(3), wa(0), wa(1), Op.mult)
        ts("a4", wa(4), wa(3), 0.0, Op.is_lt, k2, Op.mult)
        act("a2", wa(2), R("TC", 49), Fn.Abs, k2, -2.0)
        lin("k3", most, ak, 160.0)
        mate = nth("AE", 1, 4)
        tt("a5", mate, wa(4), wa(0), Op.add)
        lin("a6", nth("AE", 0, 4), mate, 0.0, -1.0)
        lin("a7", nth("AE", 3, 4), wa(2), right, 0.5)
        ts("a8", nth("AD", 1, 4), mate, right, Op.subtract, -BIG, Op.mult)
        ts("a9", nth("AD", 2, 4), mate, left, Op.add, -BIG, Op.mult)
        ts("aa", nth("AD", 3, 4), mate, most, Op.subtract, BIG, Op.mult)
        chain("ab", R("AR"), R("AD"), R("AE"))
        ts("la", R("LA"), nth("AR", 3, 4), left, Op.add, -0.5, Op.add)
        j0, w = (W1, W2) if last else (0, W1)
        J = lambda n: R(n, j0, j0 + w)
        ln = lambda i, e=None: R("LN", 4 * j0 + w * i, 4 * j0 + w * (e or i + 1))
        lin("ak", R("CK", 2, 4), R("PM"), ak, K)
        ts("n0", R("L3", 0, w), J("JY"), akp, Op.add, 4.0 / 3.0, Op.mult)
        ts("n1", ln(0), R("L3", 0, w), 4.0 * LEAF + 1, Op.mult)
        ts("n2", ln(1), J("JB"), akm, Op.add, 16.0 * LEAF + 4, Op.mult)
        ts("n3", ln(2), J("JA"), k2, Op.add, 8.0 * LEAF + 2, Op.mult)
        tt("n4", R("MX", 0, 2 * w), ln(0, 2), ln(2, 4), Op.max)
        tt("n5", R("SH", 0, w), R("MX", 0, w), R("MX", w, 2 * w), Op.max)
        ts("n6", R("VI", 0, w), R("SH", 0, w), 2, Op.logical_shift_right, 4 * LEAF - 1, Op.bitwise_and)
        ts("n7", R("VF", 0, w), R("VI", 0, w), 0.5 - 1.5 * LEAF, Op.add)
        act("n8", R("G1", WS, WS + w), R("VF", 0, w), Fn.Abs)
        g2 = R("G2", WS if last else 0, WS + w)
        act("n9", g2, R("G1", WS if last else 0, WS + w), Fn.Abs, kl, 2.0)
        if last:
            ts("lm", LO(0, W2), g2, -0.5, Op.mult, cq, Op.add)
        else:
            ts("lm", LO(56, 64), R("G2", 56, 64), -0.5, Op.mult, cq, Op.add)
            ts("lo", LO(0, 56), R("G2", 0, 56), -0.5, Op.mult, cqb, Op.add)
        for b in range(4):
            contacts(2, b)
        for b in range(4):
            mm("g%d" % b, 4 + b, 128, "EH", 128 * b, "QX", came)
            copy("pg%d" % b, PL(b, 320, 432), bank(4 + b, 0, SLOTS))
        for b in range(4):
            start("f%d" % b, 0, b)
        for h, (lo, hi) in enumerate(PART):
            for b in range(4):
                contacts(h, b)
                if h == 0:
                    start("d%d" % b, 1, b)
            quant("qz%d" % h, "QZ", lo, hi, R("ZT", 4 * lo, 4 * hi))
        if last:
            lin("lf", R("LF", 0, W2), g2, cq, -0.5)
            call("lt", {"v": lambda e: e.transpose(T.LT[:], T.LF[:])}, [R("LT")], [R("LF")])
            for i in range(8):
                store("so%d" % i, T.lo[i:i + 1, :], T.LT[32 * (i // 2):32 * (i // 2) + 20, 16 * (i % 2):16 * (i % 2) + 16], R("LT"))
        for h, (lo, hi) in enumerate(PART):
            for b in range(4):
                mm("w%d%d" % (h, b), result(h, b), hi - lo, "QW", 128 * b, "QZ", lo, False, True)
                for i, (first, end, place) in enumerate(RUNS):
                    if lo <= first < hi:
                        copy("r%d%d" % (i, b), YP(b, place, place + end - first), bank(result(h, b), first - lo, end - lo), 0.03125)
        if not last:
            for b in range(4):
                copy("xm%d" % b, X(80, 208, b), (YP(b), LO(56, 64)))

    stage[0] = "e"
    for i, (b, lo, hi) in enumerate(LAST):
        copy("x%d" % i, X(lo, hi, b), (YP(b), LO(lo // 16, hi // 16)))
    for h, (lo, hi) in enumerate(PART):
        quant("q%d" % h, "QF", lo, hi, X(lo, hi))
        store("oc%d" % h, T.oc[:, 4 * lo:4 * hi], T.QF[:, lo:hi].bitcast(dt.uint8), R("QF", lo, hi))
        mm("v%d" % h, 2 + h, hi - lo, "QV", 0, "QF", lo)
        copy("y%d" % h, R("YO", lo, hi), bank(2 + h, 0, hi - lo))
        store("sy%d" % h, T.y[:, lo:hi], T.YO[:, lo:hi], R("YO", lo, hi))
    for i in range(4):
        store("os%d" % i, T.osc[4 * i:4 * i + 4, :], T.QFs[32 * i:32 * i + 4, :], R("QFs"))
    return calls


def before(calls):
    uses, deps = {}, {}
    for name, (forms, outs, ins, kind) in calls.items():
        deps[name] = {}
        for rs, writes in ((ins, False), (outs if kind != "far" else [], True)):
            for r in rs:
                cols = set(range(*r[1:]))
                for w2, cols2, other in uses.get(r[0], []):
                    if (writes or w2) and not cols.isdisjoint(cols2):
                        deps[name][other] = True
                    elif r[0] == "PS" and r[1] // 512 == min(cols2) // 512:
                        deps[name].setdefault(other, False)
        for rs, writes in ((ins if kind != "far" else [], False), (outs, True)):
            for r in rs:
                cols = set(range(*r[1:]))
                old = uses.get(r[0], [])
                if writes:
                    old = [e for e in old if not e[1] <= cols]
                uses[r[0]] = old + [(writes, cols, name)]
    return deps


def spread(calls, words):
    order = []
    for t in "012":
        for name, q in words:
            for full in ("c" + name[1:] if name[0] == "." and t == "0" else t + name, "e" + name[1:] if name[0] == "!" and t == "2" else ""):
                if full in calls:
                    order.append((full, q))
    return order


def rank_program(g, core, T, topo):
    if T.rank_of(core) is None:
        return
    calls = plan(core, T, topo)
    order = spread(calls, [word.split(":") for word in ORDER.split()])
    where = dict(order)
    deps = before(calls)
    queue = {"v": g.vector, "a": g.scalar, "t": g.tensor, "g": g, "s": g.sync}
    total, seen, clock, token, free = {}, {q: {} for q in queue}, {}, {}, list(DMAS)

    def wait(q, tokens):
        need = {}
        for s, n in tokens:
            need[s] = max(need.get(s, 0), n)
        for s, n in sorted(need.items(), key=lambda e: -len(clock.get(e, {}))):
            if seen[q].get(s, 0) < n:
                queue[q].wait_ge(T.sem[s], n)
                for s2, n2 in list(clock.get((s, n), {}).items()) + [(s, n)]:
                    seen[q][s2] = max(seen[q].get(s2, 0), n2)

    for name, q in order:
        forms, outs, ins, kind = calls[name]
        wait(q, [token[d] for d, sure in deps[name].items() if where[d] != q or sure and q != "t"])
        if kind == "far":
            n, token[name] = forms[q](queue[q])
            total["sent"] = total.get("sent", 0) + n
            total[token[name][0]] = token[name][1]
        else:
            sem, n = (q, 1) if kind == "run" else ("out" if kind == "out" else free.pop(0), 16)
            forms[q](queue[q]).then_inc(T.sem[sem], n)
            total[sem] = total.get(sem, 0) + n
            token[name] = (sem, total[sem])
            clock[token[name]] = dict(seen[q])
    wait("g", list(total.items()))
